import numpy as np
import ml_dtypes


def mxq(x, axis, fmt="e4m3"):
    dtype, down = {"e4m3": (ml_dtypes.float8_e4m3fn, 7), "e5m2": (ml_dtypes.float8_e5m2, 14)}[fmt]
    v = np.moveaxis(np.asarray(x, np.float32).astype(ml_dtypes.bfloat16).astype(np.float64), axis, -1)
    blocks = v.reshape(v.shape[:-1] + (-1, 32))
    amax = np.abs(blocks).max(-1, keepdims=True)
    byte = np.maximum(np.where(amax > 0, np.frexp(amax)[1] - 1 + 127, 0) - down, 1)
    scale = np.exp2(byte - 127.0)
    codes = (blocks / scale).astype(np.float32).astype(dtype).astype(np.float64)
    return np.moveaxis((codes * scale).reshape(v.shape), -1, axis)


WIDE = False


def mx_kscale(k):
    if not WIDE:
        return np.ones(k)
    levels = np.array([10, -10, 5, -5, 0])
    if k % 512:
        return np.exp2(np.random.permutation(np.resize(levels, k // 32))).repeat(32)
    a = np.empty((k // 512, 16))
    for p in range(k // 512):
        a[p, :8] = np.random.permutation(np.resize(levels, 8))
        for g in range(8):
            far = levels[np.abs(levels - a[p, g]) >= 10]
            a[p, g + 8] = far[np.random.randint(len(far))]
    return np.exp2(a.ravel()).repeat(32)


def f64(x):
    return np.asarray(x).astype(np.float64)


def striped(idx):
    return np.tile(idx.reshape(-1, 16).T, (8, 1)).astype(np.uint16)


def unstriped(offs):
    return offs[:16].T.reshape(-1).astype(np.int64)


E2M1 = np.array([0.0, 0.5, 1.0, 1.5, 2.0, 3.0, 4.0, 6.0, -0.0, -0.5, -1.0, -1.5, -2.0, -3.0, -4.0, -6.0])


def pack_weight(w, fmt):
    k, n = w.shape
    w = f64(np.asarray(w, np.float32).astype(ml_dtypes.bfloat16)).reshape(k // 32, 32, n)
    amax = np.abs(w).max(1)
    if fmt == "e4m3":
        byte = np.frexp(amax)[1] - 1 + 127 - 7
    else:
        mant, ex = np.frexp(amax / 6.0)
        byte = np.where(mant > 0.5, ex, ex - 1) + 127
    byte = np.clip(np.where(amax > 0, byte, 1), 1, 254)
    scaled = (w * np.exp2(127.0 - byte)[:, None, :]).reshape(k, n).astype(np.float32)
    by_word = np.ascontiguousarray(scaled.reshape(k // 512, 128, 4, n).transpose(0, 1, 3, 2))
    if fmt == "e4m3":
        words = by_word.astype(ml_dtypes.float8_e4m3fn).view(np.uint8)
    else:
        c = by_word.astype(ml_dtypes.float4_e2m1fn).view(np.uint8) & 0xF
        words = (c[..., 0::2] | (c[..., 1::2] << 4)).reshape(k // 512, 128, 2 * n)
    return np.ascontiguousarray(words), np.ascontiguousarray(byte.astype(np.uint8).reshape(k // 512, 16, n))


def unpack_weight(words, scales, fmt):
    g, _, n = scales.shape
    words = np.ascontiguousarray(words).reshape(g, 128, n, -1)
    if fmt == "e4m3":
        vals = words.view(ml_dtypes.float8_e4m3fn).astype(np.float64)
    else:
        nib = np.empty((g, 128, n, 4), np.uint8)
        nib[..., 0::2] = words & 0xF
        nib[..., 1::2] = words >> 4
        vals = E2M1[nib]
    vals = vals * np.repeat(np.exp2(scales.astype(np.float64) - 127.0), 8, axis=1)[..., None]
    return vals.transpose(0, 1, 3, 2).reshape(g * 512, n)


def gelu(v):
    return 0.5 * v * (1.0 + np.tanh(np.sqrt(2.0 / np.pi) * (v + 0.044715 * v**3)))


K, T, E, C, H, N = 512, 768, 12, 128, 512, 128


def by_expert(wq, xq):
    return np.concatenate([wq[e].T @ xq[:, e * C:(e + 1) * C] for e in range(E)], axis=1)


def setup_inputs():
    n = np.random.standard_normal
    s = mx_kscale(K)[:, None]
    u = mx_kscale(H)
    first = np.random.permutation(np.repeat(np.arange(E), T // E))
    second = (first + 1 + np.random.permutation(np.repeat(np.arange(E - 1), -(-T // (E - 1)))[:T])) % E
    while np.bincount(second, minlength=E).max() != T // E:
        load = np.bincount(second, minlength=E); hi, lo = int(load.argmax()), int(load.argmin())
        t = np.flatnonzero((second == hi) & (first != lo))[0]; second[t] = lo
    slot_token = np.empty(E * C, np.int64); pos = np.empty((2, T), np.int64); fill = np.zeros(E, np.int64)
    place = np.stack([np.random.permutation(C) for _ in range(E)])
    for r, deal in enumerate((first, second)):
        for t in np.random.permutation(T):
            e = deal[t]; j = e * C + place[e, fill[e]]; fill[e] += 1; slot_token[j] = t; pos[r, t] = j
    g = np.random.uniform(0.2, 0.8, T)
    x = pack_weight(n((K, T)) * s, "e4m3")
    return {
        "x_words": x[0],
        "x_scales": x[1],
        "w1": (n((E + 1, K, H)) / np.sqrt(K) / s[None]).astype(np.float32),
        "w3": (n((E + 1, K, H)) / np.sqrt(K) / s[None] * u[None, None, :]).astype(np.float32),
        "w2": (n((E + 1, H, N)) / np.sqrt(H) / u[None, :, None]).astype(np.float32),
        "gate": np.stack([np.tile(g, (N, 1)), np.tile(1.0 - g, (N, 1))]).astype(np.float32),
        "offs": striped(slot_token),
        "pos1": striped(pos[0]),
        "pos2": striped(pos[1]),
    }


def reference(x_words, x_scales, w1, w3, w2, gate, offs, pos1, pos2):
    idx = unstriped(offs)
    w1q, w3q, w2q = mxq(f64(w1), 1, "e4m3"), mxq(f64(w3), 1, "e4m3"), mxq(f64(w2), 1, "e4m3")
    xs = unpack_weight(x_words, x_scales, "e4m3")
    hs = gelu(w1q[E].T @ xs) * (w3q[E].T @ xs)
    ys = w2q[E].T @ mxq(hs, 0, "e4m3")
    xq = unpack_weight(x_words, x_scales, "e4m3")[:, idx]
    h = gelu(by_expert(w1q, xq))
    h = h * by_expert(w3q, xq)
    y = by_expert(w2q, mxq(h, 0, "e4m3"))
    return ys + f64(gate[0]) * y[:, unstriped(pos1)] + f64(gate[1]) * y[:, unstriped(pos2)]

@@ -1,0 +1,244 @@
+from contextlib import ExitStack
+
+import concourse.mybir as mybir
+
+K, T, E, C, H, N = 512, 768, 12, 128, 512, 128
+S = E * C
+FLOPS = 2 * (S + T) * (2 * K * H + H * N)
+
+F32 = mybir.dt.float32
+BF16 = mybir.dt.bfloat16
+I32 = mybir.dt.int32
+U32 = mybir.dt.uint32
+U16 = mybir.dt.uint16
+U8 = mybir.dt.uint8
+FP8X4 = mybir.dt.float8_e4m3fn_x4
+GELU = mybir.ActivationFunctionType.Gelu_apprx_tanh
+MULT = mybir.AluOpType.mult
+ADD = mybir.AluOpType.add
+
+P = 128
+PACK = 4
+GATHER = 512
+STREAM_BUFS = 16
+LATE_W2 = 3
+V1 = [128,128,128,128,128,128,128,128,128,128,128,96,128]
+V3 = [0,0,0,0,0,0,0,0,0,64,64,64,0]
+CHUNKS = [256,256,256]
+FINE = True
+GATHERS = [512,512,512]
+
+
+def tile_moe_shr_glu_gelu_kernel(
+    tc, x_words, x_scales, w1, w3, w2, gate, offs, pos1, pos2, out
+):
+    nc = tc.nc
+    with ExitStack() as ctx:
+        keep = ctx.enter_context(tc.tile_pool(name="keep", bufs=1))
+        stream = ctx.enter_context(tc.tile_pool(name="stream", bufs=STREAM_BUFS))
+        work = ctx.enter_context(tc.tile_pool(name="work", bufs=3))
+        up_psum = ctx.enter_context(tc.psum_pool(name="up_psum", bufs=3))
+        down_psum = ctx.enter_context(tc.psum_pool(name="down_psum", bufs=2))
+
+        tok_words = keep.tile([P, T], I32, name="tok_words", align_bytes=64)
+        tok_scales = keep.tile([P, T], U8, name="tok_scales", align_bytes=64)
+        slot_words = keep.tile([P, S], U32, name="slot_words", align_bytes=64)
+        slot_scales = keep.tile([P, S], U8, name="slot_scales", align_bytes=64)
+        offs_sb = keep.tile([P, S // 16], U16, name="offs_sb")
+        pos1_sb = keep.tile([P, T // 16], U16, name="pos1_sb")
+        pos2_sb = keep.tile([P, T // 16], U16, name="pos2_sb")
+        h_codes = keep.tile([P, S + T], U32, name="h_codes", align_bytes=64)
+        h_scales = keep.tile([P, S + T], U8, name="h_scales", align_bytes=64)
+        y_slots = keep.tile([P, S], F32, name="y_slots")
+
+        nc.sync.dma_start(
+            out=tok_words[:], in_=x_words[0].rearrange("p t r -> p (t r)").bitcast(I32)
+        )
+        nc.sync.dma_start(out=offs_sb[:], in_=offs)
+        for q in range(4):
+            nc.sync.dma_start(
+                out=tok_scales[32 * q : 32 * q + 32, :].bitcast(I32),
+                in_=x_scales[0, 4 * q : 4 * q + 4, :].bitcast(I32).partition_broadcast(8),
+            )
+
+        def load(rows):
+            width = rows.shape[1]
+            raw = stream.tile([P, PACK, width], F32, name="raw", tag="raw")
+            nc.sync.dma_start(out=raw[:], in_=rows.rearrange("(p j) c -> p j c", j=PACK))
+            return raw
+
+        def cast(on_vector, dst, src):
+            if on_vector:
+                nc.vector.tensor_copy(out=dst, in_=src)
+            else:
+                nc.scalar.copy(out=dst, in_=src)
+
+        def quantize(grouped, tag):
+            width = grouped.shape[1] // PACK
+            codes = work.tile([P, width], U32, name=tag + "_codes", tag=tag + "_codes", align_bytes=64)
+            scales = work.tile([P, width], U8, name=tag + "_scales", tag=tag + "_scales", align_bytes=64)
+            nc.vector.quantize_mx(out=codes[:].bitcast(FP8X4), scales=scales[:], in_=grouped[:])
+            return codes, scales
+
+        def up_weights(pieces, vector_share, tag, fine=False):
+            grouped = work.tile([P, PACK * H], BF16, name=tag + "_bf", tag=tag + "_bf", align_bytes=64)
+            dst = grouped[:].rearrange("p (t m j) -> p m j t", t=PACK, j=PACK)
+            codes = work.tile([P, H], U32, name=tag + "_codes", tag=tag + "_codes", align_bytes=64)
+            scales = work.tile([P, H], U8, name=tag + "_scales", tag=tag + "_scales", align_bytes=64)
+            split = P - vector_share
+            m0 = 0
+            for raw in pieces:
+                count = raw.shape[2] // PACK
+                src = raw[:].rearrange("p j (m t) -> p m j t", t=PACK)
+                cut = min(max(split - m0, 0), count)
+                if cut > 0:
+                    nc.scalar.copy(out=dst[:, m0 : m0 + cut], in_=src[:, :cut])
+                if cut < count:
+                    nc.vector.tensor_copy(out=dst[:, m0 + cut : m0 + count], in_=src[:, cut:])
+                if fine:
+                    for t in range(PACK):
+                        c0 = P * t + m0
+                        nc.vector.quantize_mx(
+                            out=codes[:, c0 : c0 + count].bitcast(FP8X4),
+                            scales=scales[:, c0 : c0 + count],
+                            in_=grouped[:, PACK * c0 : PACK * (c0 + count)],
+                        )
+                m0 += count
+            if not fine:
+                nc.vector.quantize_mx(out=codes[:].bitcast(FP8X4), scales=scales[:], in_=grouped[:])
+            return codes, scales
+
+        def down_weights(raw):
+            grouped = work.tile([P, PACK * N], BF16, name="w2_bf", tag="w2_bf", align_bytes=64)
+            cast(
+                False,
+                grouped[:].rearrange("p (c i j) -> p c j i", i=4, j=PACK),
+                raw[:].rearrange("p j (c i) -> p c j i", i=4),
+            )
+            return quantize(grouped, "w2")
+
+        def up_product(weights, words, scales, tag):
+            codes, code_scales = weights
+            bank = up_psum.tile([P, PACK, C], F32, name=tag, tag=tag)
+            for t in range(PACK):
+                cols = slice(P * t, P * (t + 1))
+                nc.tensor.matmul_mx(
+                    out=bank[:, t, :],
+                    lhsT=codes[:, cols].bitcast(FP8X4),
+                    lhsT_scale=code_scales[:, cols],
+                    rhs=words.bitcast(FP8X4),
+                    rhs_scale=scales,
+                    start=True,
+                    stop=True,
+                )
+            return bank
+
+        def activate(w1q, words, scales):
+            a_bank = up_product(w1q, words, scales, "a_bank")
+            act = work.tile([P, C, PACK], F32, name="act", tag="act")
+            nc.scalar.activation(out=act[:], in_=a_bank[:].rearrange("p t n -> p n t"), func=GELU)
+            return act
+
+        def hidden(act, w3q, words, scales, h0):
+            b_bank = up_product(w3q, words, scales, "b_bank")
+            h_bf = work.tile([P, C, PACK], BF16, name="h_bf", tag="h_bf", align_bytes=64)
+            nc.vector.tensor_tensor(
+                out=h_bf[:], in0=b_bank[:].rearrange("p t n -> p n t"), in1=act[:], op=MULT
+            )
+            nc.vector.quantize_mx(
+                out=h_codes[:, h0 : h0 + C].bitcast(FP8X4),
+                scales=h_scales[:, h0 : h0 + C],
+                in_=h_bf[:].rearrange("p n t -> p (n t)"),
+            )
+
+        def down_product(w2q, h0, count, bank):
+            codes, code_scales = w2q
+            nc.tensor.matmul_mx(
+                out=bank,
+                lhsT=codes[:].bitcast(FP8X4),
+                lhsT_scale=code_scales[:],
+                rhs=h_codes[:, h0 : h0 + count].bitcast(FP8X4),
+                rhs_scale=h_scales[:, h0 : h0 + count],
+                start=True,
+                stop=True,
+            )
+
+        def expert_output(e, w2_raw):
+            w2q = down_weights(w2_raw)
+            bank = down_psum.tile([P, C], F32, name="y_bank", tag="y_bank")
+            down_product(w2q, e * C, C, bank[:])
+            nc.scalar.copy(out=y_slots[:, e * C : (e + 1) * C], in_=bank[:])
+
+        def gather_slots(s0):
+            offsets = offs_sb[:, s0 // 16 : (s0 + GATHER) // 16]
+            nc.vector.tensor_copy(
+                out=slot_words[:, s0 : s0 + GATHER],
+                in_=tok_words[:].bitcast(U32).indirect(offsets),
+            )
+            nc.vector.tensor_copy(
+                out=slot_scales[:, s0 : s0 + GATHER], in_=tok_scales[:].indirect(offsets)
+            )
+
+        w1_raw = load(w1[E])
+        w3_raw = load(w3[E])
+        nc.sync.dma_start(out=pos1_sb[:], in_=pos1)
+        nc.sync.dma_start(out=pos2_sb[:], in_=pos2)
+        w1q = up_weights([w1_raw], V1[E], "w1")
+        w3q = up_weights([w3_raw], V3[E], "w3")
+        for t0 in range(0, T, C):
+            words = tok_words[:, t0 : t0 + C]
+            scales = tok_scales[:, t0 : t0 + C]
+            act = activate(w1q, words, scales)
+            hidden(act, w3q, words, scales, S + t0)
+
+        late = {}
+        for e in range(E):
+            last = e == E - 1
+            if (e * C) % GATHER == 0:
+                gather_slots(e * C)
+            w1_raw = load(w1[e])
+            if last:
+                w3_pieces = [load(w3[e][:, : H // 2]), load(w3[e][:, H // 2 :])]
+                for d in range(E - LATE_W2, E):
+                    late[d] = load(w2[d])
+                gate1_sb = stream.tile([P, T], F32, name="gate1_sb", tag="raw")
+                nc.sync.dma_start(out=gate1_sb[:], in_=gate[0])
+                late[E] = load(w2[E])
+                gate2_sb = stream.tile([P, T], F32, name="gate2_sb", tag="raw")
+                nc.sync.dma_start(out=gate2_sb[:], in_=gate[1])
+            else:
+                w3_pieces = [load(w3[e])]
+            if e < E - LATE_W2:
+                w2_raw = load(w2[e])
+            words = slot_words[:, e * C : (e + 1) * C]
+            scales = slot_scales[:, e * C : (e + 1) * C]
+            w1q = up_weights([w1_raw], V1[e], "w1")
+            act = activate(w1q, words, scales)
+            w3q = up_weights(w3_pieces, V3[e], "w3", FINE and last)
+            hidden(act, w3q, words, scales, e * C)
+            if e < E - LATE_W2:
+                expert_output(e, w2_raw)
+        for d in range(E - LATE_W2, E):
+            expert_output(d, late[d])
+
+        w2q = down_weights(late[E])
+        t0 = 0
+        for CHUNK in CHUNKS:
+            toks = slice(t0, t0 + CHUNK)
+            cols = slice(t0 // 16, (t0 + CHUNK) // 16)
+            ys_bank = up_psum.tile([P, CHUNK], F32, name="ys_bank", tag="a_bank")
+            down_product(w2q, S + t0, CHUNK, ys_bank[:])
+            first = work.tile([P, CHUNK], F32, name="first", tag="first")
+            second = work.tile([P, CHUNK], F32, name="second", tag="second")
+            both = work.tile([P, CHUNK], F32, name="both", tag="both")
+            total = work.tile([P, CHUNK], F32, name="total", tag="total")
+            nc.vector.tensor_tensor(
+                out=first[:], in0=y_slots[:].indirect(pos1_sb[:, cols]), in1=gate1_sb[:, toks], op=MULT
+            )
+            nc.vector.tensor_tensor(
+                out=second[:], in0=y_slots[:].indirect(pos2_sb[:, cols]), in1=gate2_sb[:, toks], op=MULT
+            )
+            nc.vector.tensor_tensor(out=both[:], in0=ys_bank[:], in1=first[:], op=ADD)
+            nc.vector.tensor_tensor(out=total[:], in0=both[:], in1=second[:], op=ADD)
+            nc.sync.dma_start(out=out[:, toks], in_=total[:])
+            t0 += CHUNK

@@ -21,10 +21,20 @@ P = 128
 PACK = 4
 GATHER = 512
 STREAM_BUFS = 16
-LATE_W2 = 3
-V1 = [128,128,128,128,128,128,128,128,128,128,128,96,128]
-V3 = [0,0,0,0,0,0,0,0,0,64,64,64,0]
-CHUNKS = [256,256,256]
+LOADS = [["x",0],["offs",0],["xs",0],["w1",12],["w3",12],["w1",0],["w3",0],["w1",1],["w3",1],["w2",0],["pos",0],["w1",2],["w3",2],["w2",1],["w1",3],["w3",3],["w2",2],["w1",4],["w3",4],["w2",3],["w1",5],["w3",5],["w2",4],["w1",6],["w3",6],["w2",5],["w1",7],["w3",7],["w2",6],["w1",8],["w3",8],["w2",7],["w1",9],["w3",9],["w2",8],["w1",10],["w3",10],["w1",11],["w3",11],["w2",9],["w2",10],["w2",11],["w2",12],["gate",0],["gate",1]]
+C2V = [True,True,True,True,True,True,True,True,True,True,False,False,False]
+GPOS = [1,5,9]
+FORCE = [False,False,False,False,False,False,False,False,False,False,False,False,False]
+ORDER = [12,0,1,2,3,4,5,6,7,8,9,10,11]
+OUT_AFTER = [2,3,4,5,6,7,8,9,10,12,12,12]
+V1 = ["V","V","V","V","V","V","V","V","V","V","V","VV","S"]
+V3 = ["S","S","S","S","S","S","S","S","S","S","SS","SV","V"]
+CHUNKS = [512,128,128]
+HALVES = True
+FIRST_BUFS = 3
+BF_BUFS = 2
+ADDORDER = 1
+W1HALVES = True
 FINE = True
 GATHERS = [512,512,512]
 
@@ -51,15 +61,6 @@ def tile_moe_shr_glu_gelu_kernel(
         h_scales = keep.tile([P, S + T], U8, name="h_scales", align_bytes=64)
         y_slots = keep.tile([P, S], F32, name="y_slots")
 
-        nc.sync.dma_start(
-            out=tok_words[:], in_=x_words[0].rearrange("p t r -> p (t r)").bitcast(I32)
-        )
-        nc.sync.dma_start(out=offs_sb[:], in_=offs)
-        for q in range(4):
-            nc.sync.dma_start(
-                out=tok_scales[32 * q : 32 * q + 32, :].bitcast(I32),
-                in_=x_scales[0, 4 * q : 4 * q + 4, :].bitcast(I32).partition_broadcast(8),
-            )
 
         def load(rows):
             width = rows.shape[1]
@@ -80,38 +81,32 @@ def tile_moe_shr_glu_gelu_kernel(
             nc.vector.quantize_mx(out=codes[:].bitcast(FP8X4), scales=scales[:], in_=grouped[:])
             return codes, scales
 
-        def up_weights(pieces, vector_share, tag, fine=False):
-            grouped = work.tile([P, PACK * H], BF16, name=tag + "_bf", tag=tag + "_bf", align_bytes=64)
-            dst = grouped[:].rearrange("p (t m j) -> p m j t", t=PACK, j=PACK)
+        def up_weights(pieces, engines, tag):
             codes = work.tile([P, H], U32, name=tag + "_codes", tag=tag + "_codes", align_bytes=64)
             scales = work.tile([P, H], U8, name=tag + "_scales", tag=tag + "_scales", align_bytes=64)
-            split = P - vector_share
-            m0 = 0
-            for raw in pieces:
-                count = raw.shape[2] // PACK
-                src = raw[:].rearrange("p j (m t) -> p m j t", t=PACK)
-                cut = min(max(split - m0, 0), count)
-                if cut > 0:
-                    nc.scalar.copy(out=dst[:, m0 : m0 + cut], in_=src[:, :cut])
-                if cut < count:
-                    nc.vector.tensor_copy(out=dst[:, m0 + cut : m0 + count], in_=src[:, cut:])
-                if fine:
+            views = [raw[:].rearrange("p j (m t) -> p m j t", t=PACK) for raw in pieces]
+            if len(engines) > len(views):
+                views = [views[0][:, : P // 2], views[0][:, P // 2 :]]
+            count = P // len(views)
+            for half, src in enumerate(views):
+                grouped = work.tile([P, PACK * PACK * count], BF16, name=tag + "_bf", tag=tag + "_bf", align_bytes=64, bufs=BF_BUFS)
+                cast(engines[half] == "V", grouped[:].rearrange("p (t m j) -> p m j t", t=PACK, j=PACK), src)
+                if count == P:
+                    nc.vector.quantize_mx(out=codes[:].bitcast(FP8X4), scales=scales[:], in_=grouped[:])
+                else:
                     for t in range(PACK):
-                        c0 = P * t + m0
+                        c0 = P * t + count * half
                         nc.vector.quantize_mx(
                             out=codes[:, c0 : c0 + count].bitcast(FP8X4),
                             scales=scales[:, c0 : c0 + count],
-                            in_=grouped[:, PACK * c0 : PACK * (c0 + count)],
+                            in_=grouped[:, PACK * count * t : PACK * count * (t + 1)],
                         )
-                m0 += count
-            if not fine:
-                nc.vector.quantize_mx(out=codes[:].bitcast(FP8X4), scales=scales[:], in_=grouped[:])
             return codes, scales
 
-        def down_weights(raw):
+        def down_weights(raw, on_vector):
             grouped = work.tile([P, PACK * N], BF16, name="w2_bf", tag="w2_bf", align_bytes=64)
             cast(
-                False,
+                on_vector,
                 grouped[:].rearrange("p (c i j) -> p c j i", i=4, j=PACK),
                 raw[:].rearrange("p j (c i) -> p c j i", i=4),
             )
@@ -133,17 +128,20 @@ def tile_moe_shr_glu_gelu_kernel(
                 )
             return bank
 
-        def activate(w1q, words, scales):
+        def activate(w1q, words, scales, room):
             a_bank = up_product(w1q, words, scales, "a_bank")
-            act = work.tile([P, C, PACK], F32, name="act", tag="act")
-            nc.scalar.activation(out=act[:], in_=a_bank[:].rearrange("p t n -> p n t"), func=GELU)
+            if room is None:
+                act = work.tile([P, C, PACK], F32, name="act", tag="act")[:]
+            else:
+                act = room.rearrange("p (n t) -> p n t", t=PACK)
+            nc.scalar.activation(out=act, in_=a_bank[:].rearrange("p t n -> p n t"), func=GELU)
             return act
 
         def hidden(act, w3q, words, scales, h0):
             b_bank = up_product(w3q, words, scales, "b_bank")
             h_bf = work.tile([P, C, PACK], BF16, name="h_bf", tag="h_bf", align_bytes=64)
             nc.vector.tensor_tensor(
-                out=h_bf[:], in0=b_bank[:].rearrange("p t n -> p n t"), in1=act[:], op=MULT
+                out=h_bf[:], in0=b_bank[:].rearrange("p t n -> p n t"), in1=act, op=MULT
             )
             nc.vector.quantize_mx(
                 out=h_codes[:, h0 : h0 + C].bitcast(FP8X4),
@@ -164,7 +162,7 @@ def tile_moe_shr_glu_gelu_kernel(
             )
 
         def expert_output(e, w2_raw):
-            w2q = down_weights(w2_raw)
+            w2q = down_weights(w2_raw, C2V[e])
             bank = down_psum.tile([P, C], F32, name="y_bank", tag="y_bank")
             down_product(w2q, e * C, C, bank[:])
             nc.scalar.copy(out=y_slots[:, e * C : (e + 1) * C], in_=bank[:])
@@ -179,66 +177,81 @@ def tile_moe_shr_glu_gelu_kernel(
                 out=slot_scales[:, s0 : s0 + GATHER], in_=tok_scales[:].indirect(offsets)
             )
 
-        w1_raw = load(w1[E])
-        w3_raw = load(w3[E])
-        nc.sync.dma_start(out=pos1_sb[:], in_=pos1)
-        nc.sync.dma_start(out=pos2_sb[:], in_=pos2)
-        w1q = up_weights([w1_raw], V1[E], "w1")
-        w3q = up_weights([w3_raw], V3[E], "w3")
-        for t0 in range(0, T, C):
-            words = tok_words[:, t0 : t0 + C]
-            scales = tok_scales[:, t0 : t0 + C]
-            act = activate(w1q, words, scales)
-            hidden(act, w3q, words, scales, S + t0)
+        raws = {}
+        gates = {}
+        issued = []
 
-        late = {}
-        for e in range(E):
-            last = e == E - 1
-            if (e * C) % GATHER == 0:
-                gather_slots(e * C)
-            w1_raw = load(w1[e])
-            if last:
-                w3_pieces = [load(w3[e][:, : H // 2]), load(w3[e][:, H // 2 :])]
-                for d in range(E - LATE_W2, E):
-                    late[d] = load(w2[d])
-                gate1_sb = stream.tile([P, T], F32, name="gate1_sb", tag="raw")
-                nc.sync.dma_start(out=gate1_sb[:], in_=gate[0])
-                late[E] = load(w2[E])
-                gate2_sb = stream.tile([P, T], F32, name="gate2_sb", tag="raw")
-                nc.sync.dma_start(out=gate2_sb[:], in_=gate[1])
+        def issue_until(name, e):
+            while (name, e) not in issued:
+                kind, index = LOADS[len(issued)]
+                issued.append((kind, index))
+                if kind == "x":
+                    nc.sync.dma_start(
+                        out=tok_words[:], in_=x_words[0].rearrange("p t r -> p (t r)").bitcast(I32)
+                    )
+                elif kind == "offs":
+                    nc.sync.dma_start(out=offs_sb[:], in_=offs)
+                elif kind == "pos":
+                    nc.sync.dma_start(out=pos1_sb[:], in_=pos1)
+                    nc.sync.dma_start(out=pos2_sb[:], in_=pos2)
+                elif kind == "xs":
+                    for q in range(4):
+                        nc.sync.dma_start(
+                            out=tok_scales[32 * q : 32 * q + 32, :].bitcast(I32),
+                            in_=x_scales[0, 4 * q : 4 * q + 4, :].bitcast(I32).partition_broadcast(8),
+                        )
+                elif kind == "gate":
+                    gates[index] = stream.tile([P, T], F32, name="gate_sb", tag="raw")
+                    nc.sync.dma_start(out=gates[index][:], in_=gate[index])
+                elif kind == "w3" and index == ORDER[-1] and HALVES:
+                    raws[kind, index] = [load(w3[index][:, : H // 2]), load(w3[index][:, H // 2 :])]
+                elif kind == "w1" and index == ORDER[-1] and W1HALVES:
+                    raws[kind, index] = [load(w1[index][:, : H // 2]), load(w1[index][:, H // 2 :])]
+                else:
+                    raws[kind, index] = [load({"w1": w1, "w3": w3, "w2": w2}[kind][index])]
+
+        issue_until(*LOADS[-1])
+        for step, e in enumerate(ORDER):
+            for g in range(3):
+                if GPOS[g] == step:
+                    gather_slots(g * GATHER)
+            w1q = up_weights(raws["w1", e], V1[e], "w1")
+            w3q = up_weights(raws["w3", e], V3[e], "w3")
+            spent = raws["w3", e][0][:].rearrange("p j c -> p (j c)")
+            if e == E:
+                groups = [(tok_words[:, t0 : t0 + C], tok_scales[:, t0 : t0 + C], S + t0) for t0 in range(0, T, C)]
             else:
-                w3_pieces = [load(w3[e])]
-            if e < E - LATE_W2:
-                w2_raw = load(w2[e])
-            words = slot_words[:, e * C : (e + 1) * C]
-            scales = slot_scales[:, e * C : (e + 1) * C]
-            w1q = up_weights([w1_raw], V1[e], "w1")
-            act = activate(w1q, words, scales)
-            w3q = up_weights(w3_pieces, V3[e], "w3", FINE and last)
-            hidden(act, w3q, words, scales, e * C)
-            if e < E - LATE_W2:
-                expert_output(e, w2_raw)
-        for d in range(E - LATE_W2, E):
-            expert_output(d, late[d])
+                groups = [(slot_words[:, e * C : (e + 1) * C], slot_scales[:, e * C : (e + 1) * C], e * C)]
+            for i, (words, scales, h0) in enumerate(groups):
+                room = spent[:, 512 * (i % 4) : 512 * (i % 4 + 1)] if FORCE[e] else None
+                act = activate(w1q, words, scales, room)
+                hidden(act, w3q, words, scales, h0)
+            for d in range(E):
+                if OUT_AFTER[d] == step:
+                    expert_output(d, raws["w2", d][0])
 
-        w2q = down_weights(late[E])
+        w2q = down_weights(raws["w2", E][0], C2V[E])
         t0 = 0
         for CHUNK in CHUNKS:
             toks = slice(t0, t0 + CHUNK)
             cols = slice(t0 // 16, (t0 + CHUNK) // 16)
             ys_bank = up_psum.tile([P, CHUNK], F32, name="ys_bank", tag="a_bank")
             down_product(w2q, S + t0, CHUNK, ys_bank[:])
-            first = work.tile([P, CHUNK], F32, name="first", tag="first")
+            first = work.tile([P, CHUNK], F32, name="first", tag="first", bufs=FIRST_BUFS)
             second = work.tile([P, CHUNK], F32, name="second", tag="second")
             both = work.tile([P, CHUNK], F32, name="both", tag="both")
             total = work.tile([P, CHUNK], F32, name="total", tag="total")
             nc.vector.tensor_tensor(
-                out=first[:], in0=y_slots[:].indirect(pos1_sb[:, cols]), in1=gate1_sb[:, toks], op=MULT
+                out=first[:], in0=y_slots[:].indirect(pos1_sb[:, cols]), in1=gates[0][:, toks], op=MULT
             )
             nc.vector.tensor_tensor(
-                out=second[:], in0=y_slots[:].indirect(pos2_sb[:, cols]), in1=gate2_sb[:, toks], op=MULT
+                out=second[:], in0=y_slots[:].indirect(pos2_sb[:, cols]), in1=gates[1][:, toks], op=MULT
             )
-            nc.vector.tensor_tensor(out=both[:], in0=ys_bank[:], in1=first[:], op=ADD)
-            nc.vector.tensor_tensor(out=total[:], in0=both[:], in1=second[:], op=ADD)
+            if ADDORDER:
+                nc.vector.tensor_tensor(out=both[:], in0=ys_bank[:], in1=first[:], op=ADD)
+                nc.vector.tensor_tensor(out=total[:], in0=both[:], in1=second[:], op=ADD)
+            else:
+                nc.vector.tensor_tensor(out=both[:], in0=first[:], in1=second[:], op=ADD)
+                nc.vector.tensor_tensor(out=total[:], in0=ys_bank[:], in1=both[:], op=ADD)
             nc.sync.dma_start(out=out[:, toks], in_=total[:])
             t0 += CHUNK

@@ -20,19 +20,22 @@ ADD = mybir.AluOpType.add
 P = 128
 PACK = 4
 GATHER = 512
-STREAM_BUFS = 16
-LOADS = [["x",0],["offs",0],["xs",0],["w1",12],["w3",12],["w1",0],["w3",0],["w1",1],["w3",1],["w2",0],["pos",0],["w1",2],["w3",2],["w2",1],["w1",3],["w3",3],["w2",2],["w1",4],["w3",4],["w2",3],["w1",5],["w3",5],["w2",4],["w1",6],["w3",6],["w2",5],["w1",7],["w3",7],["w2",6],["w1",8],["w3",8],["w2",7],["w1",9],["w3",9],["w2",8],["w1",10],["w3",10],["w1",11],["w3",11],["w2",9],["w2",10],["w2",11],["w2",12],["gate",0],["gate",1]]
+STREAM_BUFS = 12
+LOADS = [["x",0],["offs",0],["xs",0],["w3",12],["w1",12],["w1",0],["w3",0],["w1",1],["w3",1],["w2",0],["pos",0],["w1",2],["w3",2],["w2",1],["w1",3],["w3",3],["w2",2],["w1",4],["w3",4],["w2",3],["w1",5],["w3",5],["w2",4],["w1",6],["w3",6],["w2",5],["w1",7],["w3",7],["w2",6],["w1",8],["w3",8],["w2",7],["w1",9],["w3",9],["w2",8],["w1",10],["w3",10],["w1",11],["w3",11],["w2",9],["w2",10],["w2",11],["w2",12],["gate",0],["gate",1]]
 C2V = [True,True,True,True,True,True,True,True,True,True,False,False,False]
 GPOS = [1,5,9]
-FORCE = [False,False,False,False,False,False,False,False,False,False,False,False,False]
+FORCE = [False,False,False,False,False,False,False,False,False,False,False,False,True]
 ORDER = [12,0,1,2,3,4,5,6,7,8,9,10,11]
 OUT_AFTER = [2,3,4,5,6,7,8,9,10,12,12,12]
-V1 = ["V","V","V","V","V","V","V","V","V","V","V","VV","S"]
-V3 = ["S","S","S","S","S","S","S","S","S","S","SS","SV","V"]
+V1 = ["SV","V","V","V","V","V","V","V","V","V","V","VV","SS"]
+V3 = ["V","S","S","S","S","S","S","S","S","S","SS","SV","S"]
 CHUNKS = [512,128,128]
 HALVES = True
 FIRST_BUFS = 3
-BF_BUFS = 2
+BF_BUFS = 4
+MERGE = {}
+XSQ = "sync"
+GATE1 = False
 ADDORDER = 1
 W1HALVES = True
 FINE = True
@@ -196,10 +199,16 @@ def tile_moe_shr_glu_gelu_kernel(
                     nc.sync.dma_start(out=pos2_sb[:], in_=pos2)
                 elif kind == "xs":
                     for q in range(4):
-                        nc.sync.dma_start(
+                        (nc.sync if XSQ == "sync" else nc.scalar).dma_start(
                             out=tok_scales[32 * q : 32 * q + 32, :].bitcast(I32),
                             in_=x_scales[0, 4 * q : 4 * q + 4, :].bitcast(I32).partition_broadcast(8),
                         )
+                elif kind == "gate" and GATE1:
+                    if not gates:
+                        both_gates = stream.tile([P, 2, T], F32, name="gate_sb", tag="raw")
+                        nc.sync.dma_start(out=both_gates[:], in_=gate.rearrange("g p t -> p g t"))
+                        gates[0] = both_gates[:, 0]
+                        gates[1] = both_gates[:, 1]
                 elif kind == "gate":
                     gates[index] = stream.tile([P, T], F32, name="gate_sb", tag="raw")
                     nc.sync.dma_start(out=gates[index][:], in_=gate[index])
@@ -208,7 +217,13 @@ def tile_moe_shr_glu_gelu_kernel(
                 elif kind == "w1" and index == ORDER[-1] and W1HALVES:
                     raws[kind, index] = [load(w1[index][:, : H // 2]), load(w1[index][:, H // 2 :])]
                 else:
-                    raws[kind, index] = [load({"w1": w1, "w3": w3, "w2": w2}[kind][index])]
+                    count = MERGE.get(kind + str(index), 1)
+                    if (kind, index) not in raws:
+                        source = {"w1": w1, "w3": w3, "w2": w2}[kind][index : index + count]
+                        raw = stream.tile([P, count, PACK, source.shape[2]], F32, name="raw", tag="raw")
+                        nc.sync.dma_start(out=raw[:], in_=source.rearrange("e (p j) c -> p e j c", j=PACK))
+                        for k in range(count):
+                            raws[kind, index + k] = [raw[:, k]]
 
         issue_until(*LOADS[-1])
         for step, e in enumerate(ORDER):

@@ -20,20 +20,20 @@ ADD = mybir.AluOpType.add
 P = 128
 PACK = 4
 GATHER = 512
-STREAM_BUFS = 12
-LOADS = [["x",0],["offs",0],["xs",0],["w3",12],["w1",12],["w1",0],["w3",0],["w1",1],["w3",1],["w2",0],["pos",0],["w1",2],["w3",2],["w2",1],["w1",3],["w3",3],["w2",2],["w1",4],["w3",4],["w2",3],["w1",5],["w3",5],["w2",4],["w1",6],["w3",6],["w2",5],["w1",7],["w3",7],["w2",6],["w1",8],["w3",8],["w2",7],["w1",9],["w3",9],["w2",8],["w1",10],["w3",10],["w1",11],["w3",11],["w2",9],["w2",10],["w2",11],["w2",12],["gate",0],["gate",1]]
-C2V = [True,True,True,True,True,True,True,True,True,True,False,False,False]
-GPOS = [1,5,9]
-FORCE = [False,False,False,False,False,False,False,False,False,False,False,False,True]
+STREAM_BUFS = 7
+LOADS = [["x",0],["offs",0],["w3",12],["xs",0],["w1",12],["w1",0],["w3",0],["w1",1],["w3",1],["pos",0],["w1",2],["w3",2],["w1",3],["w3",3],["w1",4],["w3",4],["w2",0],["w1",5],["w3",5],["w2",1],["w1",6],["w3",6],["w2",2],["w1",7],["w3",7],["w2",3],["w1",8],["w3",8],["w2",4],["w1",9],["w3",9],["w2",5],["w1",10],["w3",10],["w2",6],["w2",7],["w1",11],["w3",11],["w2",8],["w2",9],["w2",10],["w2",11],["w2",12],["gate",0],["gate",1]]
+C2V = [True,True,True,True,True,True,True,False,False,True,False,False,False]
+GPOS = [0,2,5]
+FORCE = [True,True,True,True,True,True,True,True,True,True,True,False,False]
 ORDER = [12,0,1,2,3,4,5,6,7,8,9,10,11]
-OUT_AFTER = [2,3,4,5,6,7,8,9,10,12,12,12]
-V1 = ["SV","V","V","V","V","V","V","V","V","V","V","VV","SS"]
-V3 = ["V","S","S","S","S","S","S","S","S","S","SS","SV","S"]
+OUT_AFTER = [5,6,7,8,9,10,11,12,12,12,12,12]
+V1 = ["V","S","V","S","V","S","V","S","V","S","V","VS","S"]
+V3 = ["V","S","V","S","V","S","V","S","V","S","S","V","VS"]
 CHUNKS = [512,128,128]
-HALVES = True
+HALVES = False
 FIRST_BUFS = 3
 BF_BUFS = 4
-MERGE = {}
+MERGE = {"w20":2,"w22":2,"w24":2,"w26":2,"w28":2,"w10":2,"w30":2,"w12":2,"w32":2,"w14":2,"w34":2,"w16":2,"w36":2,"w18":2,"w38":2}
 XSQ = "sync"
 GATE1 = False
 ADDORDER = 1

@@ -20,26 +20,9 @@ ADD = mybir.AluOpType.add
 P = 128
 PACK = 4
 GATHER = 512
-STREAM_BUFS = 7
-LOADS = [["x",0],["offs",0],["w3",12],["xs",0],["w1",12],["w1",0],["w3",0],["w1",1],["w3",1],["pos",0],["w1",2],["w3",2],["w1",3],["w3",3],["w1",4],["w3",4],["w2",0],["w1",5],["w3",5],["w2",1],["w1",6],["w3",6],["w2",2],["w1",7],["w3",7],["w2",3],["w1",8],["w3",8],["w2",4],["w1",9],["w3",9],["w2",5],["w1",10],["w3",10],["w2",6],["w2",7],["w1",11],["w3",11],["w2",8],["w2",9],["w2",10],["w2",11],["w2",12],["gate",0],["gate",1]]
-C2V = [True,True,True,True,True,True,True,False,False,True,False,False,False]
-GPOS = [0,2,5]
-FORCE = [True,True,True,True,True,True,True,True,True,True,True,False,False]
-ORDER = [12,0,1,2,3,4,5,6,7,8,9,10,11]
-OUT_AFTER = [5,6,7,8,9,10,11,12,12,12,12,12]
-V1 = ["V","S","V","S","V","S","V","S","V","S","V","VS","S"]
-V3 = ["V","S","V","S","V","S","V","S","V","S","S","V","VS"]
-CHUNKS = [512,128,128]
-HALVES = False
-FIRST_BUFS = 3
-BF_BUFS = 4
-MERGE = {"w20":2,"w22":2,"w24":2,"w26":2,"w28":2,"w10":2,"w30":2,"w12":2,"w32":2,"w14":2,"w34":2,"w16":2,"w36":2,"w18":2,"w38":2}
-XSQ = "sync"
-GATE1 = False
-ADDORDER = 1
-W1HALVES = True
-FINE = True
-GATHERS = [512,512,512]
+STREAM_BUFS = 15
+GROUP = 4
+CHUNKS = [384, 256, 128]
 
 
 def tile_moe_shr_glu_gelu_kernel(
@@ -64,209 +47,261 @@ def tile_moe_shr_glu_gelu_kernel(
         h_scales = keep.tile([P, S + T], U8, name="h_scales", align_bytes=64)
         y_slots = keep.tile([P, S], F32, name="y_slots")
 
-
-        def load(rows):
-            width = rows.shape[1]
-            raw = stream.tile([P, PACK, width], F32, name="raw", tag="raw")
+        def load_up(rows):
+            raw = stream.tile([P, PACK, rows.shape[1]], F32, name="raw", tag="raw")
             nc.sync.dma_start(out=raw[:], in_=rows.rearrange("(p j) c -> p j c", j=PACK))
             return raw
 
-        def cast(on_vector, dst, src):
-            if on_vector:
+        def load_down(e0, count):
+            raw = stream.tile([P, count, PACK, N], F32, name="raw", tag="raw")
+            nc.sync.dma_start(out=raw[:], in_=w2[e0 : e0 + count].rearrange("e (p j) c -> p e j c", j=PACK))
+            return raw
+
+        def load_gate(r):
+            tile = stream.tile([P, T], F32, name="raw", tag="raw")
+            nc.sync.dma_start(out=tile[:], in_=gate[r])
+            return tile
+
+        def cast(engine, dst, src):
+            if engine == "V":
                 nc.vector.tensor_copy(out=dst, in_=src)
             else:
                 nc.scalar.copy(out=dst, in_=src)
 
         def quantize(grouped, tag):
             width = grouped.shape[1] // PACK
-            codes = work.tile([P, width], U32, name=tag + "_codes", tag=tag + "_codes", align_bytes=64)
-            scales = work.tile([P, width], U8, name=tag + "_scales", tag=tag + "_scales", align_bytes=64)
+            bufs = 2 if width > N else 3
+            tag = tag + str(width)
+            codes = work.tile([P, width], U32, name=tag + "_codes", tag=tag + "_codes", align_bytes=64, bufs=bufs)
+            scales = work.tile([P, width], U8, name=tag + "_scales", tag=tag + "_scales", align_bytes=64, bufs=bufs)
             nc.vector.quantize_mx(out=codes[:].bitcast(FP8X4), scales=scales[:], in_=grouped[:])
             return codes, scales
 
-        def up_weights(pieces, engines, tag):
-            codes = work.tile([P, H], U32, name=tag + "_codes", tag=tag + "_codes", align_bytes=64)
-            scales = work.tile([P, H], U8, name=tag + "_scales", tag=tag + "_scales", align_bytes=64)
-            views = [raw[:].rearrange("p j (m t) -> p m j t", t=PACK) for raw in pieces]
-            if len(engines) > len(views):
-                views = [views[0][:, : P // 2], views[0][:, P // 2 :]]
-            count = P // len(views)
-            for half, src in enumerate(views):
-                grouped = work.tile([P, PACK * PACK * count], BF16, name=tag + "_bf", tag=tag + "_bf", align_bytes=64, bufs=BF_BUFS)
-                cast(engines[half] == "V", grouped[:].rearrange("p (t m j) -> p m j t", t=PACK, j=PACK), src)
-                if count == P:
-                    nc.vector.quantize_mx(out=codes[:].bitcast(FP8X4), scales=scales[:], in_=grouped[:])
-                else:
-                    for t in range(PACK):
-                        c0 = P * t + count * half
-                        nc.vector.quantize_mx(
-                            out=codes[:, c0 : c0 + count].bitcast(FP8X4),
-                            scales=scales[:, c0 : c0 + count],
-                            in_=grouped[:, PACK * count * t : PACK * count * (t + 1)],
-                        )
-            return codes, scales
+        def up_tile(count, tag):
+            return work.tile([P, count * PACK * H], BF16, name=tag + "_bf", tag=tag + "_bf", align_bytes=64, bufs=3)
 
-        def down_weights(raw, on_vector):
-            grouped = work.tile([P, PACK * N], BF16, name="w2_bf", tag="w2_bf", align_bytes=64)
+        def round_up(grouped, slot, m0, raw, engine):
+            view = grouped[:, slot * PACK * H : (slot + 1) * PACK * H].rearrange("p (t m j) -> p m j t", t=PACK, j=PACK)
+            count = raw.shape[2] // PACK
+            cast(engine, view[:, m0 : m0 + count], raw[:].rearrange("p j (m t) -> p m j t", t=PACK))
+
+        def round_down(raw, engine):
+            count = raw.shape[1]
+            grouped = work.tile([P, count * PACK * N], BF16, name="w2_bf", tag="w2_bf" + str(count), align_bytes=64, bufs=1 if count > 1 else 3)
             cast(
-                on_vector,
-                grouped[:].rearrange("p (c i j) -> p c j i", i=4, j=PACK),
-                raw[:].rearrange("p j (c i) -> p c j i", i=4),
+                engine,
+                grouped[:].rearrange("p (e c i j) -> p e c j i", e=count, i=4, j=PACK),
+                raw[:].rearrange("p e j (c i) -> p e c j i", i=4),
             )
-            return quantize(grouped, "w2")
+            return grouped
 
-        def up_product(weights, words, scales, tag):
+        def product(bank, weights, cols, words, scales):
             codes, code_scales = weights
-            bank = up_psum.tile([P, PACK, C], F32, name=tag, tag=tag)
-            for t in range(PACK):
-                cols = slice(P * t, P * (t + 1))
-                nc.tensor.matmul_mx(
-                    out=bank[:, t, :],
-                    lhsT=codes[:, cols].bitcast(FP8X4),
-                    lhsT_scale=code_scales[:, cols],
-                    rhs=words.bitcast(FP8X4),
-                    rhs_scale=scales,
-                    start=True,
-                    stop=True,
-                )
-            return bank
-
-        def activate(w1q, words, scales, room):
-            a_bank = up_product(w1q, words, scales, "a_bank")
-            if room is None:
-                act = work.tile([P, C, PACK], F32, name="act", tag="act")[:]
-            else:
-                act = room.rearrange("p (n t) -> p n t", t=PACK)
-            nc.scalar.activation(out=act, in_=a_bank[:].rearrange("p t n -> p n t"), func=GELU)
-            return act
-
-        def hidden(act, w3q, words, scales, h0):
-            b_bank = up_product(w3q, words, scales, "b_bank")
-            h_bf = work.tile([P, C, PACK], BF16, name="h_bf", tag="h_bf", align_bytes=64)
-            nc.vector.tensor_tensor(
-                out=h_bf[:], in0=b_bank[:].rearrange("p t n -> p n t"), in1=act, op=MULT
-            )
-            nc.vector.quantize_mx(
-                out=h_codes[:, h0 : h0 + C].bitcast(FP8X4),
-                scales=h_scales[:, h0 : h0 + C],
-                in_=h_bf[:].rearrange("p n t -> p (n t)"),
-            )
-
-        def down_product(w2q, h0, count, bank):
-            codes, code_scales = w2q
             nc.tensor.matmul_mx(
                 out=bank,
-                lhsT=codes[:].bitcast(FP8X4),
-                lhsT_scale=code_scales[:],
-                rhs=h_codes[:, h0 : h0 + count].bitcast(FP8X4),
-                rhs_scale=h_scales[:, h0 : h0 + count],
+                lhsT=codes[:, cols].bitcast(FP8X4),
+                lhsT_scale=code_scales[:, cols],
+                rhs=words.bitcast(FP8X4),
+                rhs_scale=scales,
                 start=True,
                 stop=True,
             )
 
-        def expert_output(e, w2_raw):
-            w2q = down_weights(w2_raw, C2V[e])
-            bank = down_psum.tile([P, C], F32, name="y_bank", tag="y_bank")
-            down_product(w2q, e * C, C, bank[:])
-            nc.scalar.copy(out=y_slots[:, e * C : (e + 1) * C], in_=bank[:])
+        def up_product(weights, slot, words, scales, tag):
+            bank = up_psum.tile([P, PACK, C], F32, name=tag, tag=tag)
+            for t in range(PACK):
+                c0 = slot * H + P * t
+                product(bank[:, t, :], weights, slice(c0, c0 + P), words, scales)
+            return bank[:].rearrange("p t n -> p n t")
+
+        def column_groups(experts):
+            if experts == [E]:
+                return [(0, tok_words[:, t0 : t0 + C], tok_scales[:, t0 : t0 + C]) for t0 in range(0, T, C)]
+            return [
+                (slot, slot_words[:, e * C : (e + 1) * C], slot_scales[:, e * C : (e + 1) * C])
+                for slot, e in enumerate(experts)
+            ]
+
+        def rooms_of(raw):
+            flat = raw[:].rearrange("p j c -> p (j c)")
+            return [
+                flat[:, c0 : c0 + PACK * C].rearrange("p (n t) -> p n t", t=PACK)
+                for c0 in range(0, flat.shape[1], PACK * C)
+            ]
+
+        def activations(experts, w1q, rooms):
+            groups = column_groups(experts)
+            for columns, room in zip(groups, rooms):
+                nc.scalar.activation(out=room, in_=up_product(w1q, *columns, "a_bank"), func=GELU)
+            return rooms[: len(groups)]
+
+        def hidden(experts, w3q, acts):
+            if experts == [E]:
+                h_bf = keep.tile([P, PACK * T], BF16, name="hs_bf", align_bytes=64)
+            else:
+                h_bf = work.tile([P, len(experts) * PACK * C], BF16, name="h_bf", tag="h_bf", align_bytes=64, bufs=2)
+            for i, columns in enumerate(column_groups(experts)):
+                view = h_bf[:, i * PACK * C : (i + 1) * PACK * C].rearrange("p (n t) -> p n t", t=PACK)
+                nc.vector.tensor_tensor(out=view, in0=up_product(w3q, *columns, "b_bank"), in1=acts[i], op=MULT)
+            return h_bf
+
+        def quantize_hidden(experts, h_bf):
+            total = h_bf.shape[1] // PACK
+            width = min(total, 2 * C)
+            for c0 in range(0, total, width):
+                h0 = experts[0] * C + c0
+                nc.vector.quantize_mx(
+                    out=h_codes[:, h0 : h0 + width].bitcast(FP8X4),
+                    scales=h_scales[:, h0 : h0 + width],
+                    in_=h_bf[:, c0 * PACK : (c0 + width) * PACK],
+                )
+
+        def slot_outputs(e0, w2q):
+            count = w2q[0].shape[1] // N
+            bank = down_psum.tile([P, count * C], F32, name="y_bank", tag="y_bank")
+            for i in range(count):
+                cols = slice((e0 + i) * C, (e0 + i + 1) * C)
+                product(bank[:, i * C : (i + 1) * C], w2q, slice(i * N, (i + 1) * N), h_codes[:, cols], h_scales[:, cols])
+            nc.scalar.copy(out=y_slots[:, e0 * C : (e0 + count) * C], in_=bank[:])
 
         def gather_slots(s0):
             offsets = offs_sb[:, s0 // 16 : (s0 + GATHER) // 16]
-            nc.vector.tensor_copy(
-                out=slot_words[:, s0 : s0 + GATHER],
-                in_=tok_words[:].bitcast(U32).indirect(offsets),
+            nc.vector.tensor_copy(out=slot_words[:, s0 : s0 + GATHER], in_=tok_words[:].bitcast(U32).indirect(offsets))
+            nc.vector.tensor_copy(out=slot_scales[:, s0 : s0 + GATHER], in_=tok_scales[:].indirect(offsets))
+
+        last = E - 1
+        half = H // 2
+
+        nc.sync.dma_start(out=tok_words[:], in_=x_words[0].rearrange("p t r -> p (t r)").bitcast(I32))
+        nc.sync.dma_start(out=offs_sb[:], in_=offs)
+        raw1, raw3, raw2 = {}, {}, {}
+        raw1[E] = load_up(w1[E])
+        for q in range(4):
+            nc.sync.dma_start(
+                out=tok_scales[32 * q : 32 * q + 32, :].bitcast(I32),
+                in_=x_scales[0, 4 * q : 4 * q + 4, :].bitcast(I32).partition_broadcast(8),
             )
-            nc.vector.tensor_copy(
-                out=slot_scales[:, s0 : s0 + GATHER], in_=tok_scales[:].indirect(offsets)
-            )
+        raw3[E] = load_up(w3[E])
+        for e in range(last):
+            raw1[e] = load_up(w1[e])
+            raw3[e] = load_up(w3[e])
+            if e == 1:
+                nc.sync.dma_start(out=pos1_sb[:], in_=pos1)
+                nc.sync.dma_start(out=pos2_sb[:], in_=pos2)
+            if (e + 1) % GROUP == 0:
+                raw2[e + 1 - GROUP] = load_down(e + 1 - GROUP, GROUP)
+        last1 = [load_up(w1[last][:, :half]), load_up(w1[last][:, half:])]
+        last3 = [load_up(w3[last][:, :half]), load_up(w3[last][:, half:])]
+        raw2[10] = load_down(10, 2)
+        raw2[8] = load_down(8, 1)
+        raw2[9] = load_down(9, 1)
+        raw2[E] = load_down(E, 1)
+        gates = [load_gate(0), load_gate(1)]
 
-        raws = {}
-        gates = {}
-        issued = []
+        gather_slots(0)
+        w1_bf = up_tile(1, "w1")
+        round_up(w1_bf, 0, 0, raw1[E], "S")
+        w1q = quantize(w1_bf, "w1")
+        w3_bf = up_tile(1, "w3")
+        round_up(w3_bf, 0, 0, raw3[E], "S")
+        w3q = quantize(w3_bf, "w3")
+        gather_slots(GATHER)
+        gather_slots(2 * GATHER)
+        before = [E]
+        w2q = None
+        for e in range(last):
+            w1_bf = up_tile(1, "w1")
+            round_up(w1_bf, 0, 0, raw1[e], "S")
+            acts = activations(before, w1q, rooms_of(raw1[e]) + rooms_of(raw1[before[0]]))
+            w1q = quantize(w1_bf, "w1")
+            w3_bf = up_tile(1, "w3")
+            round_up(w3_bf, 0, 0, raw3[e], "V")
+            h_bf = hidden(before, w3q, acts)
+            w3q = quantize(w3_bf, "w3")
+            quantize_hidden(before, h_bf)
+            if w2q is not None:
+                slot_outputs(e - GROUP, w2q)
+                w2q = None
+            if (e + 1) % GROUP == 0:
+                w2q = quantize(round_down(raw2[e + 1 - GROUP], "S"), "w2")
+            before = [e]
 
-        def issue_until(name, e):
-            while (name, e) not in issued:
-                kind, index = LOADS[len(issued)]
-                issued.append((kind, index))
-                if kind == "x":
-                    nc.sync.dma_start(
-                        out=tok_words[:], in_=x_words[0].rearrange("p t r -> p (t r)").bitcast(I32)
-                    )
-                elif kind == "offs":
-                    nc.sync.dma_start(out=offs_sb[:], in_=offs)
-                elif kind == "pos":
-                    nc.sync.dma_start(out=pos1_sb[:], in_=pos1)
-                    nc.sync.dma_start(out=pos2_sb[:], in_=pos2)
-                elif kind == "xs":
-                    for q in range(4):
-                        (nc.sync if XSQ == "sync" else nc.scalar).dma_start(
-                            out=tok_scales[32 * q : 32 * q + 32, :].bitcast(I32),
-                            in_=x_scales[0, 4 * q : 4 * q + 4, :].bitcast(I32).partition_broadcast(8),
-                        )
-                elif kind == "gate" and GATE1:
-                    if not gates:
-                        both_gates = stream.tile([P, 2, T], F32, name="gate_sb", tag="raw")
-                        nc.sync.dma_start(out=both_gates[:], in_=gate.rearrange("g p t -> p g t"))
-                        gates[0] = both_gates[:, 0]
-                        gates[1] = both_gates[:, 1]
-                elif kind == "gate":
-                    gates[index] = stream.tile([P, T], F32, name="gate_sb", tag="raw")
-                    nc.sync.dma_start(out=gates[index][:], in_=gate[index])
-                elif kind == "w3" and index == ORDER[-1] and HALVES:
-                    raws[kind, index] = [load(w3[index][:, : H // 2]), load(w3[index][:, H // 2 :])]
-                elif kind == "w1" and index == ORDER[-1] and W1HALVES:
-                    raws[kind, index] = [load(w1[index][:, : H // 2]), load(w1[index][:, H // 2 :])]
-                else:
-                    count = MERGE.get(kind + str(index), 1)
-                    if (kind, index) not in raws:
-                        source = {"w1": w1, "w3": w3, "w2": w2}[kind][index : index + count]
-                        raw = stream.tile([P, count, PACK, source.shape[2]], F32, name="raw", tag="raw")
-                        nc.sync.dma_start(out=raw[:], in_=source.rearrange("e (p j) c -> p e j c", j=PACK))
-                        for k in range(count):
-                            raws[kind, index + k] = [raw[:, k]]
+        w1_bf = up_tile(1, "w1")
+        round_up(w1_bf, 0, 0, last1[0], "S")
+        round_up(w1_bf, 0, P // 2, last1[1], "S")
+        acts = activations(before, w1q, rooms_of(last1[1]))
+        w1q = quantize(w1_bf, "w1")
 
-        issue_until(*LOADS[-1])
-        for step, e in enumerate(ORDER):
-            for g in range(3):
-                if GPOS[g] == step:
-                    gather_slots(g * GATHER)
-            w1q = up_weights(raws["w1", e], V1[e], "w1")
-            w3q = up_weights(raws["w3", e], V3[e], "w3")
-            spent = raws["w3", e][0][:].rearrange("p j c -> p (j c)")
-            if e == E:
-                groups = [(tok_words[:, t0 : t0 + C], tok_scales[:, t0 : t0 + C], S + t0) for t0 in range(0, T, C)]
-            else:
-                groups = [(slot_words[:, e * C : (e + 1) * C], slot_scales[:, e * C : (e + 1) * C], e * C)]
-            for i, (words, scales, h0) in enumerate(groups):
-                room = spent[:, 512 * (i % 4) : 512 * (i % 4 + 1)] if FORCE[e] else None
-                act = activate(w1q, words, scales, room)
-                hidden(act, w3q, words, scales, h0)
-            for d in range(E):
-                if OUT_AFTER[d] == step:
-                    expert_output(d, raws["w2", d][0])
+        parts = [work.tile([P, PACK * half], BF16, name="w3_part", tag="w3_part", align_bytes=64, bufs=2) for i in range(2)]
 
-        w2q = down_weights(raws["w2", E][0], C2V[E])
-        t0 = 0
-        for CHUNK in CHUNKS:
-            toks = slice(t0, t0 + CHUNK)
-            cols = slice(t0 // 16, (t0 + CHUNK) // 16)
-            ys_bank = up_psum.tile([P, CHUNK], F32, name="ys_bank", tag="a_bank")
-            down_product(w2q, S + t0, CHUNK, ys_bank[:])
-            first = work.tile([P, CHUNK], F32, name="first", tag="first", bufs=FIRST_BUFS)
-            second = work.tile([P, CHUNK], F32, name="second", tag="second")
-            both = work.tile([P, CHUNK], F32, name="both", tag="both")
-            total = work.tile([P, CHUNK], F32, name="total", tag="total")
+        def round_last(i):
+            source = last3[i][:].rearrange("p j (m t) -> p m j t", t=PACK)
+            for u, engine in enumerate("VS"):
+                view = parts[u][:].rearrange("p (t m j) -> p m j t", t=2, j=PACK)
+                cast(engine, view[:, i * P // 2 : (i + 1) * P // 2], source[:, :, :, 2 * u : 2 * u + 2])
+
+        round_last(0)
+        h_bf = hidden(before, w3q, acts)
+        round_last(1)
+        quantize_hidden(before, h_bf)
+        acts = activations([last], w1q, rooms_of(last3[1]))
+        codes = work.tile([P, H], U32, name="w3_codes", tag="w3512_codes", align_bytes=64, bufs=2)
+        scales = work.tile([P, H], U8, name="w3_scales", tag="w3512_scales", align_bytes=64, bufs=2)
+        for u in range(2):
+            cols = slice(u * half, (u + 1) * half)
+            nc.vector.quantize_mx(out=codes[:, cols].bitcast(FP8X4), scales=scales[:, cols], in_=parts[u][:])
+        w2q = quantize(round_down(raw2[10], "V"), "w2")
+        h_bf = hidden([last], (codes, scales), acts)
+        bank = down_psum.tile([P, 2 * C], F32, name="y_bank", tag="y_bank")
+        for i in range(2):
+            weights = quantize(round_down(raw2[8 + i], "S"), "w2")
+            cols = slice((8 + i) * C, (9 + i) * C)
+            product(bank[:, i * C : (i + 1) * C], weights, slice(0, N), h_codes[:, cols], h_scales[:, cols])
+            if i == 0:
+                quantize_hidden([last], h_bf)
+                slot_outputs(10, w2q)
+        nc.scalar.copy(out=y_slots[:, 8 * C : 10 * C], in_=bank[:])
+        shared_bf = round_down(raw2[E], "S")
+
+        w2q = quantize(shared_bf, "w2")
+        starts = [sum(CHUNKS[:i]) for i in range(len(CHUNKS))]
+        banks, firsts, seconds = [], [], []
+        for t0, width in zip(starts, CHUNKS):
+            bank = up_psum.tile([P, width], F32, name="ys_bank", tag="a_bank")
+            done = 0
+            for piece in (256, 128):
+                if width - done >= piece:
+                    cols = slice(S + t0 + done, S + t0 + done + piece)
+                    product(bank[:, done : done + piece], w2q, slice(0, N), h_codes[:, cols], h_scales[:, cols])
+                    done = done + piece
+            banks.append(bank)
+
+        def fetch(i, pos_sb, r):
+            t0, width = starts[i], CHUNKS[i]
+            part = work.tile([P, width], F32, name="part", tag="part" + str(r))
             nc.vector.tensor_tensor(
-                out=first[:], in0=y_slots[:].indirect(pos1_sb[:, cols]), in1=gates[0][:, toks], op=MULT
+                out=part[:],
+                in0=y_slots[:].indirect(pos_sb[:, t0 // 16 : (t0 + width) // 16]),
+                in1=gates[r][:, t0 : t0 + width],
+                op=MULT,
             )
-            nc.vector.tensor_tensor(
-                out=second[:], in0=y_slots[:].indirect(pos2_sb[:, cols]), in1=gates[1][:, toks], op=MULT
-            )
-            if ADDORDER:
-                nc.vector.tensor_tensor(out=both[:], in0=ys_bank[:], in1=first[:], op=ADD)
-                nc.vector.tensor_tensor(out=total[:], in0=both[:], in1=second[:], op=ADD)
-            else:
-                nc.vector.tensor_tensor(out=both[:], in0=first[:], in1=second[:], op=ADD)
-                nc.vector.tensor_tensor(out=total[:], in0=ys_bank[:], in1=both[:], op=ADD)
-            nc.sync.dma_start(out=out[:, toks], in_=total[:])
-            t0 += CHUNK
+            return part
+
+        def add(a, b, tag):
+            total = work.tile([P, a.shape[1]], F32, name=tag, tag=tag)
+            nc.vector.tensor_tensor(out=total[:], in0=a[:], in1=b[:], op=ADD)
+            return total
+
+        first = fetch(0, pos1_sb, 0)
+        second = fetch(0, pos2_sb, 1)
+        for i in range(len(CHUNKS)):
+            more = i + 1 < len(CHUNKS)
+            if more:
+                next_first = fetch(i + 1, pos1_sb, 0)
+            both = add(banks[i], first, "both")
+            if more:
+                next_second = fetch(i + 1, pos2_sb, 1)
+            total = add(both, second, "total")
+            nc.sync.dma_start(out=out[:, starts[i] : starts[i] + CHUNKS[i]], in_=total[:])
+            if more:
+                first, second = next_first, next_second

@@ -1,6 +1,7 @@
 from contextlib import ExitStack
 
 import concourse.mybir as mybir
+from concourse.masks import make_identity
 
 K, T, E, C, H, N = 512, 768, 12, 128, 512, 128
 S = E * C
@@ -20,9 +21,10 @@ ADD = mybir.AluOpType.add
 P = 128
 PACK = 4
 GATHER = 512
-STREAM_BUFS = 15
-GROUP = 4
-CHUNKS = [384, 256, 128]
+STREAM_BUFS = 14
+EARLY = {3: (0, 4), 6: (4, 2)}
+TURNED = 384
+CHUNKS = [(0, 256), (256, 128)]
 
 
 def tile_moe_shr_glu_gelu_kernel(
@@ -46,21 +48,18 @@ def tile_moe_shr_glu_gelu_kernel(
         h_codes = keep.tile([P, S + T], U32, name="h_codes", align_bytes=64)
         h_scales = keep.tile([P, S + T], U8, name="h_scales", align_bytes=64)
         y_slots = keep.tile([P, S], F32, name="y_slots")
+        identity = keep.tile([P, P], F32, name="identity")
+        make_identity(nc, identity[:])
 
         def load_up(rows):
-            raw = stream.tile([P, PACK, rows.shape[1]], F32, name="raw", tag="raw")
+            raw = stream.tile([P, PACK, rows.shape[1]], F32, name="raw", tag="raw", align_bytes=64)
             nc.sync.dma_start(out=raw[:], in_=rows.rearrange("(p j) c -> p j c", j=PACK))
             return raw
 
         def load_down(e0, count):
-            raw = stream.tile([P, count, PACK, N], F32, name="raw", tag="raw")
+            raw = stream.tile([P, count, PACK, N], F32, name="raw", tag="raw", align_bytes=64)
             nc.sync.dma_start(out=raw[:], in_=w2[e0 : e0 + count].rearrange("e (p j) c -> p e j c", j=PACK))
             return raw
-
-        def load_gate(r):
-            tile = stream.tile([P, T], F32, name="raw", tag="raw")
-            nc.sync.dma_start(out=tile[:], in_=gate[r])
-            return tile
 
         def cast(engine, dst, src):
             if engine == "V":
@@ -85,9 +84,12 @@ def tile_moe_shr_glu_gelu_kernel(
             count = raw.shape[2] // PACK
             cast(engine, view[:, m0 : m0 + count], raw[:].rearrange("p j (m t) -> p m j t", t=PACK))
 
-        def round_down(raw, engine):
+        def round_down(raw, engine, grouped=None):
             count = raw.shape[1]
-            grouped = work.tile([P, count * PACK * N], BF16, name="w2_bf", tag="w2_bf" + str(count), align_bytes=64, bufs=1 if count > 1 else 3)
+            if grouped is None:
+                grouped = work.tile(
+                    [P, count * PACK * N], BF16, name="w2_bf", tag="w2_bf" + str(count), align_bytes=64, bufs=2 if count <= 2 else 1
+                )
             cast(
                 engine,
                 grouped[:].rearrange("p (e c i j) -> p e c j i", e=count, i=4, j=PACK),
@@ -182,21 +184,25 @@ def tile_moe_shr_glu_gelu_kernel(
                 in_=x_scales[0, 4 * q : 4 * q + 4, :].bitcast(I32).partition_broadcast(8),
             )
         raw3[E] = load_up(w3[E])
-        for e in range(last):
+        for e in range(last - 1):
             raw1[e] = load_up(w1[e])
             raw3[e] = load_up(w3[e])
             if e == 1:
                 nc.sync.dma_start(out=pos1_sb[:], in_=pos1)
                 nc.sync.dma_start(out=pos2_sb[:], in_=pos2)
-            if (e + 1) % GROUP == 0:
-                raw2[e + 1 - GROUP] = load_down(e + 1 - GROUP, GROUP)
-        last1 = [load_up(w1[last][:, :half]), load_up(w1[last][:, half:])]
-        last3 = [load_up(w3[last][:, :half]), load_up(w3[last][:, half:])]
+            if e in EARLY:
+                raw2[EARLY[e][0]] = load_down(*EARLY[e])
+        for e in (10, 11):
+            raw1[e] = load_up(w1[e])
+        for e in (10, 11):
+            raw3[e] = load_up(w3[e])
         raw2[10] = load_down(10, 2)
+        raw2[6] = load_down(6, 2)
         raw2[8] = load_down(8, 1)
         raw2[9] = load_down(9, 1)
         raw2[E] = load_down(E, 1)
-        gates = [load_gate(0), load_gate(1)]
+        gates = stream.tile([P, 2, T], F32, name="raw", tag="raw", align_bytes=64)
+        nc.sync.dma_start(out=gates[:], in_=gate.rearrange("g p t -> p g t"))
 
         gather_slots(0)
         w1_bf = up_tile(1, "w1")
@@ -208,8 +214,7 @@ def tile_moe_shr_glu_gelu_kernel(
         gather_slots(GATHER)
         gather_slots(2 * GATHER)
         before = [E]
-        w2q = None
-        for e in range(last):
+        for e in range(last - 1):
             w1_bf = up_tile(1, "w1")
             round_up(w1_bf, 0, 0, raw1[e], "S")
             acts = activations(before, w1q, rooms_of(raw1[e]) + rooms_of(raw1[before[0]]))
@@ -219,89 +224,116 @@ def tile_moe_shr_glu_gelu_kernel(
             h_bf = hidden(before, w3q, acts)
             w3q = quantize(w3_bf, "w3")
             quantize_hidden(before, h_bf)
-            if w2q is not None:
-                slot_outputs(e - GROUP, w2q)
-                w2q = None
-            if (e + 1) % GROUP == 0:
-                w2q = quantize(round_down(raw2[e + 1 - GROUP], "S"), "w2")
+            if e - 1 in EARLY:
+                slot_outputs(EARLY[e - 1][0], w2q)
+            if e in EARLY:
+                w2q = quantize(round_down(raw2[EARLY[e][0]], "S"), "w2")
             before = [e]
 
-        w1_bf = up_tile(1, "w1")
-        round_up(w1_bf, 0, 0, last1[0], "S")
-        round_up(w1_bf, 0, P // 2, last1[1], "S")
-        acts = activations(before, w1q, rooms_of(last1[1]))
-        w1q = quantize(w1_bf, "w1")
-
-        parts = [work.tile([P, PACK * half], BF16, name="w3_part", tag="w3_part", align_bytes=64, bufs=2) for i in range(2)]
-
-        def round_last(i):
-            source = last3[i][:].rearrange("p j (m t) -> p m j t", t=PACK)
+        def round_shared(raw):
+            source = raw[:].rearrange("p j (m t) -> p m j t", t=PACK)
+            parts = []
             for u, engine in enumerate("VS"):
-                view = parts[u][:].rearrange("p (t m j) -> p m j t", t=2, j=PACK)
-                cast(engine, view[:, i * P // 2 : (i + 1) * P // 2], source[:, :, :, 2 * u : 2 * u + 2])
+                part = work.tile([P, PACK * half], BF16, name="part_bf", tag="part_bf", align_bytes=64, bufs=4)
+                view = part[:].rearrange("p (t m j) -> p m j t", t=2, j=PACK)
+                cast(engine, view, source[:, :, :, 2 * u : 2 * u + 2])
+                parts.append(part)
+            return parts
 
-        round_last(0)
+        def quantize_parts(parts, tag):
+            codes = work.tile([P, H], U32, name="codes", tag=tag + "512_codes", align_bytes=64, bufs=2)
+            scales = work.tile([P, H], U8, name="scales", tag=tag + "512_scales", align_bytes=64, bufs=2)
+            for u in range(2):
+                cols = slice(u * half, (u + 1) * half)
+                nc.vector.quantize_mx(out=codes[:, cols].bitcast(FP8X4), scales=scales[:, cols], in_=parts[u][:])
+            return codes, scales
+
+        w1_bf = up_tile(1, "w1")
+        round_up(w1_bf, 0, 0, raw1[10], "S")
+        acts = activations(before, w1q, rooms_of(raw1[10]))
+        w1q = quantize(w1_bf, "w1")
+        parts = round_shared(raw1[11])
         h_bf = hidden(before, w3q, acts)
-        round_last(1)
+        acts = activations([10], w1q, rooms_of(raw1[11]))
+        w1q = quantize_parts(parts, "w1")
         quantize_hidden(before, h_bf)
-        acts = activations([last], w1q, rooms_of(last3[1]))
-        codes = work.tile([P, H], U32, name="w3_codes", tag="w3512_codes", align_bytes=64, bufs=2)
-        scales = work.tile([P, H], U8, name="w3_scales", tag="w3512_scales", align_bytes=64, bufs=2)
-        for u in range(2):
-            cols = slice(u * half, (u + 1) * half)
-            nc.vector.quantize_mx(out=codes[:, cols].bitcast(FP8X4), scales=scales[:, cols], in_=parts[u][:])
-        w2q = quantize(round_down(raw2[10], "V"), "w2")
-        h_bf = hidden([last], (codes, scales), acts)
-        bank = down_psum.tile([P, 2 * C], F32, name="y_bank", tag="y_bank")
+        parts = round_shared(raw3[10])
+        acts = acts + activations([11], w1q, rooms_of(raw3[10]))
+        w3q = [quantize_parts(parts, "w3")]
+        w3q.append(quantize_parts(round_shared(raw3[11]), "w3"))
+        h_bf = raw3[11][:, 0, :].bitcast(BF16)
         for i in range(2):
-            weights = quantize(round_down(raw2[8 + i], "S"), "w2")
+            view = h_bf[:, i * PACK * C : (i + 1) * PACK * C].rearrange("p (n t) -> p n t", t=PACK)
+            columns = column_groups([10 + i])[0]
+            nc.vector.tensor_tensor(out=view, in0=up_product(w3q[i], *columns, "b_bank"), in1=acts[i], op=MULT)
+        w2q = quantize(round_down(raw2[10], "S"), "w2")
+        pair_bf = round_down(raw2[6], "S")
+        late_bf = [round_down(raw2[e], "S") for e in (8, 9)]
+        quantize_hidden([10, 11], h_bf)
+        slot_outputs(10, w2q)
+        slot_outputs(6, quantize(pair_bf, "w2"))
+        bank = up_psum.tile([P, 2 * C], F32, name="y_bank", tag="a_bank")
+        for i in range(2):
+            weights = quantize(late_bf[i], "w2")
             cols = slice((8 + i) * C, (9 + i) * C)
             product(bank[:, i * C : (i + 1) * C], weights, slice(0, N), h_codes[:, cols], h_scales[:, cols])
-            if i == 0:
-                quantize_hidden([last], h_bf)
-                slot_outputs(10, w2q)
-        nc.scalar.copy(out=y_slots[:, 8 * C : 10 * C], in_=bank[:])
-        shared_bf = round_down(raw2[E], "S")
+        shared_bf = round_down(raw2[E], "V", late_bf[1])
+        nc.vector.tensor_copy(out=y_slots[:, 8 * C : 10 * C], in_=bank[:])
 
         w2q = quantize(shared_bf, "w2")
-        starts = [sum(CHUNKS[:i]) for i in range(len(CHUNKS))]
-        banks, firsts, seconds = [], [], []
-        for t0, width in zip(starts, CHUNKS):
+        ys_banks = []
+        for t0, width in ((0, TURNED), (TURNED, T - TURNED)):
             bank = up_psum.tile([P, width], F32, name="ys_bank", tag="a_bank")
-            done = 0
-            for piece in (256, 128):
-                if width - done >= piece:
-                    cols = slice(S + t0 + done, S + t0 + done + piece)
-                    product(bank[:, done : done + piece], w2q, slice(0, N), h_codes[:, cols], h_scales[:, cols])
-                    done = done + piece
-            banks.append(bank)
+            for c0, piece in CHUNKS:
+                cols = slice(S + t0 + c0, S + t0 + c0 + piece)
+                product(bank[:, c0 : c0 + piece], w2q, slice(0, N), h_codes[:, cols], h_scales[:, cols])
+            ys_banks.append(bank)
+        ys_sb = keep.tile([P, TURNED], F32, name="ys_sb")
+        nc.scalar.copy(out=ys_sb[:], in_=ys_banks[0][:])
 
-        def fetch(i, pos_sb, r):
-            t0, width = starts[i], CHUNKS[i]
-            part = work.tile([P, width], F32, name="part", tag="part" + str(r))
+        parts = keep.tile([P, 2, T], F32, name="parts")
+
+        def fetch(t0, width, r):
+            part = parts[:, r, t0 : t0 + width]
             nc.vector.tensor_tensor(
-                out=part[:],
-                in0=y_slots[:].indirect(pos_sb[:, t0 // 16 : (t0 + width) // 16]),
-                in1=gates[r][:, t0 : t0 + width],
+                out=part,
+                in0=y_slots[:].indirect((pos1_sb, pos2_sb)[r][:, t0 // 16 : (t0 + width) // 16]),
+                in1=gates[:, r, t0 : t0 + width],
                 op=MULT,
             )
             return part
 
-        def add(a, b, tag):
-            total = work.tile([P, a.shape[1]], F32, name=tag, tag=tag)
-            nc.vector.tensor_tensor(out=total[:], in0=a[:], in1=b[:], op=ADD)
+        turned = []
+        for t0, width in CHUNKS:
+            fetch(t0, width, 0)
+            fetch(t0, width, 1)
+            for c0 in range(t0, t0 + width, P):
+                terms = (ys_sb[:, c0 : c0 + P], parts[:, 0, c0 : c0 + P], parts[:, 1, c0 : c0 + P])
+                sums = up_psum.tile([P, P], F32, name="sums", tag="b_bank")
+                for i, term in enumerate(terms):
+                    nc.tensor.matmul(sums[:], lhsT=term, rhs=identity[:], is_transpose=True, start=i == 0, stop=i == 2)
+                block = work.tile([P, P], F32, name="turned", tag="turned")
+                nc.scalar.copy(out=block[:], in_=sums[:])
+                turned.append(block)
+        for t0, width in CHUNKS:
+            back = down_psum.tile([P, width], F32, name="back", tag="y_bank")
+            for c0 in range(0, width, P):
+                nc.tensor.transpose(back[:, c0 : c0 + P], turned[(t0 + c0) // P][:], identity[:])
+            total = work.tile([P, width], F32, name="total", tag="total", bufs=2)
+            nc.scalar.copy(out=total[:], in_=back[:])
+            nc.sync.dma_start(out=out[:, t0 : t0 + width], in_=total[:])
+
+        def add(in0, in1, tag):
+            total = work.tile([P, in1.shape[1]], F32, name=tag, tag=tag, bufs=2)
+            nc.vector.tensor_tensor(out=total[:], in0=in0, in1=in1, op=ADD)
             return total
 
-        first = fetch(0, pos1_sb, 0)
-        second = fetch(0, pos2_sb, 1)
-        for i in range(len(CHUNKS)):
-            more = i + 1 < len(CHUNKS)
-            if more:
-                next_first = fetch(i + 1, pos1_sb, 0)
-            both = add(banks[i], first, "both")
-            if more:
-                next_second = fetch(i + 1, pos2_sb, 1)
-            total = add(both, second, "total")
-            nc.sync.dma_start(out=out[:, starts[i] : starts[i] + CHUNKS[i]], in_=total[:])
-            if more:
-                first, second = next_first, next_second
+        waiting = None
+        for c0, width in CHUNKS:
+            t0 = TURNED + c0
+            first = fetch(t0, width, 0)
+            if waiting is not None:
+                nc.sync.dma_start(out=waiting[0], in_=add(waiting[1], waiting[2], "last_total")[:])
+            second = fetch(t0, width, 1)
+            waiting = (out[:, t0 : t0 + width], add(ys_banks[1][:, c0 : c0 + width], first, "both")[:], second)
+        nc.sync.dma_start(out=waiting[0], in_=add(waiting[1], waiting[2], "last_total")[:])

@@ -22,7 +22,7 @@ P = 128
 PACK = 4
 GATHER = 512
 STREAM_BUFS = 14
-EARLY = {3: (0, 4), 6: (4, 2)}
+EARLY = {4: (0, 2)}
 TURNED = 384
 CHUNKS = [(0, 256), (256, 128)]
 
@@ -48,6 +48,7 @@ def tile_moe_shr_glu_gelu_kernel(
         h_codes = keep.tile([P, S + T], U32, name="h_codes", align_bytes=64)
         h_scales = keep.tile([P, S + T], U8, name="h_scales", align_bytes=64)
         y_slots = keep.tile([P, S], F32, name="y_slots")
+        nc.gpsimd.memset(tok_scales[:].bitcast(I32), 0)
         identity = keep.tile([P, P], F32, name="identity")
         make_identity(nc, identity[:])
 
@@ -69,7 +70,7 @@ def tile_moe_shr_glu_gelu_kernel(
 
         def quantize(grouped, tag):
             width = grouped.shape[1] // PACK
-            bufs = 2 if width > N else 3
+            bufs = 2 if width == H else 4
             tag = tag + str(width)
             codes = work.tile([P, width], U32, name=tag + "_codes", tag=tag + "_codes", align_bytes=64, bufs=bufs)
             scales = work.tile([P, width], U8, name=tag + "_scales", tag=tag + "_scales", align_bytes=64, bufs=bufs)
@@ -88,7 +89,7 @@ def tile_moe_shr_glu_gelu_kernel(
             count = raw.shape[1]
             if grouped is None:
                 grouped = work.tile(
-                    [P, count * PACK * N], BF16, name="w2_bf", tag="w2_bf" + str(count), align_bytes=64, bufs=2 if count <= 2 else 1
+                    [P, count * PACK * N], BF16, name="w2_bf", tag="w2_bf" + str(count), align_bytes=64, bufs=2 * count
                 )
             cast(
                 engine,
@@ -158,12 +159,15 @@ def tile_moe_shr_glu_gelu_kernel(
                     in_=h_bf[:, c0 * PACK : (c0 + width) * PACK],
                 )
 
-        def slot_outputs(e0, w2q):
-            count = w2q[0].shape[1] // N
-            bank = down_psum.tile([P, count * C], F32, name="y_bank", tag="y_bank")
-            for i in range(count):
-                cols = slice((e0 + i) * C, (e0 + i + 1) * C)
-                product(bank[:, i * C : (i + 1) * C], w2q, slice(i * N, (i + 1) * N), h_codes[:, cols], h_scales[:, cols])
+        def slot_outputs(e0, groups, pool, tag):
+            count = sum(w2q[0].shape[1] // N for w2q in groups)
+            bank = pool.tile([P, count * C], F32, name=tag, tag=tag)
+            done = 0
+            for w2q in groups:
+                for i in range(w2q[0].shape[1] // N):
+                    cols = slice((e0 + done) * C, (e0 + done + 1) * C)
+                    product(bank[:, done * C : (done + 1) * C], w2q, slice(i * N, (i + 1) * N), h_codes[:, cols], h_scales[:, cols])
+                    done = done + 1
             nc.scalar.copy(out=y_slots[:, e0 * C : (e0 + count) * C], in_=bank[:])
 
         def gather_slots(s0):
@@ -180,29 +184,33 @@ def tile_moe_shr_glu_gelu_kernel(
         raw1[E] = load_up(w1[E])
         for q in range(4):
             nc.sync.dma_start(
-                out=tok_scales[32 * q : 32 * q + 32, :].bitcast(I32),
-                in_=x_scales[0, 4 * q : 4 * q + 4, :].bitcast(I32).partition_broadcast(8),
+                out=tok_scales[32 * q : 32 * q + 4, :].bitcast(I32),
+                in_=x_scales[0, 4 * q : 4 * q + 4, :].bitcast(I32),
             )
         raw3[E] = load_up(w3[E])
         for e in range(last - 1):
             raw1[e] = load_up(w1[e])
             raw3[e] = load_up(w3[e])
-            if e == 1:
-                nc.sync.dma_start(out=pos1_sb[:], in_=pos1)
-                nc.sync.dma_start(out=pos2_sb[:], in_=pos2)
             if e in EARLY:
                 raw2[EARLY[e][0]] = load_down(*EARLY[e])
         for e in (10, 11):
             raw1[e] = load_up(w1[e])
         for e in (10, 11):
             raw3[e] = load_up(w3[e])
-        raw2[10] = load_down(10, 2)
-        raw2[6] = load_down(6, 2)
+        for e in (2, 4, 6, 10):
+            raw2[e] = load_down(e, 2)
         raw2[8] = load_down(8, 1)
         raw2[9] = load_down(9, 1)
         raw2[E] = load_down(E, 1)
-        gates = stream.tile([P, 2, T], F32, name="raw", tag="raw", align_bytes=64)
-        nc.sync.dma_start(out=gates[:], in_=gate.rearrange("g p t -> p g t"))
+        nc.sync.dma_start(out=pos1_sb[:], in_=pos1)
+        head = TURNED
+        gates = []
+        for t0, width in ((0, head), (head, T - head)):
+            tile = stream.tile([P, 2, width], F32, name="raw", tag="raw", align_bytes=64)
+            nc.sync.dma_start(out=tile[:], in_=gate[:, :, t0 : t0 + width].rearrange("g p t -> p g t"))
+            gates.append(tile)
+            if t0 == 0:
+                nc.sync.dma_start(out=pos2_sb[:], in_=pos2)
 
         gather_slots(0)
         w1_bf = up_tile(1, "w1")
@@ -225,7 +233,7 @@ def tile_moe_shr_glu_gelu_kernel(
             w3q = quantize(w3_bf, "w3")
             quantize_hidden(before, h_bf)
             if e - 1 in EARLY:
-                slot_outputs(EARLY[e - 1][0], w2q)
+                slot_outputs(EARLY[e - 1][0], [w2q], down_psum, "y_bank")
             if e in EARLY:
                 w2q = quantize(round_down(raw2[EARLY[e][0]], "S"), "w2")
             before = [e]
@@ -266,19 +274,21 @@ def tile_moe_shr_glu_gelu_kernel(
             view = h_bf[:, i * PACK * C : (i + 1) * PACK * C].rearrange("p (n t) -> p n t", t=PACK)
             columns = column_groups([10 + i])[0]
             nc.vector.tensor_tensor(out=view, in0=up_product(w3q[i], *columns, "b_bank"), in1=acts[i], op=MULT)
-        w2q = quantize(round_down(raw2[10], "S"), "w2")
-        pair_bf = round_down(raw2[6], "S")
-        late_bf = [round_down(raw2[e], "S") for e in (8, 9)]
+        on_scalar = {e: round_down(raw2[e], "S") for e in (2, 4, 6, 8)}
+        w2q = {2: quantize(on_scalar[2], "w2")}
         quantize_hidden([10, 11], h_bf)
-        slot_outputs(10, w2q)
-        slot_outputs(6, quantize(pair_bf, "w2"))
-        bank = up_psum.tile([P, 2 * C], F32, name="y_bank", tag="a_bank")
-        for i in range(2):
-            weights = quantize(late_bf[i], "w2")
-            cols = slice((8 + i) * C, (9 + i) * C)
-            product(bank[:, i * C : (i + 1) * C], weights, slice(0, N), h_codes[:, cols], h_scales[:, cols])
-        shared_bf = round_down(raw2[E], "V", late_bf[1])
-        nc.vector.tensor_copy(out=y_slots[:, 8 * C : 10 * C], in_=bank[:])
+        w2q[4] = quantize(on_scalar[4], "w2")
+        w2_bf = round_down(raw2[10], "V")
+        w2q[6] = quantize(on_scalar[6], "w2")
+        w2q[10] = quantize(w2_bf, "w2")
+        w2_bf = round_down(raw2[9], "V")
+        w2q[8] = quantize(on_scalar[8], "w2")
+        w2q[9] = quantize(w2_bf, "w2")
+        shared_bf = round_down(raw2[E], "V", w2_bf)
+        slot_outputs(2, [w2q[2], w2q[4]], down_psum, "y_bank")
+        slot_outputs(6, [w2q[6]], down_psum, "y_bank")
+        slot_outputs(10, [w2q[10]], up_psum, "a_bank")
+        slot_outputs(8, [w2q[8], w2q[9]], up_psum, "a_bank")
 
         w2q = quantize(shared_bf, "w2")
         ys_banks = []
@@ -298,15 +308,15 @@ def tile_moe_shr_glu_gelu_kernel(
             nc.vector.tensor_tensor(
                 out=part,
                 in0=y_slots[:].indirect((pos1_sb, pos2_sb)[r][:, t0 // 16 : (t0 + width) // 16]),
-                in1=gates[:, r, t0 : t0 + width],
+                in1=gates[0][:, r, :] if t0 == 0 else gates[1][:, r, t0 - head : t0 - head + width],
                 op=MULT,
             )
             return part
 
         turned = []
+        fetch(0, TURNED, 0)
+        fetch(0, TURNED, 1)
         for t0, width in CHUNKS:
-            fetch(t0, width, 0)
-            fetch(t0, width, 1)
             for c0 in range(t0, t0 + width, P):
                 terms = (ys_sb[:, c0 : c0 + P], parts[:, 0, c0 : c0 + P], parts[:, 1, c0 : c0 + P])
                 sums = up_psum.tile([P, P], F32, name="sums", tag="b_bank")

@@ -22,7 +22,6 @@ P = 128
 PACK = 4
 GATHER = 512
 STREAM_BUFS = 14
-EARLY = {4: (0, 2)}
 TURNED = 384
 CHUNKS = [(0, 256), (256, 128)]
 
@@ -60,7 +59,7 @@ def tile_moe_shr_glu_gelu_kernel(
         def load_down(e0, count):
             raw = stream.tile([P, count, PACK, N], F32, name="raw", tag="raw", align_bytes=64)
             nc.sync.dma_start(out=raw[:], in_=w2[e0 : e0 + count].rearrange("e (p j) c -> p e j c", j=PACK))
-            return raw
+            return raw[:]
 
         def cast(engine, dst, src):
             if engine == "V":
@@ -70,7 +69,7 @@ def tile_moe_shr_glu_gelu_kernel(
 
         def quantize(grouped, tag):
             width = grouped.shape[1] // PACK
-            bufs = 2 if width == H else 4
+            bufs = 2 if width == H else 5
             tag = tag + str(width)
             codes = work.tile([P, width], U32, name=tag + "_codes", tag=tag + "_codes", align_bytes=64, bufs=bufs)
             scales = work.tile([P, width], U8, name=tag + "_scales", tag=tag + "_scales", align_bytes=64, bufs=bufs)
@@ -81,20 +80,27 @@ def tile_moe_shr_glu_gelu_kernel(
             return work.tile([P, count * PACK * H], BF16, name=tag + "_bf", tag=tag + "_bf", align_bytes=64, bufs=3)
 
         def round_up(grouped, slot, m0, raw, engine):
-            view = grouped[:, slot * PACK * H : (slot + 1) * PACK * H].rearrange("p (t m j) -> p m j t", t=PACK, j=PACK)
-            count = raw.shape[2] // PACK
-            cast(engine, view[:, m0 : m0 + count], raw[:].rearrange("p j (m t) -> p m j t", t=PACK))
+            if engine == "V":
+                nc.vector.tensor_copy(
+                    out=grouped[:].rearrange("p (u v m j) -> p u m j v", u=2, v=2, j=PACK),
+                    in_=raw[:].rearrange("p j (m u v) -> p u m j v", u=2, v=2),
+                )
+            else:
+                nc.scalar.copy(
+                    out=grouped[:].rearrange("p (t m j) -> p m j t", t=PACK, j=PACK),
+                    in_=raw[:].rearrange("p j (m t) -> p m j t", t=PACK),
+                )
 
         def round_down(raw, engine, grouped=None):
             count = raw.shape[1]
             if grouped is None:
                 grouped = work.tile(
-                    [P, count * PACK * N], BF16, name="w2_bf", tag="w2_bf" + str(count), align_bytes=64, bufs=2 * count
+                    [P, count * PACK * N], BF16, name="w2_bf", tag="w2_bf" + str(count), align_bytes=64, bufs=4
                 )
             cast(
                 engine,
                 grouped[:].rearrange("p (e c i j) -> p e c j i", e=count, i=4, j=PACK),
-                raw[:].rearrange("p e j (c i) -> p e c j i", i=4),
+                raw.rearrange("p e j (c i) -> p e c j i", i=4),
             )
             return grouped
 
@@ -191,13 +197,11 @@ def tile_moe_shr_glu_gelu_kernel(
         for e in range(last - 1):
             raw1[e] = load_up(w1[e])
             raw3[e] = load_up(w3[e])
-            if e in EARLY:
-                raw2[EARLY[e][0]] = load_down(*EARLY[e])
         for e in (10, 11):
             raw1[e] = load_up(w1[e])
         for e in (10, 11):
             raw3[e] = load_up(w3[e])
-        for e in (2, 4, 6, 10):
+        for e in (0, 2, 4, 6, 10):
             raw2[e] = load_down(e, 2)
         raw2[8] = load_down(8, 1)
         raw2[9] = load_down(9, 1)
@@ -228,14 +232,10 @@ def tile_moe_shr_glu_gelu_kernel(
             acts = activations(before, w1q, rooms_of(raw1[e]) + rooms_of(raw1[before[0]]))
             w1q = quantize(w1_bf, "w1")
             w3_bf = up_tile(1, "w3")
-            round_up(w3_bf, 0, 0, raw3[e], "V")
+            round_up(w3_bf, 0, 0, raw3[e], "S" if e in (2, 6) else "V")
             h_bf = hidden(before, w3q, acts)
             w3q = quantize(w3_bf, "w3")
             quantize_hidden(before, h_bf)
-            if e - 1 in EARLY:
-                slot_outputs(EARLY[e - 1][0], [w2q], down_psum, "y_bank")
-            if e in EARLY:
-                w2q = quantize(round_down(raw2[EARLY[e][0]], "S"), "w2")
             before = [e]
 
         def round_shared(raw):
@@ -274,10 +274,14 @@ def tile_moe_shr_glu_gelu_kernel(
             view = h_bf[:, i * PACK * C : (i + 1) * PACK * C].rearrange("p (n t) -> p n t", t=PACK)
             columns = column_groups([10 + i])[0]
             nc.vector.tensor_tensor(out=view, in0=up_product(w3q[i], *columns, "b_bank"), in1=acts[i], op=MULT)
-        on_scalar = {e: round_down(raw2[e], "S") for e in (2, 4, 6, 8)}
-        w2q = {2: quantize(on_scalar[2], "w2")}
+        raw2[6], raw2[7] = raw2[6][:, 0:1], raw2[6][:, 1:2]
+        on_scalar = {e: round_down(raw2[e], "S") for e in (0, 2, 4, 6, 8)}
+        w2q = {0: quantize(on_scalar[0], "w2")}
         quantize_hidden([10, 11], h_bf)
+        w2q[2] = quantize(on_scalar[2], "w2")
+        w2_bf = round_down(raw2[7], "V")
         w2q[4] = quantize(on_scalar[4], "w2")
+        w2q[7] = quantize(w2_bf, "w2")
         w2_bf = round_down(raw2[10], "V")
         w2q[6] = quantize(on_scalar[6], "w2")
         w2q[10] = quantize(w2_bf, "w2")
@@ -285,8 +289,8 @@ def tile_moe_shr_glu_gelu_kernel(
         w2q[8] = quantize(on_scalar[8], "w2")
         w2q[9] = quantize(w2_bf, "w2")
         shared_bf = round_down(raw2[E], "V", w2_bf)
-        slot_outputs(2, [w2q[2], w2q[4]], down_psum, "y_bank")
-        slot_outputs(6, [w2q[6]], down_psum, "y_bank")
+        slot_outputs(0, [w2q[0], w2q[2]], down_psum, "y_bank")
+        slot_outputs(4, [w2q[4], w2q[6], w2q[7]], down_psum, "y_bank")
         slot_outputs(10, [w2q[10]], up_psum, "a_bank")
         slot_outputs(8, [w2q[8], w2q[9]], up_psum, "a_bank")
 

@@ -4,8 +4,9 @@ import concourse.mybir as mybir
 from concourse.masks import make_identity
 
 K, T, E, C, H, N = 512, 768, 12, 128, 512, 128
-S = E * C
-FLOPS = 2 * (S + T) * (2 * K * H + H * N)
+SLOTS = E * C
+SHARED = E
+FLOPS = 2 * (SLOTS + T) * (2 * K * H + H * N)
 
 F32 = mybir.dt.float32
 BF16 = mybir.dt.bfloat16
@@ -20,8 +21,11 @@ ADD = mybir.AluOpType.add
 
 P = 128
 PACK = 4
+ALIGN = 64
+LIST = 16
 GATHER = 512
 STREAM_BUFS = 14
+W3_ON_SCALAR = range(1, E - 2, 3)
 TURNED = 384
 CHUNKS = [(0, 256), (256, 128)]
 
@@ -30,6 +34,7 @@ def tile_moe_shr_glu_gelu_kernel(
     tc, x_words, x_scales, w1, w3, w2, gate, offs, pos1, pos2, out
 ):
     nc = tc.nc
+    on_vector, on_scalar = nc.vector.tensor_copy, nc.scalar.copy
     with ExitStack() as ctx:
         keep = ctx.enter_context(tc.tile_pool(name="keep", bufs=1))
         stream = ctx.enter_context(tc.tile_pool(name="stream", bufs=STREAM_BUFS))
@@ -37,77 +42,89 @@ def tile_moe_shr_glu_gelu_kernel(
         up_psum = ctx.enter_context(tc.psum_pool(name="up_psum", bufs=3))
         down_psum = ctx.enter_context(tc.psum_pool(name="down_psum", bufs=2))
 
-        tok_words = keep.tile([P, T], I32, name="tok_words", align_bytes=64)
-        tok_scales = keep.tile([P, T], U8, name="tok_scales", align_bytes=64)
-        slot_words = keep.tile([P, S], U32, name="slot_words", align_bytes=64)
-        slot_scales = keep.tile([P, S], U8, name="slot_scales", align_bytes=64)
-        offs_sb = keep.tile([P, S // 16], U16, name="offs_sb")
-        pos1_sb = keep.tile([P, T // 16], U16, name="pos1_sb")
-        pos2_sb = keep.tile([P, T // 16], U16, name="pos2_sb")
-        h_codes = keep.tile([P, S + T], U32, name="h_codes", align_bytes=64)
-        h_scales = keep.tile([P, S + T], U8, name="h_scales", align_bytes=64)
-        y_slots = keep.tile([P, S], F32, name="y_slots")
+        tok_words = keep.tile([P, T], I32, name="tok_words", align_bytes=ALIGN)
+        tok_scales = keep.tile([P, T], U8, name="tok_scales", align_bytes=ALIGN)
+        slot_words = keep.tile([P, SLOTS], U32, name="slot_words", align_bytes=ALIGN)
+        slot_scales = keep.tile([P, SLOTS], U8, name="slot_scales", align_bytes=ALIGN)
+        offs_sb = keep.tile([P, SLOTS // LIST], U16, name="offs_sb")
+        pos1_sb = keep.tile([P, T // LIST], U16, name="pos1_sb")
+        pos2_sb = keep.tile([P, T // LIST], U16, name="pos2_sb")
+        h_codes = keep.tile([P, SLOTS + T], U32, name="h_codes", align_bytes=ALIGN)
+        h_scales = keep.tile([P, SLOTS + T], U8, name="h_scales", align_bytes=ALIGN)
+        y_slots = keep.tile([P, SLOTS], F32, name="y_slots")
         nc.gpsimd.memset(tok_scales[:].bitcast(I32), 0)
         identity = keep.tile([P, P], F32, name="identity")
         make_identity(nc, identity[:])
 
-        def load_up(rows):
-            raw = stream.tile([P, PACK, rows.shape[1]], F32, name="raw", tag="raw", align_bytes=64)
-            nc.sync.dma_start(out=raw[:], in_=rows.rearrange("(p j) c -> p j c", j=PACK))
+        def load_up(weight):
+            raw = stream.tile([P, PACK, H], F32, name="raw", tag="raw", align_bytes=ALIGN)
+            nc.sync.dma_start(out=raw[:], in_=weight.rearrange("(p j) c -> p j c", j=PACK))
             return raw
 
         def load_down(e0, count):
-            raw = stream.tile([P, count, PACK, N], F32, name="raw", tag="raw", align_bytes=64)
+            raw = stream.tile([P, count, PACK, N], F32, name="raw", tag="raw", align_bytes=ALIGN)
             nc.sync.dma_start(out=raw[:], in_=w2[e0 : e0 + count].rearrange("e (p j) c -> p e j c", j=PACK))
             return raw[:]
 
-        def cast(engine, dst, src):
-            if engine == "V":
-                nc.vector.tensor_copy(out=dst, in_=src)
-            else:
-                nc.scalar.copy(out=dst, in_=src)
-
-        def quantize(grouped, tag):
-            width = grouped.shape[1] // PACK
+        def code_tiles(width, tag):
             bufs = 2 if width == H else 5
             tag = tag + str(width)
-            codes = work.tile([P, width], U32, name=tag + "_codes", tag=tag + "_codes", align_bytes=64, bufs=bufs)
-            scales = work.tile([P, width], U8, name=tag + "_scales", tag=tag + "_scales", align_bytes=64, bufs=bufs)
-            nc.vector.quantize_mx(out=codes[:].bitcast(FP8X4), scales=scales[:], in_=grouped[:])
+            codes = work.tile([P, width], U32, name=tag + "_codes", tag=tag + "_codes", align_bytes=ALIGN, bufs=bufs)
+            scales = work.tile([P, width], U8, name=tag + "_scales", tag=tag + "_scales", align_bytes=ALIGN, bufs=bufs)
             return codes, scales
 
-        def up_tile(count, tag):
-            return work.tile([P, count * PACK * H], BF16, name=tag + "_bf", tag=tag + "_bf", align_bytes=64, bufs=3)
+        def quantize(rounded, tag):
+            codes, scales = code_tiles(rounded.shape[1] // PACK, tag)
+            nc.vector.quantize_mx(out=codes[:].bitcast(FP8X4), scales=scales[:], in_=rounded[:])
+            return codes, scales
 
-        def round_up(grouped, slot, m0, raw, engine):
-            if engine == "V":
-                nc.vector.tensor_copy(
-                    out=grouped[:].rearrange("p (u v m j) -> p u m j v", u=2, v=2, j=PACK),
-                    in_=raw[:].rearrange("p j (m u v) -> p u m j v", u=2, v=2),
-                )
-            else:
-                nc.scalar.copy(
-                    out=grouped[:].rearrange("p (t m j) -> p m j t", t=PACK, j=PACK),
+        def round_up(raw, by_scalar, tag):
+            rounded = work.tile([P, PACK * H], BF16, name=tag + "_bf", tag=tag + "_bf", align_bytes=ALIGN)
+            if by_scalar:
+                on_scalar(
+                    out=rounded[:].rearrange("p (t m j) -> p m j t", t=PACK, j=PACK),
                     in_=raw[:].rearrange("p j (m t) -> p m j t", t=PACK),
                 )
-
-        def round_down(raw, engine, grouped=None):
-            count = raw.shape[1]
-            if grouped is None:
-                grouped = work.tile(
-                    [P, count * PACK * N], BF16, name="w2_bf", tag="w2_bf" + str(count), align_bytes=64, bufs=4
+            else:
+                on_vector(
+                    out=rounded[:].rearrange("p (u v m j) -> p u m j v", u=2, v=2, j=PACK),
+                    in_=raw[:].rearrange("p j (m u v) -> p u m j v", u=2, v=2),
                 )
-            cast(
-                engine,
-                grouped[:].rearrange("p (e c i j) -> p e c j i", e=count, i=4, j=PACK),
-                raw.rearrange("p e j (c i) -> p e c j i", i=4),
-            )
-            return grouped
+            return rounded
 
-        def product(bank, weights, cols, words, scales):
+        def round_up_together(raw):
+            source = raw[:].rearrange("p j (m t) -> p m j t", t=PACK)
+            halves = []
+            for u, copy in enumerate((on_vector, on_scalar)):
+                rounded = work.tile([P, PACK * H // 2], BF16, name="part_bf", tag="part_bf", align_bytes=ALIGN, bufs=4)
+                view = rounded[:].rearrange("p (t m j) -> p m j t", t=2, j=PACK)
+                copy(out=view, in_=source[:, :, :, 2 * u : 2 * u + 2])
+                halves.append(rounded)
+            return halves
+
+        def quantize_halves(halves, tag):
+            codes, scales = code_tiles(H, tag)
+            for u, rounded in enumerate(halves):
+                cols = slice(u * H // 2, (u + 1) * H // 2)
+                nc.vector.quantize_mx(out=codes[:, cols].bitcast(FP8X4), scales=scales[:, cols], in_=rounded[:])
+            return codes, scales
+
+        def round_down(raw, copy, rounded=None):
+            count = raw.shape[1]
+            if rounded is None:
+                rounded = work.tile(
+                    [P, count * PACK * N], BF16, name="w2_bf", tag="w2_bf" + str(count), align_bytes=ALIGN, bufs=4
+                )
+            copy(
+                out=rounded[:].rearrange("p (e c i j) -> p e c j i", e=count, i=4, j=PACK),
+                in_=raw.rearrange("p e j (c i) -> p e c j i", i=4),
+            )
+            return rounded
+
+        def product(target, weights, cols, words, scales):
             codes, code_scales = weights
             nc.tensor.matmul_mx(
-                out=bank,
+                out=target,
                 lhsT=codes[:, cols].bitcast(FP8X4),
                 lhsT_scale=code_scales[:, cols],
                 rhs=words.bitcast(FP8X4),
@@ -116,49 +133,44 @@ def tile_moe_shr_glu_gelu_kernel(
                 stop=True,
             )
 
-        def up_product(weights, slot, words, scales, tag):
+        def up_product(weights, words, scales, tag):
             bank = up_psum.tile([P, PACK, C], F32, name=tag, tag=tag)
             for t in range(PACK):
-                c0 = slot * H + P * t
-                product(bank[:, t, :], weights, slice(c0, c0 + P), words, scales)
+                product(bank[:, t, :], weights, slice(P * t, P * (t + 1)), words, scales)
             return bank[:].rearrange("p t n -> p n t")
 
-        def column_groups(experts):
-            if experts == [E]:
-                return [(0, tok_words[:, t0 : t0 + C], tok_scales[:, t0 : t0 + C]) for t0 in range(0, T, C)]
-            return [
-                (slot, slot_words[:, e * C : (e + 1) * C], slot_scales[:, e * C : (e + 1) * C])
-                for slot, e in enumerate(experts)
-            ]
+        def column_groups(e):
+            if e == SHARED:
+                return [(tok_words[:, t0 : t0 + C], tok_scales[:, t0 : t0 + C]) for t0 in range(0, T, C)]
+            return [(slot_words[:, e * C : (e + 1) * C], slot_scales[:, e * C : (e + 1) * C])]
 
         def rooms_of(raw):
-            flat = raw[:].rearrange("p j c -> p (j c)")
-            return [
-                flat[:, c0 : c0 + PACK * C].rearrange("p (n t) -> p n t", t=PACK)
-                for c0 in range(0, flat.shape[1], PACK * C)
-            ]
+            return [raw[:, j, :].rearrange("p (n t) -> p n t", t=PACK) for j in range(PACK)]
 
-        def activations(experts, w1q, rooms):
-            groups = column_groups(experts)
+        def activations(e, w1q, rooms):
+            groups = column_groups(e)
             for columns, room in zip(groups, rooms):
                 nc.scalar.activation(out=room, in_=up_product(w1q, *columns, "a_bank"), func=GELU)
             return rooms[: len(groups)]
 
-        def hidden(experts, w3q, acts):
-            if experts == [E]:
-                h_bf = keep.tile([P, PACK * T], BF16, name="hs_bf", align_bytes=64)
+        def multiply(w3q, columns, act, h_bf, place):
+            view = h_bf[:, place * PACK * C : (place + 1) * PACK * C].rearrange("p (n t) -> p n t", t=PACK)
+            nc.vector.tensor_tensor(out=view, in0=up_product(w3q, *columns, "b_bank"), in1=act, op=MULT)
+
+        def hidden(e, w3q, acts):
+            if e == SHARED:
+                h_bf = keep.tile([P, PACK * T], BF16, name="hs_bf", align_bytes=ALIGN)
             else:
-                h_bf = work.tile([P, len(experts) * PACK * C], BF16, name="h_bf", tag="h_bf", align_bytes=64, bufs=2)
-            for i, columns in enumerate(column_groups(experts)):
-                view = h_bf[:, i * PACK * C : (i + 1) * PACK * C].rearrange("p (n t) -> p n t", t=PACK)
-                nc.vector.tensor_tensor(out=view, in0=up_product(w3q, *columns, "b_bank"), in1=acts[i], op=MULT)
+                h_bf = work.tile([P, PACK * C], BF16, name="h_bf", tag="h_bf", align_bytes=ALIGN, bufs=2)
+            for place, columns in enumerate(column_groups(e)):
+                multiply(w3q, columns, acts[place], h_bf, place)
             return h_bf
 
-        def quantize_hidden(experts, h_bf):
-            total = h_bf.shape[1] // PACK
-            width = min(total, 2 * C)
-            for c0 in range(0, total, width):
-                h0 = experts[0] * C + c0
+        def quantize_hidden(e, h_bf):
+            count = h_bf.shape[1] // PACK
+            width = min(count, 2 * C)
+            for c0 in range(0, count, width):
+                h0 = e * C + c0
                 nc.vector.quantize_mx(
                     out=h_codes[:, h0 : h0 + width].bitcast(FP8X4),
                     scales=h_scales[:, h0 : h0 + width],
@@ -166,188 +178,160 @@ def tile_moe_shr_glu_gelu_kernel(
                 )
 
         def slot_outputs(e0, groups, pool, tag):
-            count = sum(w2q[0].shape[1] // N for w2q in groups)
+            count = sum(codes.shape[1] // N for codes, scales in groups)
             bank = pool.tile([P, count * C], F32, name=tag, tag=tag)
-            done = 0
-            for w2q in groups:
-                for i in range(w2q[0].shape[1] // N):
-                    cols = slice((e0 + done) * C, (e0 + done + 1) * C)
-                    product(bank[:, done * C : (done + 1) * C], w2q, slice(i * N, (i + 1) * N), h_codes[:, cols], h_scales[:, cols])
-                    done = done + 1
-            nc.scalar.copy(out=y_slots[:, e0 * C : (e0 + count) * C], in_=bank[:])
+            place = 0
+            for weights in groups:
+                for n0 in range(0, weights[0].shape[1], N):
+                    cols = slice((e0 + place) * C, (e0 + place + 1) * C)
+                    target = bank[:, place * C : (place + 1) * C]
+                    product(target, weights, slice(n0, n0 + N), h_codes[:, cols], h_scales[:, cols])
+                    place = place + 1
+            on_scalar(out=y_slots[:, e0 * C : (e0 + count) * C], in_=bank[:])
 
         def gather_slots(s0):
-            offsets = offs_sb[:, s0 // 16 : (s0 + GATHER) // 16]
-            nc.vector.tensor_copy(out=slot_words[:, s0 : s0 + GATHER], in_=tok_words[:].bitcast(U32).indirect(offsets))
-            nc.vector.tensor_copy(out=slot_scales[:, s0 : s0 + GATHER], in_=tok_scales[:].indirect(offsets))
+            offsets = offs_sb[:, s0 // LIST : (s0 + GATHER) // LIST]
+            on_vector(out=slot_words[:, s0 : s0 + GATHER], in_=tok_words[:].bitcast(U32).indirect(offsets))
+            on_vector(out=slot_scales[:, s0 : s0 + GATHER], in_=tok_scales[:].indirect(offsets))
 
-        last = E - 1
-        half = H // 2
-
+        last_two = (E - 2, E - 1)
         nc.sync.dma_start(out=tok_words[:], in_=x_words[0].rearrange("p t r -> p (t r)").bitcast(I32))
         nc.sync.dma_start(out=offs_sb[:], in_=offs)
         raw1, raw3, raw2 = {}, {}, {}
-        raw1[E] = load_up(w1[E])
+        raw1[SHARED] = load_up(w1[SHARED])
         for q in range(4):
             nc.sync.dma_start(
                 out=tok_scales[32 * q : 32 * q + 4, :].bitcast(I32),
                 in_=x_scales[0, 4 * q : 4 * q + 4, :].bitcast(I32),
             )
-        raw3[E] = load_up(w3[E])
-        for e in range(last - 1):
+        raw3[SHARED] = load_up(w3[SHARED])
+        for e in range(E - 2):
             raw1[e] = load_up(w1[e])
             raw3[e] = load_up(w3[e])
-        for e in (10, 11):
+        for e in last_two:
             raw1[e] = load_up(w1[e])
-        for e in (10, 11):
+        for e in last_two:
             raw3[e] = load_up(w3[e])
         for e in (0, 2, 4, 6, 10):
             raw2[e] = load_down(e, 2)
-        raw2[8] = load_down(8, 1)
-        raw2[9] = load_down(9, 1)
-        raw2[E] = load_down(E, 1)
+        for e in (8, 9, SHARED):
+            raw2[e] = load_down(e, 1)
         nc.sync.dma_start(out=pos1_sb[:], in_=pos1)
-        head = TURNED
         gates = []
-        for t0, width in ((0, head), (head, T - head)):
-            tile = stream.tile([P, 2, width], F32, name="raw", tag="raw", align_bytes=64)
-            nc.sync.dma_start(out=tile[:], in_=gate[:, :, t0 : t0 + width].rearrange("g p t -> p g t"))
-            gates.append(tile)
+        for t0, width in ((0, TURNED), (TURNED, T - TURNED)):
+            gate_sb = stream.tile([P, 2, width], F32, name="raw", tag="raw", align_bytes=ALIGN)
+            nc.sync.dma_start(out=gate_sb[:], in_=gate[:, :, t0 : t0 + width].rearrange("g p t -> p g t"))
+            gates.append(gate_sb)
             if t0 == 0:
                 nc.sync.dma_start(out=pos2_sb[:], in_=pos2)
 
         gather_slots(0)
-        w1_bf = up_tile(1, "w1")
-        round_up(w1_bf, 0, 0, raw1[E], "S")
-        w1q = quantize(w1_bf, "w1")
-        w3_bf = up_tile(1, "w3")
-        round_up(w3_bf, 0, 0, raw3[E], "S")
-        w3q = quantize(w3_bf, "w3")
-        gather_slots(GATHER)
-        gather_slots(2 * GATHER)
-        before = [E]
-        for e in range(last - 1):
-            w1_bf = up_tile(1, "w1")
-            round_up(w1_bf, 0, 0, raw1[e], "S")
-            acts = activations(before, w1q, rooms_of(raw1[e]) + rooms_of(raw1[before[0]]))
+        w1q = quantize(round_up(raw1[SHARED], True, "w1"), "w1")
+        w3q = quantize(round_up(raw3[SHARED], True, "w3"), "w3")
+        for s0 in range(GATHER, SLOTS, GATHER):
+            gather_slots(s0)
+
+        before = SHARED
+        for e in range(E - 2):
+            w1_bf = round_up(raw1[e], True, "w1")
+            acts = activations(before, w1q, rooms_of(raw1[e]) + rooms_of(raw1[before]))
             w1q = quantize(w1_bf, "w1")
-            w3_bf = up_tile(1, "w3")
-            round_up(w3_bf, 0, 0, raw3[e], "S" if e in (2, 6) else "V")
+            w3_bf = round_up(raw3[e], e in W3_ON_SCALAR, "w3")
             h_bf = hidden(before, w3q, acts)
             w3q = quantize(w3_bf, "w3")
             quantize_hidden(before, h_bf)
-            before = [e]
+            before = e
 
-        def round_shared(raw):
-            source = raw[:].rearrange("p j (m t) -> p m j t", t=PACK)
-            parts = []
-            for u, engine in enumerate("VS"):
-                part = work.tile([P, PACK * half], BF16, name="part_bf", tag="part_bf", align_bytes=64, bufs=4)
-                view = part[:].rearrange("p (t m j) -> p m j t", t=2, j=PACK)
-                cast(engine, view, source[:, :, :, 2 * u : 2 * u + 2])
-                parts.append(part)
-            return parts
-
-        def quantize_parts(parts, tag):
-            codes = work.tile([P, H], U32, name="codes", tag=tag + "512_codes", align_bytes=64, bufs=2)
-            scales = work.tile([P, H], U8, name="scales", tag=tag + "512_scales", align_bytes=64, bufs=2)
-            for u in range(2):
-                cols = slice(u * half, (u + 1) * half)
-                nc.vector.quantize_mx(out=codes[:, cols].bitcast(FP8X4), scales=scales[:, cols], in_=parts[u][:])
-            return codes, scales
-
-        w1_bf = up_tile(1, "w1")
-        round_up(w1_bf, 0, 0, raw1[10], "S")
-        acts = activations(before, w1q, rooms_of(raw1[10]))
+        near, final = last_two
+        w1_bf = round_up(raw1[near], True, "w1")
+        acts = activations(before, w1q, rooms_of(raw1[near]))
         w1q = quantize(w1_bf, "w1")
-        parts = round_shared(raw1[11])
+        halves = round_up_together(raw1[final])
         h_bf = hidden(before, w3q, acts)
-        acts = activations([10], w1q, rooms_of(raw1[11]))
-        w1q = quantize_parts(parts, "w1")
+        acts = activations(near, w1q, rooms_of(raw1[final]))
+        w1q = quantize_halves(halves, "w1")
         quantize_hidden(before, h_bf)
-        parts = round_shared(raw3[10])
-        acts = acts + activations([11], w1q, rooms_of(raw3[10]))
-        w3q = [quantize_parts(parts, "w3")]
-        w3q.append(quantize_parts(round_shared(raw3[11]), "w3"))
-        h_bf = raw3[11][:, 0, :].bitcast(BF16)
-        for i in range(2):
-            view = h_bf[:, i * PACK * C : (i + 1) * PACK * C].rearrange("p (n t) -> p n t", t=PACK)
-            columns = column_groups([10 + i])[0]
-            nc.vector.tensor_tensor(out=view, in0=up_product(w3q[i], *columns, "b_bank"), in1=acts[i], op=MULT)
+        halves = round_up_together(raw3[near])
+        acts = acts + activations(final, w1q, rooms_of(raw3[near]))
+        last_w3q = [quantize_halves(halves, "w3"), quantize_halves(round_up_together(raw3[final]), "w3")]
+        h_bf = raw3[final][:, 0, :].bitcast(BF16)
+        for place, e in enumerate(last_two):
+            multiply(last_w3q[place], column_groups(e)[0], acts[place], h_bf, place)
+
         raw2[6], raw2[7] = raw2[6][:, 0:1], raw2[6][:, 1:2]
-        on_scalar = {e: round_down(raw2[e], "S") for e in (0, 2, 4, 6, 8)}
-        w2q = {0: quantize(on_scalar[0], "w2")}
-        quantize_hidden([10, 11], h_bf)
-        w2q[2] = quantize(on_scalar[2], "w2")
-        w2_bf = round_down(raw2[7], "V")
-        w2q[4] = quantize(on_scalar[4], "w2")
-        w2q[7] = quantize(w2_bf, "w2")
-        w2_bf = round_down(raw2[10], "V")
-        w2q[6] = quantize(on_scalar[6], "w2")
-        w2q[10] = quantize(w2_bf, "w2")
-        w2_bf = round_down(raw2[9], "V")
-        w2q[8] = quantize(on_scalar[8], "w2")
-        w2q[9] = quantize(w2_bf, "w2")
-        shared_bf = round_down(raw2[E], "V", w2_bf)
+        scalar_bf = {e: round_down(raw2[e], on_scalar) for e in (0, 2, 4, 6, 8)}
+        w2q = {0: quantize(scalar_bf[0], "w2")}
+        quantize_hidden(near, h_bf)
+        w2q[2] = quantize(scalar_bf[2], "w2")
+        for e_vector, e_scalar in ((7, 4), (10, 6), (9, 8)):
+            vector_bf = round_down(raw2[e_vector], on_vector)
+            w2q[e_scalar] = quantize(scalar_bf[e_scalar], "w2")
+            w2q[e_vector] = quantize(vector_bf, "w2")
+        shared_bf = round_down(raw2[SHARED], on_vector, vector_bf)
         slot_outputs(0, [w2q[0], w2q[2]], down_psum, "y_bank")
         slot_outputs(4, [w2q[4], w2q[6], w2q[7]], down_psum, "y_bank")
         slot_outputs(10, [w2q[10]], up_psum, "a_bank")
         slot_outputs(8, [w2q[8], w2q[9]], up_psum, "a_bank")
 
-        w2q = quantize(shared_bf, "w2")
+        w2q[SHARED] = quantize(shared_bf, "w2")
         ys_banks = []
-        for t0, width in ((0, TURNED), (TURNED, T - TURNED)):
-            bank = up_psum.tile([P, width], F32, name="ys_bank", tag="a_bank")
-            for c0, piece in CHUNKS:
-                cols = slice(S + t0 + c0, S + t0 + c0 + piece)
-                product(bank[:, c0 : c0 + piece], w2q, slice(0, N), h_codes[:, cols], h_scales[:, cols])
-            ys_banks.append(bank)
+        for t0 in (0, TURNED):
+            ys_bank = up_psum.tile([P, T // 2], F32, name="ys_bank", tag="a_bank")
+            for c0, width in CHUNKS:
+                cols = slice(SLOTS + t0 + c0, SLOTS + t0 + c0 + width)
+                product(ys_bank[:, c0 : c0 + width], w2q[SHARED], slice(0, N), h_codes[:, cols], h_scales[:, cols])
+            ys_banks.append(ys_bank)
         ys_sb = keep.tile([P, TURNED], F32, name="ys_sb")
-        nc.scalar.copy(out=ys_sb[:], in_=ys_banks[0][:])
+        on_scalar(out=ys_sb[:], in_=ys_banks[0][:])
 
-        parts = keep.tile([P, 2, T], F32, name="parts")
+        gated = keep.tile([P, 2, T], F32, name="parts")
 
         def fetch(t0, width, r):
-            part = parts[:, r, t0 : t0 + width]
+            term = gated[:, r, t0 : t0 + width]
+            g0 = t0 % TURNED
             nc.vector.tensor_tensor(
-                out=part,
-                in0=y_slots[:].indirect((pos1_sb, pos2_sb)[r][:, t0 // 16 : (t0 + width) // 16]),
-                in1=gates[0][:, r, :] if t0 == 0 else gates[1][:, r, t0 - head : t0 - head + width],
+                out=term,
+                in0=y_slots[:].indirect((pos1_sb, pos2_sb)[r][:, t0 // LIST : (t0 + width) // LIST]),
+                in1=gates[t0 // TURNED][:, r, g0 : g0 + width],
                 op=MULT,
             )
-            return part
+            return term
 
-        turned = []
         fetch(0, TURNED, 0)
         fetch(0, TURNED, 1)
-        for t0, width in CHUNKS:
-            for c0 in range(t0, t0 + width, P):
-                terms = (ys_sb[:, c0 : c0 + P], parts[:, 0, c0 : c0 + P], parts[:, 1, c0 : c0 + P])
-                sums = up_psum.tile([P, P], F32, name="sums", tag="b_bank")
-                for i, term in enumerate(terms):
-                    nc.tensor.matmul(sums[:], lhsT=term, rhs=identity[:], is_transpose=True, start=i == 0, stop=i == 2)
-                block = work.tile([P, P], F32, name="turned", tag="turned")
-                nc.scalar.copy(out=block[:], in_=sums[:])
-                turned.append(block)
+        turned = []
+        for c0 in range(0, TURNED, P):
+            terms = (ys_sb[:, c0 : c0 + P], gated[:, 0, c0 : c0 + P], gated[:, 1, c0 : c0 + P])
+            sums = up_psum.tile([P, P], F32, name="sums", tag="b_bank")
+            for i, term in enumerate(terms):
+                nc.tensor.matmul(
+                    sums[:], lhsT=term, rhs=identity[:], is_transpose=True, start=i == 0, stop=i == len(terms) - 1
+                )
+            block = work.tile([P, P], F32, name="turned", tag="turned")
+            on_scalar(out=block[:], in_=sums[:])
+            turned.append(block)
         for t0, width in CHUNKS:
             back = down_psum.tile([P, width], F32, name="back", tag="y_bank")
             for c0 in range(0, width, P):
                 nc.tensor.transpose(back[:, c0 : c0 + P], turned[(t0 + c0) // P][:], identity[:])
-            total = work.tile([P, width], F32, name="total", tag="total", bufs=2)
-            nc.scalar.copy(out=total[:], in_=back[:])
-            nc.sync.dma_start(out=out[:, t0 : t0 + width], in_=total[:])
+            result = work.tile([P, width], F32, name="total", tag="total", bufs=len(CHUNKS))
+            on_scalar(out=result[:], in_=back[:])
+            nc.sync.dma_start(out=out[:, t0 : t0 + width], in_=result[:])
 
         def add(in0, in1, tag):
-            total = work.tile([P, in1.shape[1]], F32, name=tag, tag=tag, bufs=2)
-            nc.vector.tensor_tensor(out=total[:], in0=in0, in1=in1, op=ADD)
-            return total
+            summed = work.tile([P, in1.shape[1]], F32, name=tag, tag=tag, bufs=len(CHUNKS))
+            nc.vector.tensor_tensor(out=summed[:], in0=in0, in1=in1, op=ADD)
+            return summed[:]
+
+        def finish(target, partial, second):
+            nc.sync.dma_start(out=target, in_=add(partial, second, "last_total"))
 
         waiting = None
         for c0, width in CHUNKS:
             t0 = TURNED + c0
             first = fetch(t0, width, 0)
             if waiting is not None:
-                nc.sync.dma_start(out=waiting[0], in_=add(waiting[1], waiting[2], "last_total")[:])
+                finish(*waiting)
             second = fetch(t0, width, 1)
-            waiting = (out[:, t0 : t0 + width], add(ys_banks[1][:, c0 : c0 + width], first, "both")[:], second)
-        nc.sync.dma_start(out=waiting[0], in_=add(waiting[1], waiting[2], "last_total")[:])
+            waiting = (out[:, t0 : t0 + width], add(ys_banks[1][:, c0 : c0 + width], first, "both"), second)
+        finish(*waiting)

@@ -22,6 +22,7 @@ ADD = mybir.AluOpType.add
 P = 128
 PACK = 4
 ALIGN = 64
+DMA_ALIGN = 256
 LIST = 16
 GATHER = 512
 STREAM_BUFS = 14
@@ -42,8 +43,8 @@ def tile_moe_shr_glu_gelu_kernel(
         up_psum = ctx.enter_context(tc.psum_pool(name="up_psum", bufs=3))
         down_psum = ctx.enter_context(tc.psum_pool(name="down_psum", bufs=2))
 
-        tok_words = keep.tile([P, T], I32, name="tok_words", align_bytes=ALIGN)
-        tok_scales = keep.tile([P, T], U8, name="tok_scales", align_bytes=ALIGN)
+        tok_words = keep.tile([P, T], I32, name="tok_words", align_bytes=DMA_ALIGN)
+        tok_scales = keep.tile([P, T], U8, name="tok_scales", align_bytes=DMA_ALIGN)
         slot_words = keep.tile([P, SLOTS], U32, name="slot_words", align_bytes=ALIGN)
         slot_scales = keep.tile([P, SLOTS], U8, name="slot_scales", align_bytes=ALIGN)
         offs_sb = keep.tile([P, SLOTS // LIST], U16, name="offs_sb")
@@ -57,12 +58,12 @@ def tile_moe_shr_glu_gelu_kernel(
         make_identity(nc, identity[:])
 
         def load_up(weight):
-            raw = stream.tile([P, PACK, H], F32, name="raw", tag="raw", align_bytes=ALIGN)
+            raw = stream.tile([P, PACK, H], F32, name="raw", tag="raw", align_bytes=DMA_ALIGN)
             nc.sync.dma_start(out=raw[:], in_=weight.rearrange("(p j) c -> p j c", j=PACK))
             return raw
 
         def load_down(e0, count):
-            raw = stream.tile([P, count, PACK, N], F32, name="raw", tag="raw", align_bytes=ALIGN)
+            raw = stream.tile([P, count, PACK, N], F32, name="raw", tag="raw", align_bytes=DMA_ALIGN)
             nc.sync.dma_start(out=raw[:], in_=w2[e0 : e0 + count].rearrange("e (p j) c -> p e j c", j=PACK))
             return raw[:]
 
@@ -219,7 +220,7 @@ def tile_moe_shr_glu_gelu_kernel(
         nc.sync.dma_start(out=pos1_sb[:], in_=pos1)
         gates = []
         for t0, width in ((0, TURNED), (TURNED, T - TURNED)):
-            gate_sb = stream.tile([P, 2, width], F32, name="raw", tag="raw", align_bytes=ALIGN)
+            gate_sb = stream.tile([P, 2, width], F32, name="raw", tag="raw", align_bytes=DMA_ALIGN)
             nc.sync.dma_start(out=gate_sb[:], in_=gate[:, :, t0 : t0 + width].rearrange("g p t -> p g t"))
             gates.append(gate_sb)
             if t0 == 0:
@@ -314,12 +315,12 @@ def tile_moe_shr_glu_gelu_kernel(
             back = down_psum.tile([P, width], F32, name="back", tag="y_bank")
             for c0 in range(0, width, P):
                 nc.tensor.transpose(back[:, c0 : c0 + P], turned[(t0 + c0) // P][:], identity[:])
-            result = work.tile([P, width], F32, name="total", tag="total", bufs=len(CHUNKS))
+            result = work.tile([P, width], F32, name="total", tag="total", bufs=len(CHUNKS), align_bytes=DMA_ALIGN)
             on_scalar(out=result[:], in_=back[:])
             nc.sync.dma_start(out=out[:, t0 : t0 + width], in_=result[:])
 
         def add(in0, in1, tag):
-            summed = work.tile([P, in1.shape[1]], F32, name=tag, tag=tag, bufs=len(CHUNKS))
+            summed = work.tile([P, in1.shape[1]], F32, name=tag, tag=tag, bufs=len(CHUNKS), align_bytes=DMA_ALIGN)
             nc.vector.tensor_tensor(out=summed[:], in0=in0, in1=in1, op=ADD)
             return summed[:]
 

@@ -16,6 +16,7 @@ U16 = mybir.dt.uint16
 U8 = mybir.dt.uint8
 FP8X4 = mybir.dt.float8_e4m3fn_x4
 GELU = mybir.ActivationFunctionType.Gelu_apprx_tanh
+COPY = mybir.ActivationFunctionType.Copy
 MULT = mybir.AluOpType.mult
 ADD = mybir.AluOpType.add
 
@@ -282,10 +283,7 @@ def tile_moe_shr_glu_gelu_kernel(
                 cols = slice(SLOTS + t0 + c0, SLOTS + t0 + c0 + width)
                 product(ys_bank[:, c0 : c0 + width], w2q[SHARED], slice(0, N), h_codes[:, cols], h_scales[:, cols])
             ys_banks.append(ys_bank)
-        ys_sb = keep.tile([P, TURNED], F32, name="ys_sb")
-        on_scalar(out=ys_sb[:], in_=ys_banks[0][:])
-
-        gated = keep.tile([P, 2, T], F32, name="parts")
+        gated = keep.tile([P, 2, TURNED], F32, name="parts")
 
         def fetch(t0, width, r):
             term = gated[:, r, t0 : t0 + width]
@@ -299,15 +297,28 @@ def tile_moe_shr_glu_gelu_kernel(
             return term
 
         fetch(0, TURNED, 0)
-        fetch(0, TURNED, 1)
-        turned = []
         for c0 in range(0, TURNED, P):
-            terms = (ys_sb[:, c0 : c0 + P], gated[:, 0, c0 : c0 + P], gated[:, 1, c0 : c0 + P])
-            sums = up_psum.tile([P, P], F32, name="sums", tag="b_bank")
-            for i, term in enumerate(terms):
-                nc.tensor.matmul(
-                    sums[:], lhsT=term, rhs=identity[:], is_transpose=True, start=i == 0, stop=i == len(terms) - 1
-                )
+            fetch(c0, P, 1)
+        ys_sb = keep.tile([P, TURNED], F32, name="ys_sb")
+        picked = []
+        for c0, width in CHUNKS:
+            pair = keep.tile([P, 2, width], F32, name="picked" + str(c0))
+            for r, pos_sb in enumerate((pos1_sb, pos2_sb)):
+                offsets = pos_sb[:, (TURNED + c0) // LIST : (TURNED + c0 + width) // LIST]
+                nc.scalar.activation(out=pair[:, r, :], in_=y_slots[:].indirect(offsets), func=COPY)
+                if c0 == 0 and r == 1:
+                    on_scalar(out=ys_sb[:], in_=ys_banks[0][:])
+            picked.append(pair)
+        def turn(bank, term, start, stop):
+            nc.tensor.matmul(bank[:], lhsT=term, rhs=identity[:], is_transpose=True, start=start, stop=stop)
+
+        banks = [up_psum.tile([P, P], F32, name="sums", tag="b_bank") for c0 in range(0, TURNED, P)]
+        for sums, c0 in zip(banks, range(0, TURNED, P)):
+            turn(sums, gated[:, 0, c0 : c0 + P], True, False)
+        turned = []
+        for sums, c0 in zip(banks, range(0, TURNED, P)):
+            turn(sums, ys_sb[:, c0 : c0 + P], False, False)
+            turn(sums, gated[:, 1, c0 : c0 + P], False, True)
             block = work.tile([P, P], F32, name="turned", tag="turned")
             on_scalar(out=block[:], in_=sums[:])
             turned.append(block)
@@ -319,20 +330,19 @@ def tile_moe_shr_glu_gelu_kernel(
             on_scalar(out=result[:], in_=back[:])
             nc.sync.dma_start(out=out[:, t0 : t0 + width], in_=result[:])
 
-        def add(in0, in1, tag):
-            summed = work.tile([P, in1.shape[1]], F32, name=tag, tag=tag, bufs=len(CHUNKS), align_bytes=DMA_ALIGN)
-            nc.vector.tensor_tensor(out=summed[:], in0=in0, in1=in1, op=ADD)
-            return summed[:]
+        def combine(in0, in1, op, tag, result=None):
+            if result is None:
+                result = work.tile(
+                    [P] + list(in1.shape[1:]), F32, name=tag, tag=tag, bufs=len(CHUNKS), align_bytes=DMA_ALIGN
+                )[:]
+            nc.vector.tensor_tensor(out=result, in0=in0, in1=in1, op=op)
+            return result
 
-        def finish(target, partial, second):
-            nc.sync.dma_start(out=target, in_=add(partial, second, "last_total"))
-
-        waiting = None
-        for c0, width in CHUNKS:
-            t0 = TURNED + c0
-            first = fetch(t0, width, 0)
-            if waiting is not None:
-                finish(*waiting)
-            second = fetch(t0, width, 1)
-            waiting = (out[:, t0 : t0 + width], add(ys_banks[1][:, c0 : c0 + width], first, "both"), second)
-        finish(*waiting)
+        terms = [combine(pair[:], gates[1][:, :, c0 : c0 + width], MULT, "terms") for pair, (c0, width) in zip(picked, CHUNKS)]
+        partial = [
+            combine(ys_banks[1][:, c0 : c0 + width], term[:, 0, :], ADD, "both")
+            for term, (c0, width) in zip(terms, CHUNKS)
+        ]
+        for term, both, (c0, width) in zip(terms, partial, CHUNKS):
+            total = combine(both, term[:, 1, :], ADD, "last_total")
+            nc.sync.dma_start(out=out[:, TURNED + c0 : TURNED + c0 + width], in_=total)

@@ -26,8 +26,10 @@ ALIGN = 64
 DMA_ALIGN = 256
 LIST = 16
 GATHER = 512
-STREAM_BUFS = 14
-W3_ON_SCALAR = range(1, E - 2, 3)
+NARROW_BUFS, WIDE_BUFS = 6, 4
+PAIRS = 6
+W3_ON_SCALAR = ()
+BOTH_ON_SCALAR = 2
 TURNED = 384
 CHUNKS = [(0, 256), (256, 128)]
 
@@ -39,14 +41,15 @@ def tile_moe_shr_glu_gelu_kernel(
     on_vector, on_scalar = nc.vector.tensor_copy, nc.scalar.copy
     with ExitStack() as ctx:
         keep = ctx.enter_context(tc.tile_pool(name="keep", bufs=1))
-        stream = ctx.enter_context(tc.tile_pool(name="stream", bufs=STREAM_BUFS))
+        narrow = ctx.enter_context(tc.tile_pool(name="narrow", bufs=NARROW_BUFS))
+        wide = ctx.enter_context(tc.tile_pool(name="wide", bufs=WIDE_BUFS))
         work = ctx.enter_context(tc.tile_pool(name="work", bufs=3))
         up_psum = ctx.enter_context(tc.psum_pool(name="up_psum", bufs=3))
         down_psum = ctx.enter_context(tc.psum_pool(name="down_psum", bufs=2))
 
         tok_words = keep.tile([P, T], I32, name="tok_words", align_bytes=DMA_ALIGN)
         tok_scales = keep.tile([P, T], U8, name="tok_scales", align_bytes=DMA_ALIGN)
-        slot_words = keep.tile([P, SLOTS], U32, name="slot_words", align_bytes=ALIGN)
+        slot_words = {}
         slot_scales = keep.tile([P, SLOTS], U8, name="slot_scales", align_bytes=ALIGN)
         offs_sb = keep.tile([P, SLOTS // LIST], U16, name="offs_sb")
         pos1_sb = keep.tile([P, T // LIST], U16, name="pos1_sb")
@@ -54,22 +57,37 @@ def tile_moe_shr_glu_gelu_kernel(
         h_codes = keep.tile([P, SLOTS + T], U32, name="h_codes", align_bytes=ALIGN)
         h_scales = keep.tile([P, SLOTS + T], U8, name="h_scales", align_bytes=ALIGN)
         y_slots = keep.tile([P, SLOTS], F32, name="y_slots")
-        nc.gpsimd.memset(tok_scales[:].bitcast(I32), 0)
+        nc.vector.memset(tok_scales[:].bitcast(I32), 0)
         identity = keep.tile([P, P], F32, name="identity")
         make_identity(nc, identity[:])
 
-        def load_up(weight):
-            raw = stream.tile([P, PACK, H], F32, name="raw", tag="raw", align_bytes=DMA_ALIGN)
+        late = []
+
+        def late_buffer(shape):
+            pool = narrow if len(late) % (NARROW_BUFS + WIDE_BUFS) < NARROW_BUFS else wide
+            late.append(pool)
+            return pool.tile(shape, F32, name="raw", tag="raw", align_bytes=DMA_ALIGN)
+
+        def load_pair(weights, e):
+            raw = wide.tile([P, 2, PACK, H], F32, name="raw", tag="raw", align_bytes=DMA_ALIGN)
+            nc.sync.dma_start(out=raw[:], in_=weights[e : e + 2].rearrange("e (p j) c -> p e j c", j=PACK))
+            return raw[:, 0], raw[:, 1]
+
+        def load_up(weight, early=False):
+            if early:
+                raw = narrow.tile([P, PACK, H], F32, name="raw", tag="raw", align_bytes=DMA_ALIGN)
+            else:
+                raw = late_buffer([P, PACK, H])
             nc.sync.dma_start(out=raw[:], in_=weight.rearrange("(p j) c -> p j c", j=PACK))
             return raw
 
         def load_down(e0, count):
-            raw = stream.tile([P, count, PACK, N], F32, name="raw", tag="raw", align_bytes=DMA_ALIGN)
+            raw = late_buffer([P, count, PACK, N])
             nc.sync.dma_start(out=raw[:], in_=w2[e0 : e0 + count].rearrange("e (p j) c -> p e j c", j=PACK))
             return raw[:]
 
         def code_tiles(width, tag):
-            bufs = 2 if width == H else 5
+            bufs = 3 if width == H else 5
             tag = tag + str(width)
             codes = work.tile([P, width], U32, name=tag + "_codes", tag=tag + "_codes", align_bytes=ALIGN, bufs=bufs)
             scales = work.tile([P, width], U8, name=tag + "_scales", tag=tag + "_scales", align_bytes=ALIGN, bufs=bufs)
@@ -80,8 +98,9 @@ def tile_moe_shr_glu_gelu_kernel(
             nc.vector.quantize_mx(out=codes[:].bitcast(FP8X4), scales=scales[:], in_=rounded[:])
             return codes, scales
 
-        def round_up(raw, by_scalar, tag):
-            rounded = work.tile([P, PACK * H], BF16, name=tag + "_bf", tag=tag + "_bf", align_bytes=ALIGN)
+        def round_up(raw, by_scalar, tag, rounded=None):
+            if rounded is None:
+                rounded = work.tile([P, PACK * H], BF16, name="up_bf", tag="up_bf", align_bytes=ALIGN, bufs=4)
             if by_scalar:
                 on_scalar(
                     out=rounded[:].rearrange("p (t m j) -> p m j t", t=PACK, j=PACK),
@@ -144,7 +163,8 @@ def tile_moe_shr_glu_gelu_kernel(
         def column_groups(e):
             if e == SHARED:
                 return [(tok_words[:, t0 : t0 + C], tok_scales[:, t0 : t0 + C]) for t0 in range(0, T, C)]
-            return [(slot_words[:, e * C : (e + 1) * C], slot_scales[:, e * C : (e + 1) * C])]
+            s0, c0 = e * C // GATHER * GATHER, e * C % GATHER
+            return [(slot_words[s0][:, c0 : c0 + C], slot_scales[:, e * C : (e + 1) * C])]
 
         def rooms_of(raw):
             return [raw[:, j, :].rearrange("p (n t) -> p n t", t=PACK) for j in range(PACK)]
@@ -193,21 +213,28 @@ def tile_moe_shr_glu_gelu_kernel(
 
         def gather_slots(s0):
             offsets = offs_sb[:, s0 // LIST : (s0 + GATHER) // LIST]
-            on_vector(out=slot_words[:, s0 : s0 + GATHER], in_=tok_words[:].bitcast(U32).indirect(offsets))
+            tag = "words" + str(s0)
+            slot_words[s0] = keep.tile([P, GATHER], U32, name=tag, tag=tag, align_bytes=ALIGN)
+            on_vector(out=slot_words[s0][:], in_=tok_words[:].bitcast(U32).indirect(offsets))
             on_vector(out=slot_scales[:, s0 : s0 + GATHER], in_=tok_scales[:].indirect(offsets))
 
         last_two = (E - 2, E - 1)
         nc.sync.dma_start(out=tok_words[:], in_=x_words[0].rearrange("p t r -> p (t r)").bitcast(I32))
         nc.sync.dma_start(out=offs_sb[:], in_=offs)
         raw1, raw3, raw2 = {}, {}, {}
-        raw1[SHARED] = load_up(w1[SHARED])
+        raw1[SHARED] = load_up(w1[SHARED], True)
         for q in range(4):
             nc.sync.dma_start(
                 out=tok_scales[32 * q : 32 * q + 4, :].bitcast(I32),
                 in_=x_scales[0, 4 * q : 4 * q + 4, :].bitcast(I32),
             )
-        raw3[SHARED] = load_up(w3[SHARED])
-        for e in range(E - 2):
+        raw3[SHARED] = load_up(w3[SHARED], True)
+        raw1[0] = load_up(w1[0], True)
+        for e in range(PAIRS):
+            weights, raws = ((w3, raw3), (w1, raw1))[e % 2]
+            raws[e], raws[e + 1] = load_pair(weights, e)
+        raw3[PAIRS] = load_up(w3[PAIRS])
+        for e in range(PAIRS + 1, E - 2):
             raw1[e] = load_up(w1[e])
             raw3[e] = load_up(w3[e])
         for e in last_two:
@@ -221,22 +248,49 @@ def tile_moe_shr_glu_gelu_kernel(
         nc.sync.dma_start(out=pos1_sb[:], in_=pos1)
         gates = []
         for t0, width in ((0, TURNED), (TURNED, T - TURNED)):
-            gate_sb = stream.tile([P, 2, width], F32, name="raw", tag="raw", align_bytes=DMA_ALIGN)
+            gate_sb = late_buffer([P, 2, width])
             nc.sync.dma_start(out=gate_sb[:], in_=gate[:, :, t0 : t0 + width].rearrange("g p t -> p g t"))
             gates.append(gate_sb)
             if t0 == 0:
                 nc.sync.dma_start(out=pos2_sb[:], in_=pos2)
 
         gather_slots(0)
-        w1q = quantize(round_up(raw1[SHARED], True, "w1"), "w1")
-        w3q = quantize(round_up(raw3[SHARED], True, "w3"), "w3")
+        shared_bf = [
+            keep.tile([P, PACK * H], BF16, name="shared_bf", tag="words" + str(s0), align_bytes=ALIGN)
+            for s0 in range(GATHER, SLOTS, GATHER)
+        ]
+        w1q = quantize(round_up(raw1[SHARED], True, "w1", shared_bf[0]), "w1")
+        w3q = quantize(round_up(raw3[SHARED], True, "w3", shared_bf[1]), "w3")
         for s0 in range(GATHER, SLOTS, GATHER):
             gather_slots(s0)
 
-        before = SHARED
-        for e in range(E - 2):
+        acts = activations(SHARED, w1q, rooms_of(raw3[SHARED]) + rooms_of(raw1[SHARED]))
+        w1_bf = round_up(raw1[0], True, "w1")
+        h_bf = hidden(SHARED, w3q, acts)
+        codes = {("w1", 0): quantize(w1_bf, "w1")}
+        quantize_hidden(SHARED, h_bf)
+        for e in range(PAIRS):
+            tag, raws = (("w3", raw3), ("w1", raw1))[e % 2]
+            first_bf = round_up(raws[e], e == BOTH_ON_SCALAR, tag)
+            if e == BOTH_ON_SCALAR:
+                acts = activations(e - 1, codes["w1", e - 1], rooms_of(raws[e]))
+            second_bf = round_up(raws[e + 1], True, tag)
+            if e > 0 and e != BOTH_ON_SCALAR:
+                acts = activations(e - 1, codes["w1", e - 1], rooms_of(raws[e + 1]))
+            codes[tag, e] = quantize(first_bf, tag)
+            codes[tag, e + 1] = quantize(second_bf, tag)
+            if e > 0:
+                quantize_hidden(e - 1, hidden(e - 1, codes["w3", e - 1], acts))
+        w3_bf = round_up(raw3[PAIRS], True, "w3")
+        acts = activations(PAIRS - 1, codes["w1", PAIRS - 1], rooms_of(raw3[PAIRS]))
+        h_bf = hidden(PAIRS - 1, codes["w3", PAIRS - 1], acts)
+        w1q, w3q = codes["w1", PAIRS], quantize(w3_bf, "w3")
+        quantize_hidden(PAIRS - 1, h_bf)
+
+        before = PAIRS
+        for e in range(PAIRS + 1, E - 2):
             w1_bf = round_up(raw1[e], True, "w1")
-            acts = activations(before, w1q, rooms_of(raw1[e]) + rooms_of(raw1[before]))
+            acts = activations(before, w1q, rooms_of(raw1[e]))
             w1q = quantize(w1_bf, "w1")
             w3_bf = round_up(raw3[e], e in W3_ON_SCALAR, "w3")
             h_bf = hidden(before, w3q, acts)

@@ -27,7 +27,7 @@ DMA_ALIGN = 256
 LIST = 16
 GATHER = 512
 NARROW_BUFS, WIDE_BUFS = 6, 4
-PAIRS = 6
+PAIRS = 8
 W3_ON_SCALAR = ()
 BOTH_ON_SCALAR = 2
 TURNED = 384
@@ -281,8 +281,8 @@ def tile_moe_shr_glu_gelu_kernel(
             codes[tag, e + 1] = quantize(second_bf, tag)
             if e > 0:
                 quantize_hidden(e - 1, hidden(e - 1, codes["w3", e - 1], acts))
-        w3_bf = round_up(raw3[PAIRS], True, "w3")
-        acts = activations(PAIRS - 1, codes["w1", PAIRS - 1], rooms_of(raw3[PAIRS]))
+        acts = activations(PAIRS - 1, codes["w1", PAIRS - 1], rooms_of(raw1[PAIRS])[1:])
+        w3_bf = round_up(raw3[PAIRS], False, "w3")
         h_bf = hidden(PAIRS - 1, codes["w3", PAIRS - 1], acts)
         w1q, w3q = codes["w1", PAIRS], quantize(w3_bf, "w3")
         quantize_hidden(PAIRS - 1, h_bf)

@@ -327,17 +327,18 @@ def tile_moe_shr_glu_gelu_kernel(
         slot_outputs(0, [w2q[0], w2q[2]], down_psum, "y_bank")
         slot_outputs(4, [w2q[4], w2q[6], w2q[7]], down_psum, "y_bank")
         slot_outputs(10, [w2q[10]], up_psum, "a_bank")
-        slot_outputs(8, [w2q[8], w2q[9]], up_psum, "a_bank")
+        slot_outputs(8, [w2q[8]], up_psum, "a_bank")
+        slot_outputs(9, [w2q[9]], up_psum, "b_bank")
 
         w2q[SHARED] = quantize(shared_bf, "w2")
-        ys_banks = []
-        for t0 in (0, TURNED):
-            ys_bank = up_psum.tile([P, T // 2], F32, name="ys_bank", tag="a_bank")
-            for c0, width in CHUNKS:
-                cols = slice(SLOTS + t0 + c0, SLOTS + t0 + c0 + width)
-                product(ys_bank[:, c0 : c0 + width], w2q[SHARED], slice(0, N), h_codes[:, cols], h_scales[:, cols])
-            ys_banks.append(ys_bank)
-        gated = keep.tile([P, 2, TURNED], F32, name="parts")
+        ys_banks = [up_psum.tile([P, T // 2], F32, name="ys_bank", tag="a_bank") for t0 in (0, TURNED)]
+        for c0 in range(0, TURNED, P):
+            cols = slice(SLOTS + c0, SLOTS + c0 + P)
+            product(ys_banks[0][:, c0 : c0 + P], (h_codes, h_scales), cols, w2q[SHARED][0][:], w2q[SHARED][1][:])
+        for c0, width in CHUNKS:
+            cols = slice(SLOTS + TURNED + c0, SLOTS + TURNED + c0 + width)
+            product(ys_banks[1][:, c0 : c0 + width], w2q[SHARED], slice(0, N), h_codes[:, cols], h_scales[:, cols])
+        gated = keep.tile([P, 2, T], F32, name="parts")
 
         def fetch(t0, width, r):
             term = gated[:, r, t0 : t0 + width]
@@ -354,35 +355,33 @@ def tile_moe_shr_glu_gelu_kernel(
         for c0 in range(0, TURNED, P):
             fetch(c0, P, 1)
         ys_sb = keep.tile([P, TURNED], F32, name="ys_sb")
-        picked = []
-        for c0, width in CHUNKS:
-            pair = keep.tile([P, 2, width], F32, name="picked" + str(c0))
-            for r, pos_sb in enumerate((pos1_sb, pos2_sb)):
-                offsets = pos_sb[:, (TURNED + c0) // LIST : (TURNED + c0 + width) // LIST]
-                nc.scalar.activation(out=pair[:, r, :], in_=y_slots[:].indirect(offsets), func=COPY)
-                if c0 == 0 and r == 1:
-                    on_scalar(out=ys_sb[:], in_=ys_banks[0][:])
-            picked.append(pair)
+        (wide0, wide_width), (last0, last_width) = CHUNKS
+        picked = keep.tile([P, 2, wide_width], F32, name="picked")
+        for r, pos_sb in enumerate((pos1_sb, pos2_sb)):
+            offsets = pos_sb[:, TURNED // LIST : (TURNED + wide_width) // LIST]
+            nc.scalar.activation(out=picked[:, r, :], in_=y_slots[:].indirect(offsets), func=COPY)
+        on_scalar(out=ys_sb[:], in_=ys_banks[0][:])
+
         def turn(bank, term, start, stop):
-            nc.tensor.matmul(bank[:], lhsT=term, rhs=identity[:], is_transpose=True, start=start, stop=stop)
+            nc.tensor.matmul(bank, lhsT=term, rhs=identity[:], is_transpose=True, start=start, stop=stop)
 
         banks = [up_psum.tile([P, P], F32, name="sums", tag="b_bank") for c0 in range(0, TURNED, P)]
         for sums, c0 in zip(banks, range(0, TURNED, P)):
-            turn(sums, gated[:, 0, c0 : c0 + P], True, False)
+            turn(sums[:], gated[:, 0, c0 : c0 + P], True, False)
         turned = []
         for sums, c0 in zip(banks, range(0, TURNED, P)):
-            turn(sums, ys_sb[:, c0 : c0 + P], False, False)
-            turn(sums, gated[:, 1, c0 : c0 + P], False, True)
+            turn(sums[:], gated[:, 1, c0 : c0 + P], False, True)
             block = work.tile([P, P], F32, name="turned", tag="turned")
             on_scalar(out=block[:], in_=sums[:])
             turned.append(block)
         for t0, width in CHUNKS:
             back = down_psum.tile([P, width], F32, name="back", tag="y_bank")
             for c0 in range(0, width, P):
-                nc.tensor.transpose(back[:, c0 : c0 + P], turned[(t0 + c0) // P][:], identity[:])
+                turn(back[:, c0 : c0 + P], ys_sb[:, t0 + c0 : t0 + c0 + P], True, False)
+                turn(back[:, c0 : c0 + P], turned[(t0 + c0) // P][:], False, True)
             result = work.tile([P, width], F32, name="total", tag="total", bufs=len(CHUNKS), align_bytes=DMA_ALIGN)
             on_scalar(out=result[:], in_=back[:])
-            nc.sync.dma_start(out=out[:, t0 : t0 + width], in_=result[:])
+            nc.scalar.dma_start(out=out[:, t0 : t0 + width], in_=result[:])
 
         def combine(in0, in1, op, tag, result=None):
             if result is None:
@@ -392,11 +391,12 @@ def tile_moe_shr_glu_gelu_kernel(
             nc.vector.tensor_tensor(out=result, in0=in0, in1=in1, op=op)
             return result
 
-        terms = [combine(pair[:], gates[1][:, :, c0 : c0 + width], MULT, "terms") for pair, (c0, width) in zip(picked, CHUNKS)]
-        partial = [
-            combine(ys_banks[1][:, c0 : c0 + width], term[:, 0, :], ADD, "both")
-            for term, (c0, width) in zip(terms, CHUNKS)
-        ]
-        for term, both, (c0, width) in zip(terms, partial, CHUNKS):
-            total = combine(both, term[:, 1, :], ADD, "last_total")
-            nc.sync.dma_start(out=out[:, TURNED + c0 : TURNED + c0 + width], in_=total)
+        terms = combine(picked[:], gates[1][:, :, 0:wide_width], MULT, "terms")
+        last_first = fetch(TURNED + last0, last_width, 0)
+        partial = combine(ys_banks[1][:, 0:wide_width], terms[:, 0, :], ADD, "both")
+        last_second = fetch(TURNED + last0, last_width, 1)
+        last_partial = combine(ys_banks[1][:, last0 : last0 + last_width], last_first, ADD, "both")
+        total = combine(partial, terms[:, 1, :], ADD, "last_total")
+        nc.sync.dma_start(out=out[:, TURNED : TURNED + wide_width], in_=total)
+        total = combine(last_partial, last_second, ADD, "last_total")
+        nc.sync.dma_start(out=out[:, TURNED + last0 : T], in_=total)

@@ -26,10 +26,8 @@ ALIGN = 64
 DMA_ALIGN = 256
 LIST = 16
 GATHER = 512
-NARROW_BUFS, WIDE_BUFS = 6, 4
-PAIRS = 8
-W3_ON_SCALAR = ()
-BOTH_ON_SCALAR = 2
+STREAM_BUFS = 14
+W3_ON_SCALAR = range(1, E - 2, 3)
 TURNED = 384
 CHUNKS = [(0, 256), (256, 128)]
 
@@ -41,15 +39,14 @@ def tile_moe_shr_glu_gelu_kernel(
     on_vector, on_scalar = nc.vector.tensor_copy, nc.scalar.copy
     with ExitStack() as ctx:
         keep = ctx.enter_context(tc.tile_pool(name="keep", bufs=1))
-        narrow = ctx.enter_context(tc.tile_pool(name="narrow", bufs=NARROW_BUFS))
-        wide = ctx.enter_context(tc.tile_pool(name="wide", bufs=WIDE_BUFS))
+        stream = ctx.enter_context(tc.tile_pool(name="stream", bufs=STREAM_BUFS))
         work = ctx.enter_context(tc.tile_pool(name="work", bufs=3))
         up_psum = ctx.enter_context(tc.psum_pool(name="up_psum", bufs=3))
         down_psum = ctx.enter_context(tc.psum_pool(name="down_psum", bufs=2))
 
         tok_words = keep.tile([P, T], I32, name="tok_words", align_bytes=DMA_ALIGN)
         tok_scales = keep.tile([P, T], U8, name="tok_scales", align_bytes=DMA_ALIGN)
-        slot_words = {}
+        slot_words = keep.tile([P, SLOTS], U32, name="slot_words", align_bytes=ALIGN)
         slot_scales = keep.tile([P, SLOTS], U8, name="slot_scales", align_bytes=ALIGN)
         offs_sb = keep.tile([P, SLOTS // LIST], U16, name="offs_sb")
         pos1_sb = keep.tile([P, T // LIST], U16, name="pos1_sb")
@@ -57,37 +54,22 @@ def tile_moe_shr_glu_gelu_kernel(
         h_codes = keep.tile([P, SLOTS + T], U32, name="h_codes", align_bytes=ALIGN)
         h_scales = keep.tile([P, SLOTS + T], U8, name="h_scales", align_bytes=ALIGN)
         y_slots = keep.tile([P, SLOTS], F32, name="y_slots")
-        nc.vector.memset(tok_scales[:].bitcast(I32), 0)
+        nc.gpsimd.memset(tok_scales[:].bitcast(I32), 0)
         identity = keep.tile([P, P], F32, name="identity")
         make_identity(nc, identity[:])
 
-        late = []
-
-        def late_buffer(shape):
-            pool = narrow if len(late) % (NARROW_BUFS + WIDE_BUFS) < NARROW_BUFS else wide
-            late.append(pool)
-            return pool.tile(shape, F32, name="raw", tag="raw", align_bytes=DMA_ALIGN)
-
-        def load_pair(weights, e):
-            raw = wide.tile([P, 2, PACK, H], F32, name="raw", tag="raw", align_bytes=DMA_ALIGN)
-            nc.sync.dma_start(out=raw[:], in_=weights[e : e + 2].rearrange("e (p j) c -> p e j c", j=PACK))
-            return raw[:, 0], raw[:, 1]
-
-        def load_up(weight, early=False):
-            if early:
-                raw = narrow.tile([P, PACK, H], F32, name="raw", tag="raw", align_bytes=DMA_ALIGN)
-            else:
-                raw = late_buffer([P, PACK, H])
+        def load_up(weight):
+            raw = stream.tile([P, PACK, H], F32, name="raw", tag="raw", align_bytes=DMA_ALIGN)
             nc.sync.dma_start(out=raw[:], in_=weight.rearrange("(p j) c -> p j c", j=PACK))
             return raw
 
         def load_down(e0, count):
-            raw = late_buffer([P, count, PACK, N])
+            raw = stream.tile([P, count, PACK, N], F32, name="raw", tag="raw", align_bytes=DMA_ALIGN)
             nc.sync.dma_start(out=raw[:], in_=w2[e0 : e0 + count].rearrange("e (p j) c -> p e j c", j=PACK))
             return raw[:]
 
         def code_tiles(width, tag):
-            bufs = 3 if width == H else 5
+            bufs = 2 if width == H else 5
             tag = tag + str(width)
             codes = work.tile([P, width], U32, name=tag + "_codes", tag=tag + "_codes", align_bytes=ALIGN, bufs=bufs)
             scales = work.tile([P, width], U8, name=tag + "_scales", tag=tag + "_scales", align_bytes=ALIGN, bufs=bufs)
@@ -98,9 +80,8 @@ def tile_moe_shr_glu_gelu_kernel(
             nc.vector.quantize_mx(out=codes[:].bitcast(FP8X4), scales=scales[:], in_=rounded[:])
             return codes, scales
 
-        def round_up(raw, by_scalar, tag, rounded=None):
-            if rounded is None:
-                rounded = work.tile([P, PACK * H], BF16, name="up_bf", tag="up_bf", align_bytes=ALIGN, bufs=4)
+        def round_up(raw, by_scalar, tag):
+            rounded = work.tile([P, PACK * H], BF16, name=tag + "_bf", tag=tag + "_bf", align_bytes=ALIGN)
             if by_scalar:
                 on_scalar(
                     out=rounded[:].rearrange("p (t m j) -> p m j t", t=PACK, j=PACK),
@@ -163,8 +144,7 @@ def tile_moe_shr_glu_gelu_kernel(
         def column_groups(e):
             if e == SHARED:
                 return [(tok_words[:, t0 : t0 + C], tok_scales[:, t0 : t0 + C]) for t0 in range(0, T, C)]
-            s0, c0 = e * C // GATHER * GATHER, e * C % GATHER
-            return [(slot_words[s0][:, c0 : c0 + C], slot_scales[:, e * C : (e + 1) * C])]
+            return [(slot_words[:, e * C : (e + 1) * C], slot_scales[:, e * C : (e + 1) * C])]
 
         def rooms_of(raw):
             return [raw[:, j, :].rearrange("p (n t) -> p n t", t=PACK) for j in range(PACK)]
@@ -213,28 +193,21 @@ def tile_moe_shr_glu_gelu_kernel(
 
         def gather_slots(s0):
             offsets = offs_sb[:, s0 // LIST : (s0 + GATHER) // LIST]
-            tag = "words" + str(s0)
-            slot_words[s0] = keep.tile([P, GATHER], U32, name=tag, tag=tag, align_bytes=ALIGN)
-            on_vector(out=slot_words[s0][:], in_=tok_words[:].bitcast(U32).indirect(offsets))
+            on_vector(out=slot_words[:, s0 : s0 + GATHER], in_=tok_words[:].bitcast(U32).indirect(offsets))
             on_vector(out=slot_scales[:, s0 : s0 + GATHER], in_=tok_scales[:].indirect(offsets))
 
         last_two = (E - 2, E - 1)
         nc.sync.dma_start(out=tok_words[:], in_=x_words[0].rearrange("p t r -> p (t r)").bitcast(I32))
         nc.sync.dma_start(out=offs_sb[:], in_=offs)
         raw1, raw3, raw2 = {}, {}, {}
-        raw1[SHARED] = load_up(w1[SHARED], True)
+        raw1[SHARED] = load_up(w1[SHARED])
         for q in range(4):
             nc.sync.dma_start(
                 out=tok_scales[32 * q : 32 * q + 4, :].bitcast(I32),
                 in_=x_scales[0, 4 * q : 4 * q + 4, :].bitcast(I32),
             )
-        raw3[SHARED] = load_up(w3[SHARED], True)
-        raw1[0] = load_up(w1[0], True)
-        for e in range(PAIRS):
-            weights, raws = ((w3, raw3), (w1, raw1))[e % 2]
-            raws[e], raws[e + 1] = load_pair(weights, e)
-        raw3[PAIRS] = load_up(w3[PAIRS])
-        for e in range(PAIRS + 1, E - 2):
+        raw3[SHARED] = load_up(w3[SHARED])
+        for e in range(E - 2):
             raw1[e] = load_up(w1[e])
             raw3[e] = load_up(w3[e])
         for e in last_two:
@@ -248,49 +221,22 @@ def tile_moe_shr_glu_gelu_kernel(
         nc.sync.dma_start(out=pos1_sb[:], in_=pos1)
         gates = []
         for t0, width in ((0, TURNED), (TURNED, T - TURNED)):
-            gate_sb = late_buffer([P, 2, width])
+            gate_sb = stream.tile([P, 2, width], F32, name="raw", tag="raw", align_bytes=DMA_ALIGN)
             nc.sync.dma_start(out=gate_sb[:], in_=gate[:, :, t0 : t0 + width].rearrange("g p t -> p g t"))
             gates.append(gate_sb)
             if t0 == 0:
                 nc.sync.dma_start(out=pos2_sb[:], in_=pos2)
 
         gather_slots(0)
-        shared_bf = [
-            keep.tile([P, PACK * H], BF16, name="shared_bf", tag="words" + str(s0), align_bytes=ALIGN)
-            for s0 in range(GATHER, SLOTS, GATHER)
-        ]
-        w1q = quantize(round_up(raw1[SHARED], True, "w1", shared_bf[0]), "w1")
-        w3q = quantize(round_up(raw3[SHARED], True, "w3", shared_bf[1]), "w3")
+        w1q = quantize(round_up(raw1[SHARED], True, "w1"), "w1")
+        w3q = quantize(round_up(raw3[SHARED], True, "w3"), "w3")
         for s0 in range(GATHER, SLOTS, GATHER):
             gather_slots(s0)
 
-        acts = activations(SHARED, w1q, rooms_of(raw3[SHARED]) + rooms_of(raw1[SHARED]))
-        w1_bf = round_up(raw1[0], True, "w1")
-        h_bf = hidden(SHARED, w3q, acts)
-        codes = {("w1", 0): quantize(w1_bf, "w1")}
-        quantize_hidden(SHARED, h_bf)
-        for e in range(PAIRS):
-            tag, raws = (("w3", raw3), ("w1", raw1))[e % 2]
-            first_bf = round_up(raws[e], e == BOTH_ON_SCALAR, tag)
-            if e == BOTH_ON_SCALAR:
-                acts = activations(e - 1, codes["w1", e - 1], rooms_of(raws[e]))
-            second_bf = round_up(raws[e + 1], True, tag)
-            if e > 0 and e != BOTH_ON_SCALAR:
-                acts = activations(e - 1, codes["w1", e - 1], rooms_of(raws[e + 1]))
-            codes[tag, e] = quantize(first_bf, tag)
-            codes[tag, e + 1] = quantize(second_bf, tag)
-            if e > 0:
-                quantize_hidden(e - 1, hidden(e - 1, codes["w3", e - 1], acts))
-        acts = activations(PAIRS - 1, codes["w1", PAIRS - 1], rooms_of(raw1[PAIRS])[1:])
-        w3_bf = round_up(raw3[PAIRS], False, "w3")
-        h_bf = hidden(PAIRS - 1, codes["w3", PAIRS - 1], acts)
-        w1q, w3q = codes["w1", PAIRS], quantize(w3_bf, "w3")
-        quantize_hidden(PAIRS - 1, h_bf)
-
-        before = PAIRS
-        for e in range(PAIRS + 1, E - 2):
+        before = SHARED
+        for e in range(E - 2):
             w1_bf = round_up(raw1[e], True, "w1")
-            acts = activations(before, w1q, rooms_of(raw1[e]))
+            acts = activations(before, w1q, rooms_of(raw1[e]) + rooms_of(raw1[before]))
             w1q = quantize(w1_bf, "w1")
             w3_bf = round_up(raw3[e], e in W3_ON_SCALAR, "w3")
             h_bf = hidden(before, w3q, acts)
@@ -338,38 +284,41 @@ def tile_moe_shr_glu_gelu_kernel(
         for c0, width in CHUNKS:
             cols = slice(SLOTS + TURNED + c0, SLOTS + TURNED + c0 + width)
             product(ys_banks[1][:, c0 : c0 + width], w2q[SHARED], slice(0, N), h_codes[:, cols], h_scales[:, cols])
-        gated = keep.tile([P, 2, T], F32, name="parts")
+        gated = keep.tile([P, 2, T], F32, name="gated")
+        positions = (pos1_sb, pos2_sb)
 
-        def fetch(t0, width, r):
+        def results_of(t0, width, r):
+            return y_slots[:].indirect(positions[r][:, t0 // LIST : (t0 + width) // LIST])
+
+        def fetch_gated(t0, width, r):
             term = gated[:, r, t0 : t0 + width]
             g0 = t0 % TURNED
             nc.vector.tensor_tensor(
-                out=term,
-                in0=y_slots[:].indirect((pos1_sb, pos2_sb)[r][:, t0 // LIST : (t0 + width) // LIST]),
-                in1=gates[t0 // TURNED][:, r, g0 : g0 + width],
-                op=MULT,
+                out=term, in0=results_of(t0, width, r), in1=gates[t0 // TURNED][:, r, g0 : g0 + width], op=MULT
             )
             return term
 
-        fetch(0, TURNED, 0)
+        fetch_gated(0, TURNED, 0)
         for c0 in range(0, TURNED, P):
-            fetch(c0, P, 1)
+            fetch_gated(c0, P, 1)
         ys_sb = keep.tile([P, TURNED], F32, name="ys_sb")
-        (wide0, wide_width), (last0, last_width) = CHUNKS
-        picked = keep.tile([P, 2, wide_width], F32, name="picked")
-        for r, pos_sb in enumerate((pos1_sb, pos2_sb)):
-            offsets = pos_sb[:, TURNED // LIST : (TURNED + wide_width) // LIST]
-            nc.scalar.activation(out=picked[:, r, :], in_=y_slots[:].indirect(offsets), func=COPY)
+        wide, last = (slice(c0, c0 + width) for c0, width in CHUNKS)
+        wide_width, last_width = (width for c0, width in CHUNKS)
+        wide_picked = keep.tile([P, 2, wide_width], F32, name="wide_picked")
+        for r in range(2):
+            nc.scalar.activation(out=wide_picked[:, r, :], in_=results_of(TURNED, wide_width, r), func=COPY)
+        last_picked = keep.tile([P, last_width], F32, name="last_picked")
+        nc.scalar.activation(out=last_picked[:], in_=results_of(TURNED + last.start, last_width, 1), func=COPY)
         on_scalar(out=ys_sb[:], in_=ys_banks[0][:])
 
-        def turn(bank, term, start, stop):
-            nc.tensor.matmul(bank, lhsT=term, rhs=identity[:], is_transpose=True, start=start, stop=stop)
+        def turn(target, term, start, stop):
+            nc.tensor.matmul(target, lhsT=term, rhs=identity[:], is_transpose=True, start=start, stop=stop)
 
-        banks = [up_psum.tile([P, P], F32, name="sums", tag="b_bank") for c0 in range(0, TURNED, P)]
-        for sums, c0 in zip(banks, range(0, TURNED, P)):
+        sum_banks = [up_psum.tile([P, P], F32, name="sums", tag="b_bank") for c0 in range(0, TURNED, P)]
+        for sums, c0 in zip(sum_banks, range(0, TURNED, P)):
             turn(sums[:], gated[:, 0, c0 : c0 + P], True, False)
         turned = []
-        for sums, c0 in zip(banks, range(0, TURNED, P)):
+        for sums, c0 in zip(sum_banks, range(0, TURNED, P)):
             turn(sums[:], gated[:, 1, c0 : c0 + P], False, True)
             block = work.tile([P, P], F32, name="turned", tag="turned")
             on_scalar(out=block[:], in_=sums[:])
@@ -383,20 +332,18 @@ def tile_moe_shr_glu_gelu_kernel(
             on_scalar(out=result[:], in_=back[:])
             nc.scalar.dma_start(out=out[:, t0 : t0 + width], in_=result[:])
 
-        def combine(in0, in1, op, tag, result=None):
-            if result is None:
-                result = work.tile(
-                    [P] + list(in1.shape[1:]), F32, name=tag, tag=tag, bufs=len(CHUNKS), align_bytes=DMA_ALIGN
-                )[:]
-            nc.vector.tensor_tensor(out=result, in0=in0, in1=in1, op=op)
-            return result
+        def combine(in0, in1, op, tag):
+            shape = [P] + list(in1.shape[1:])
+            combined = work.tile(shape, F32, name=tag, tag=tag, bufs=len(CHUNKS), align_bytes=DMA_ALIGN)
+            nc.vector.tensor_tensor(out=combined[:], in0=in0, in1=in1, op=op)
+            return combined[:]
 
-        terms = combine(picked[:], gates[1][:, :, 0:wide_width], MULT, "terms")
-        last_first = fetch(TURNED + last0, last_width, 0)
-        partial = combine(ys_banks[1][:, 0:wide_width], terms[:, 0, :], ADD, "both")
-        last_second = fetch(TURNED + last0, last_width, 1)
-        last_partial = combine(ys_banks[1][:, last0 : last0 + last_width], last_first, ADD, "both")
-        total = combine(partial, terms[:, 1, :], ADD, "last_total")
-        nc.sync.dma_start(out=out[:, TURNED : TURNED + wide_width], in_=total)
-        total = combine(last_partial, last_second, ADD, "last_total")
-        nc.sync.dma_start(out=out[:, TURNED + last0 : T], in_=total)
+        wide_terms = combine(wide_picked[:], gates[1][:, :, wide], MULT, "terms")
+        last_first = fetch_gated(TURNED + last.start, last_width, 0)
+        wide_partial = combine(ys_banks[1][:, wide], wide_terms[:, 0, :], ADD, "partial")
+        last_second = combine(last_picked[:], gates[1][:, 1, last], MULT, "terms")
+        last_partial = combine(ys_banks[1][:, last], last_first, ADD, "partial")
+        wide_total = combine(wide_partial, wide_terms[:, 1, :], ADD, "added")
+        nc.sync.dma_start(out=out[:, TURNED : TURNED + wide_width], in_=wide_total)
+        last_total = combine(last_partial, last_second, ADD, "added")
+        nc.sync.dma_start(out=out[:, TURNED + last.start : T], in_=last_total)

@@ -26,8 +26,9 @@ ALIGN = 64
 DMA_ALIGN = 256
 LIST = 16
 GATHER = 512
-STREAM_BUFS = 14
-W3_ON_SCALAR = range(1, E - 2, 3)
+SMALL_BUFS, LARGE_BUFS = 6, 4
+PAIRS = 8
+BOTH_ON_SCALAR = 2
 TURNED = 384
 CHUNKS = [(0, 256), (256, 128)]
 
@@ -39,14 +40,15 @@ def tile_moe_shr_glu_gelu_kernel(
     on_vector, on_scalar = nc.vector.tensor_copy, nc.scalar.copy
     with ExitStack() as ctx:
         keep = ctx.enter_context(tc.tile_pool(name="keep", bufs=1))
-        stream = ctx.enter_context(tc.tile_pool(name="stream", bufs=STREAM_BUFS))
+        small = ctx.enter_context(tc.tile_pool(name="small", bufs=SMALL_BUFS))
+        large = ctx.enter_context(tc.tile_pool(name="large", bufs=LARGE_BUFS))
         work = ctx.enter_context(tc.tile_pool(name="work", bufs=3))
         up_psum = ctx.enter_context(tc.psum_pool(name="up_psum", bufs=3))
         down_psum = ctx.enter_context(tc.psum_pool(name="down_psum", bufs=2))
 
         tok_words = keep.tile([P, T], I32, name="tok_words", align_bytes=DMA_ALIGN)
         tok_scales = keep.tile([P, T], U8, name="tok_scales", align_bytes=DMA_ALIGN)
-        slot_words = keep.tile([P, SLOTS], U32, name="slot_words", align_bytes=ALIGN)
+        slot_words = {}
         slot_scales = keep.tile([P, SLOTS], U8, name="slot_scales", align_bytes=ALIGN)
         offs_sb = keep.tile([P, SLOTS // LIST], U16, name="offs_sb")
         pos1_sb = keep.tile([P, T // LIST], U16, name="pos1_sb")
@@ -54,22 +56,37 @@ def tile_moe_shr_glu_gelu_kernel(
         h_codes = keep.tile([P, SLOTS + T], U32, name="h_codes", align_bytes=ALIGN)
         h_scales = keep.tile([P, SLOTS + T], U8, name="h_scales", align_bytes=ALIGN)
         y_slots = keep.tile([P, SLOTS], F32, name="y_slots")
-        nc.gpsimd.memset(tok_scales[:].bitcast(I32), 0)
+        nc.vector.memset(tok_scales[:].bitcast(I32), 0)
         identity = keep.tile([P, P], F32, name="identity")
         make_identity(nc, identity[:])
 
-        def load_up(weight):
-            raw = stream.tile([P, PACK, H], F32, name="raw", tag="raw", align_bytes=DMA_ALIGN)
+        late_loads = []
+
+        def late_buffer(shape):
+            pool = small if len(late_loads) % (SMALL_BUFS + LARGE_BUFS) < SMALL_BUFS else large
+            late_loads.append(shape)
+            return pool.tile(shape, F32, name="raw", tag="raw", align_bytes=DMA_ALIGN)
+
+        def load_pair(weights, e):
+            raw = large.tile([P, 2, PACK, H], F32, name="raw", tag="raw", align_bytes=DMA_ALIGN)
+            nc.sync.dma_start(out=raw[:], in_=weights[e : e + 2].rearrange("e (p j) c -> p e j c", j=PACK))
+            return raw[:, 0], raw[:, 1]
+
+        def load_up(weight, early=False):
+            if early:
+                raw = small.tile([P, PACK, H], F32, name="raw", tag="raw", align_bytes=DMA_ALIGN)
+            else:
+                raw = late_buffer([P, PACK, H])
             nc.sync.dma_start(out=raw[:], in_=weight.rearrange("(p j) c -> p j c", j=PACK))
             return raw
 
         def load_down(e0, count):
-            raw = stream.tile([P, count, PACK, N], F32, name="raw", tag="raw", align_bytes=DMA_ALIGN)
+            raw = late_buffer([P, count, PACK, N])
             nc.sync.dma_start(out=raw[:], in_=w2[e0 : e0 + count].rearrange("e (p j) c -> p e j c", j=PACK))
             return raw[:]
 
         def code_tiles(width, tag):
-            bufs = 2 if width == H else 5
+            bufs = 3 if width == H else 5
             tag = tag + str(width)
             codes = work.tile([P, width], U32, name=tag + "_codes", tag=tag + "_codes", align_bytes=ALIGN, bufs=bufs)
             scales = work.tile([P, width], U8, name=tag + "_scales", tag=tag + "_scales", align_bytes=ALIGN, bufs=bufs)
@@ -80,8 +97,9 @@ def tile_moe_shr_glu_gelu_kernel(
             nc.vector.quantize_mx(out=codes[:].bitcast(FP8X4), scales=scales[:], in_=rounded[:])
             return codes, scales
 
-        def round_up(raw, by_scalar, tag):
-            rounded = work.tile([P, PACK * H], BF16, name=tag + "_bf", tag=tag + "_bf", align_bytes=ALIGN)
+        def round_up(raw, by_scalar, rounded=None):
+            if rounded is None:
+                rounded = work.tile([P, PACK * H], BF16, name="up_bf", tag="up_bf", align_bytes=ALIGN, bufs=4)
             if by_scalar:
                 on_scalar(
                     out=rounded[:].rearrange("p (t m j) -> p m j t", t=PACK, j=PACK),
@@ -144,7 +162,8 @@ def tile_moe_shr_glu_gelu_kernel(
         def column_groups(e):
             if e == SHARED:
                 return [(tok_words[:, t0 : t0 + C], tok_scales[:, t0 : t0 + C]) for t0 in range(0, T, C)]
-            return [(slot_words[:, e * C : (e + 1) * C], slot_scales[:, e * C : (e + 1) * C])]
+            s0, c0 = e * C // GATHER * GATHER, e * C % GATHER
+            return [(slot_words[s0][:, c0 : c0 + C], slot_scales[:, e * C : (e + 1) * C])]
 
         def rooms_of(raw):
             return [raw[:, j, :].rearrange("p (n t) -> p n t", t=PACK) for j in range(PACK)]
@@ -193,21 +212,28 @@ def tile_moe_shr_glu_gelu_kernel(
 
         def gather_slots(s0):
             offsets = offs_sb[:, s0 // LIST : (s0 + GATHER) // LIST]
-            on_vector(out=slot_words[:, s0 : s0 + GATHER], in_=tok_words[:].bitcast(U32).indirect(offsets))
+            tag = "words" + str(s0)
+            slot_words[s0] = keep.tile([P, GATHER], U32, name=tag, tag=tag, align_bytes=ALIGN)
+            on_vector(out=slot_words[s0][:], in_=tok_words[:].bitcast(U32).indirect(offsets))
             on_vector(out=slot_scales[:, s0 : s0 + GATHER], in_=tok_scales[:].indirect(offsets))
 
         last_two = (E - 2, E - 1)
         nc.sync.dma_start(out=tok_words[:], in_=x_words[0].rearrange("p t r -> p (t r)").bitcast(I32))
         nc.sync.dma_start(out=offs_sb[:], in_=offs)
         raw1, raw3, raw2 = {}, {}, {}
-        raw1[SHARED] = load_up(w1[SHARED])
+        raw1[SHARED] = load_up(w1[SHARED], True)
         for q in range(4):
             nc.sync.dma_start(
                 out=tok_scales[32 * q : 32 * q + 4, :].bitcast(I32),
                 in_=x_scales[0, 4 * q : 4 * q + 4, :].bitcast(I32),
             )
-        raw3[SHARED] = load_up(w3[SHARED])
-        for e in range(E - 2):
+        raw3[SHARED] = load_up(w3[SHARED], True)
+        raw1[0] = load_up(w1[0], True)
+        for e in range(PAIRS):
+            weights, raws = ((w3, raw3), (w1, raw1))[e % 2]
+            raws[e], raws[e + 1] = load_pair(weights, e)
+        raw3[PAIRS] = load_up(w3[PAIRS])
+        for e in range(PAIRS + 1, E - 2):
             raw1[e] = load_up(w1[e])
             raw3[e] = load_up(w3[e])
         for e in last_two:
@@ -221,31 +247,58 @@ def tile_moe_shr_glu_gelu_kernel(
         nc.sync.dma_start(out=pos1_sb[:], in_=pos1)
         gates = []
         for t0, width in ((0, TURNED), (TURNED, T - TURNED)):
-            gate_sb = stream.tile([P, 2, width], F32, name="raw", tag="raw", align_bytes=DMA_ALIGN)
+            gate_sb = late_buffer([P, 2, width])
             nc.sync.dma_start(out=gate_sb[:], in_=gate[:, :, t0 : t0 + width].rearrange("g p t -> p g t"))
             gates.append(gate_sb)
             if t0 == 0:
                 nc.sync.dma_start(out=pos2_sb[:], in_=pos2)
 
         gather_slots(0)
-        w1q = quantize(round_up(raw1[SHARED], True, "w1"), "w1")
-        w3q = quantize(round_up(raw3[SHARED], True, "w3"), "w3")
+        up_shared_bf = [
+            keep.tile([P, PACK * H], BF16, name="up_shared_bf", tag="words" + str(s0), align_bytes=ALIGN)
+            for s0 in range(GATHER, SLOTS, GATHER)
+        ]
+        w1q = quantize(round_up(raw1[SHARED], True, up_shared_bf[0]), "w1")
+        w3q = quantize(round_up(raw3[SHARED], True, up_shared_bf[1]), "w3")
         for s0 in range(GATHER, SLOTS, GATHER):
             gather_slots(s0)
 
-        before = SHARED
-        for e in range(E - 2):
-            w1_bf = round_up(raw1[e], True, "w1")
-            acts = activations(before, w1q, rooms_of(raw1[e]) + rooms_of(raw1[before]))
+        acts = activations(SHARED, w1q, rooms_of(raw3[SHARED]) + rooms_of(raw1[SHARED]))
+        w1_bf = round_up(raw1[0], True)
+        h_bf = hidden(SHARED, w3q, acts)
+        up_q = {("w1", 0): quantize(w1_bf, "w1")}
+        quantize_hidden(SHARED, h_bf)
+        for e in range(PAIRS):
+            tag, raws = (("w3", raw3), ("w1", raw1))[e % 2]
+            first_bf = round_up(raws[e], e == BOTH_ON_SCALAR)
+            if e == BOTH_ON_SCALAR:
+                acts = activations(e - 1, up_q["w1", e - 1], rooms_of(raws[e]))
+            second_bf = round_up(raws[e + 1], True)
+            if e > 0 and e != BOTH_ON_SCALAR:
+                acts = activations(e - 1, up_q["w1", e - 1], rooms_of(raws[e + 1]))
+            up_q[tag, e] = quantize(first_bf, tag)
+            up_q[tag, e + 1] = quantize(second_bf, tag)
+            if e > 0:
+                quantize_hidden(e - 1, hidden(e - 1, up_q["w3", e - 1], acts))
+        acts = activations(PAIRS - 1, up_q["w1", PAIRS - 1], rooms_of(raw1[PAIRS])[1:])
+        w3_bf = round_up(raw3[PAIRS], False)
+        h_bf = hidden(PAIRS - 1, up_q["w3", PAIRS - 1], acts)
+        w1q, w3q = up_q["w1", PAIRS], quantize(w3_bf, "w3")
+        quantize_hidden(PAIRS - 1, h_bf)
+
+        before = PAIRS
+        for e in range(PAIRS + 1, E - 2):
+            w1_bf = round_up(raw1[e], True)
+            acts = activations(before, w1q, rooms_of(raw1[e]))
             w1q = quantize(w1_bf, "w1")
-            w3_bf = round_up(raw3[e], e in W3_ON_SCALAR, "w3")
+            w3_bf = round_up(raw3[e], False)
             h_bf = hidden(before, w3q, acts)
             w3q = quantize(w3_bf, "w3")
             quantize_hidden(before, h_bf)
             before = e
 
         near, final = last_two
-        w1_bf = round_up(raw1[near], True, "w1")
+        w1_bf = round_up(raw1[near], True)
         acts = activations(before, w1q, rooms_of(raw1[near]))
         w1q = quantize(w1_bf, "w1")
         halves = round_up_together(raw1[final])

@@ -57,6 +57,8 @@ def tile_moe_shr_glu_gelu_kernel(
         h_scales = keep.tile([P, SLOTS + T], U8, name="h_scales", align_bytes=ALIGN)
         y_slots = keep.tile([P, SLOTS], F32, name="y_slots")
         nc.vector.memset(tok_scales[:].bitcast(I32), 0)
+        gate_rows = keep.tile([P, T // 2], F32, name="gate_rows", tag="ys_sb", align_bytes=DMA_ALIGN)
+        nc.gpsimd.memset(gate_rows[:], 0.0)
         identity = keep.tile([P, P], F32, name="identity")
         make_identity(nc, identity[:])
 
@@ -141,6 +143,26 @@ def tile_moe_shr_glu_gelu_kernel(
             )
             return rounded
 
+        def turn(target, term, start, stop):
+            nc.tensor.matmul(target, lhsT=term, rhs=identity[:], is_transpose=True, start=start, stop=stop)
+
+        def spread_gates():
+            blocks = T // 2 // P
+            bank = down_psum.tile([P, blocks, P], F32, name="columns", tag="y_bank")
+            for c in range(blocks):
+                turn(bank[:, c, :], gate_rows[:, c * P : (c + 1) * P], True, True)
+            columns = keep.tile([P, blocks, 4], F32, name="gate_columns")
+            on_scalar(out=columns[:], in_=bank[:, :, 0:4])
+            gates = [keep.tile([P, 2, T // 2], F32, name="gates", tag="gates" + str(h)) for h in range(2)]
+            for g in range(2):
+                for h in range(2):
+                    bank = down_psum.tile([P, T // 2], F32, name="spread", tag="y_bank")
+                    for c in range(blocks):
+                        column = columns[:, c, 2 * g + h : 2 * g + h + 1]
+                        turn(bank[:, c * P : (c + 1) * P], column.to_broadcast([P, P]), True, True)
+                    on_scalar(out=gates[h][:, g, :], in_=bank[:])
+            return gates
+
         def product(target, weights, cols, words, scales):
             codes, code_scales = weights
             nc.tensor.matmul_mx(
@@ -180,7 +202,7 @@ def tile_moe_shr_glu_gelu_kernel(
 
         def hidden(e, w3q, acts):
             if e == SHARED:
-                h_bf = keep.tile([P, PACK * T], BF16, name="hs_bf", align_bytes=ALIGN)
+                h_bf = keep.tile([P, PACK * T], BF16, name="hs_bf", tag="hs_bf", align_bytes=ALIGN)
             else:
                 h_bf = work.tile([P, PACK * C], BF16, name="h_bf", tag="h_bf", align_bytes=ALIGN, bufs=2)
             for place, columns in enumerate(column_groups(e)):
@@ -218,6 +240,8 @@ def tile_moe_shr_glu_gelu_kernel(
             on_vector(out=slot_scales[:, s0 : s0 + GATHER], in_=tok_scales[:].indirect(offsets))
 
         last_two = (E - 2, E - 1)
+        half_rows = gate.rearrange("g n (h t) -> (g n h) t", h=2)
+        nc.sync.dma_start(out=gate_rows[0:4, :], in_=half_rows[0 : 3 * (P + 1) + 1 : P + 1, :])
         nc.sync.dma_start(out=tok_words[:], in_=x_words[0].rearrange("p t r -> p (t r)").bitcast(I32))
         nc.sync.dma_start(out=offs_sb[:], in_=offs)
         raw1, raw3, raw2 = {}, {}, {}
@@ -240,18 +264,15 @@ def tile_moe_shr_glu_gelu_kernel(
             raw1[e] = load_up(w1[e])
         for e in last_two:
             raw3[e] = load_up(w3[e])
-        for e in (0, 2, 4, 6, 10):
+        for e in (0, 2, 4, 6):
             raw2[e] = load_down(e, 2)
+        raw2[10] = late_buffer([P, 2, PACK, N])[:]
+        for place in range(2):
+            nc.sync.dma_start(out=raw2[10][:, place], in_=w2[10 + place].rearrange("(p j) c -> p j c", j=PACK))
         for e in (8, 9, SHARED):
             raw2[e] = load_down(e, 1)
         nc.sync.dma_start(out=pos1_sb[:], in_=pos1)
-        gates = []
-        for t0, width in ((0, TURNED), (TURNED, T - TURNED)):
-            gate_sb = late_buffer([P, 2, width])
-            nc.sync.dma_start(out=gate_sb[:], in_=gate[:, :, t0 : t0 + width].rearrange("g p t -> p g t"))
-            gates.append(gate_sb)
-            if t0 == 0:
-                nc.sync.dma_start(out=pos2_sb[:], in_=pos2)
+        nc.sync.dma_start(out=pos2_sb[:], in_=pos2)
 
         gather_slots(0)
         up_shared_bf = [
@@ -262,6 +283,8 @@ def tile_moe_shr_glu_gelu_kernel(
         w3q = quantize(round_up(raw3[SHARED], True, up_shared_bf[1]), "w3")
         for s0 in range(GATHER, SLOTS, GATHER):
             gather_slots(s0)
+
+        gates = spread_gates()
 
         acts = activations(SHARED, w1q, rooms_of(raw3[SHARED]) + rooms_of(raw1[SHARED]))
         w1_bf = round_up(raw1[0], True)
@@ -337,7 +360,7 @@ def tile_moe_shr_glu_gelu_kernel(
         for c0, width in CHUNKS:
             cols = slice(SLOTS + TURNED + c0, SLOTS + TURNED + c0 + width)
             product(ys_banks[1][:, c0 : c0 + width], w2q[SHARED], slice(0, N), h_codes[:, cols], h_scales[:, cols])
-        gated = keep.tile([P, 2, T], F32, name="gated")
+        gated = keep.tile([P, 2, T], F32, name="gated", tag="hs_bf", align_bytes=ALIGN)
         positions = (pos1_sb, pos2_sb)
 
         def results_of(t0, width, r):
@@ -354,7 +377,7 @@ def tile_moe_shr_glu_gelu_kernel(
         fetch_gated(0, TURNED, 0)
         for c0 in range(0, TURNED, P):
             fetch_gated(c0, P, 1)
-        ys_sb = keep.tile([P, TURNED], F32, name="ys_sb")
+        ys_sb = keep.tile([P, TURNED], F32, name="ys_sb", tag="ys_sb", align_bytes=DMA_ALIGN)
         wide, last = (slice(c0, c0 + width) for c0, width in CHUNKS)
         wide_width, last_width = (width for c0, width in CHUNKS)
         wide_picked = keep.tile([P, 2, wide_width], F32, name="wide_picked")
@@ -363,9 +386,6 @@ def tile_moe_shr_glu_gelu_kernel(
         last_picked = keep.tile([P, last_width], F32, name="last_picked")
         nc.scalar.activation(out=last_picked[:], in_=results_of(TURNED + last.start, last_width, 1), func=COPY)
         on_scalar(out=ys_sb[:], in_=ys_banks[0][:])
-
-        def turn(target, term, start, stop):
-            nc.tensor.matmul(target, lhsT=term, rhs=identity[:], is_transpose=True, start=start, stop=stop)
 
         sum_banks = [up_psum.tile([P, P], F32, name="sums", tag="b_bank") for c0 in range(0, TURNED, P)]
         for sums, c0 in zip(sum_banks, range(0, TURNED, P)):

@@ -347,6 +347,9 @@ def tile_moe_shr_glu_gelu_kernel(
             w2q[e_vector] = quantize(vector_bf, "w2")
         shared_bf = round_down(raw2[SHARED], on_vector, vector_bf)
         slot_outputs(0, [w2q[0], w2q[2]], down_psum, "y_bank")
+        for half in range(2):
+            idle = up_psum.tile([P, 4 * C], F32, name="idle", tag="b_bank")
+            product(idle[:], w2q[4], slice(half * N, (half + 1) * N), h_codes[:, : 4 * C], h_scales[:, : 4 * C])
         slot_outputs(4, [w2q[4], w2q[6], w2q[7]], down_psum, "y_bank")
         slot_outputs(10, [w2q[10]], up_psum, "a_bank")
         slot_outputs(8, [w2q[8]], up_psum, "a_bank")

@@ -181,6 +181,10 @@ def tile_moe_shr_glu_gelu_kernel(
                 product(bank[:, t, :], weights, slice(P * t, P * (t + 1)), words, scales)
             return bank[:].rearrange("p t n -> p n t")
 
+        def warm_up(weights, n0, pool, tag):
+            idle = pool.tile([P, 4 * C], F32, name="idle", tag=tag)
+            product(idle[:], weights, slice(n0, n0 + P), h_codes[:, : 4 * C], h_scales[:, : 4 * C])
+
         def column_groups(e):
             if e == SHARED:
                 return [(tok_words[:, t0 : t0 + C], tok_scales[:, t0 : t0 + C]) for t0 in range(0, T, C)]
@@ -336,6 +340,8 @@ def tile_moe_shr_glu_gelu_kernel(
         for place, e in enumerate(last_two):
             multiply(last_w3q[place], column_groups(e)[0], acts[place], h_bf, place)
 
+        warm_up(last_w3q[0], H - P, down_psum, "y_bank")
+
         raw2[6], raw2[7] = raw2[6][:, 0:1], raw2[6][:, 1:2]
         scalar_bf = {e: round_down(raw2[e], on_scalar) for e in (0, 2, 4, 6, 8)}
         w2q = {0: quantize(scalar_bf[0], "w2")}
@@ -348,8 +354,7 @@ def tile_moe_shr_glu_gelu_kernel(
         shared_bf = round_down(raw2[SHARED], on_vector, vector_bf)
         slot_outputs(0, [w2q[0], w2q[2]], down_psum, "y_bank")
         for half in range(2):
-            idle = up_psum.tile([P, 4 * C], F32, name="idle", tag="b_bank")
-            product(idle[:], w2q[4], slice(half * N, (half + 1) * N), h_codes[:, : 4 * C], h_scales[:, : 4 * C])
+            warm_up(w2q[4], half * N, up_psum, "b_bank")
         slot_outputs(4, [w2q[4], w2q[6], w2q[7]], down_psum, "y_bank")
         slot_outputs(10, [w2q[10]], up_psum, "a_bank")
         slot_outputs(8, [w2q[8]], up_psum, "a_bank")
@@ -363,6 +368,7 @@ def tile_moe_shr_glu_gelu_kernel(
         for c0, width in CHUNKS:
             cols = slice(SLOTS + TURNED + c0, SLOTS + TURNED + c0 + width)
             product(ys_banks[1][:, c0 : c0 + width], w2q[SHARED], slice(0, N), h_codes[:, cols], h_scales[:, cols])
+        warm_up(w2q[SHARED], 0, down_psum, "y_bank")
         gated = keep.tile([P, 2, T], F32, name="gated", tag="hs_bf", align_bytes=ALIGN)
         positions = (pos1_sb, pos2_sb)
 

@@ -28,7 +28,8 @@ LIST = 16
 GATHER = 512
 SMALL_BUFS, LARGE_BUFS = 6, 4
 PAIRS = 8
-BOTH_ON_SCALAR = 2
+H_GROUPS = {3: (0, 4), 7: (4, 4), 9: (8, 2)}
+GATE_ROW0, GATE_STEP = 8, 4
 TURNED = 384
 CHUNKS = [(0, 256), (256, 128)]
 
@@ -49,7 +50,7 @@ def tile_moe_shr_glu_gelu_kernel(
         tok_words = keep.tile([P, T], I32, name="tok_words", align_bytes=DMA_ALIGN)
         tok_scales = keep.tile([P, T], U8, name="tok_scales", align_bytes=DMA_ALIGN)
         slot_words = {}
-        slot_scales = keep.tile([P, SLOTS], U8, name="slot_scales", align_bytes=ALIGN)
+        slot_scales = {}
         offs_sb = keep.tile([P, SLOTS // LIST], U16, name="offs_sb")
         pos1_sb = keep.tile([P, T // LIST], U16, name="pos1_sb")
         pos2_sb = keep.tile([P, T // LIST], U16, name="pos2_sb")
@@ -115,20 +116,19 @@ def tile_moe_shr_glu_gelu_kernel(
             return rounded
 
         def round_up_together(raw):
+            rounded = work.tile([P, PACK * H], BF16, name="up_bf", tag="up_bf", align_bytes=ALIGN, bufs=4)
             source = raw[:].rearrange("p j (m t) -> p m j t", t=PACK)
-            halves = []
             for u, copy in enumerate((on_vector, on_scalar)):
-                rounded = work.tile([P, PACK * H // 2], BF16, name="part_bf", tag="part_bf", align_bytes=ALIGN, bufs=4)
-                view = rounded[:].rearrange("p (t m j) -> p m j t", t=2, j=PACK)
-                copy(out=view, in_=source[:, :, :, 2 * u : 2 * u + 2])
-                halves.append(rounded)
-            return halves
+                half = rounded[:, u * PACK * H // 2 : (u + 1) * PACK * H // 2]
+                copy(out=half.rearrange("p (t m j) -> p m j t", t=2, j=PACK), in_=source[:, :, :, 2 * u : 2 * u + 2])
+            return rounded
 
-        def quantize_halves(halves, tag):
+        def quantize_halves(rounded, tag):
             codes, scales = code_tiles(H, tag)
-            for u, rounded in enumerate(halves):
+            for u in range(2):
                 cols = slice(u * H // 2, (u + 1) * H // 2)
-                nc.vector.quantize_mx(out=codes[:, cols].bitcast(FP8X4), scales=scales[:, cols], in_=rounded[:])
+                half = rounded[:, u * PACK * H // 2 : (u + 1) * PACK * H // 2]
+                nc.vector.quantize_mx(out=codes[:, cols].bitcast(FP8X4), scales=scales[:, cols], in_=half)
             return codes, scales
 
         def round_down(raw, copy, rounded=None):
@@ -152,7 +152,7 @@ def tile_moe_shr_glu_gelu_kernel(
             for c in range(blocks):
                 turn(bank[:, c, :], gate_rows[:, c * P : (c + 1) * P], True, True)
             columns = keep.tile([P, blocks, 4], F32, name="gate_columns")
-            on_scalar(out=columns[:], in_=bank[:, :, 0:4])
+            on_scalar(out=columns[:], in_=bank[:, :, GATE_ROW0 : GATE_ROW0 + 4 * GATE_STEP : GATE_STEP])
             gates = [keep.tile([P, 2, T // 2], F32, name="gates", tag="gates" + str(h)) for h in range(2)]
             for g in range(2):
                 for h in range(2):
@@ -189,7 +189,7 @@ def tile_moe_shr_glu_gelu_kernel(
             if e == SHARED:
                 return [(tok_words[:, t0 : t0 + C], tok_scales[:, t0 : t0 + C]) for t0 in range(0, T, C)]
             s0, c0 = e * C // GATHER * GATHER, e * C % GATHER
-            return [(slot_words[s0][:, c0 : c0 + C], slot_scales[:, e * C : (e + 1) * C])]
+            return [(slot_words[s0][:, c0 : c0 + C], slot_scales[s0][:, c0 : c0 + C])]
 
         def rooms_of(raw):
             return [raw[:, j, :].rearrange("p (n t) -> p n t", t=PACK) for j in range(PACK)]
@@ -204,25 +204,29 @@ def tile_moe_shr_glu_gelu_kernel(
             view = h_bf[:, place * PACK * C : (place + 1) * PACK * C].rearrange("p (n t) -> p n t", t=PACK)
             nc.vector.tensor_tensor(out=view, in0=up_product(w3q, *columns, "b_bank"), in1=act, op=MULT)
 
-        def hidden(e, w3q, acts):
-            if e == SHARED:
-                h_bf = keep.tile([P, PACK * T], BF16, name="hs_bf", tag="hs_bf", align_bytes=ALIGN)
-            else:
-                h_bf = work.tile([P, PACK * C], BF16, name="h_bf", tag="h_bf", align_bytes=ALIGN, bufs=2)
-            for place, columns in enumerate(column_groups(e)):
-                multiply(w3q, columns, acts[place], h_bf, place)
-            return h_bf
+        def h_tile(columns):
+            return keep.tile([P, PACK * columns], BF16, name="h_bf", tag="h_bf", align_bytes=ALIGN)
 
         def quantize_hidden(e, h_bf):
             count = h_bf.shape[1] // PACK
-            width = min(count, 2 * C)
-            for c0 in range(0, count, width):
+            for c0 in range(0, count, 4 * C):
+                width = min(count - c0, 4 * C)
                 h0 = e * C + c0
                 nc.vector.quantize_mx(
                     out=h_codes[:, h0 : h0 + width].bitcast(FP8X4),
                     scales=h_scales[:, h0 : h0 + width],
                     in_=h_bf[:, c0 * PACK : (c0 + width) * PACK],
                 )
+
+        open_h = {}
+
+        def hidden(e, act):
+            first, count = H_GROUPS[min(last for last in H_GROUPS if last >= e)]
+            if e == first:
+                open_h[first] = h_tile(count * C)
+            multiply(up_q["w3", e], column_groups(e)[0], act, open_h[first], e - first)
+            if e == first + count - 1:
+                quantize_hidden(first, open_h[first])
 
         def slot_outputs(e0, groups, pool, tag):
             count = sum(codes.shape[1] // N for codes, scales in groups)
@@ -236,16 +240,13 @@ def tile_moe_shr_glu_gelu_kernel(
                     place = place + 1
             on_scalar(out=y_slots[:, e0 * C : (e0 + count) * C], in_=bank[:])
 
-        def gather_slots(s0):
+        def gather(s0, gathered, source, dtype, tag):
             offsets = offs_sb[:, s0 // LIST : (s0 + GATHER) // LIST]
-            tag = "words" + str(s0)
-            slot_words[s0] = keep.tile([P, GATHER], U32, name=tag, tag=tag, align_bytes=ALIGN)
-            on_vector(out=slot_words[s0][:], in_=tok_words[:].bitcast(U32).indirect(offsets))
-            on_vector(out=slot_scales[:, s0 : s0 + GATHER], in_=tok_scales[:].indirect(offsets))
+            gathered[s0] = keep.tile([P, GATHER], dtype, name=tag, tag=tag + str(s0), align_bytes=ALIGN)
+            on_vector(out=gathered[s0][:], in_=source.indirect(offsets))
 
         last_two = (E - 2, E - 1)
         half_rows = gate.rearrange("g n (h t) -> (g n h) t", h=2)
-        nc.sync.dma_start(out=gate_rows[0:4, :], in_=half_rows[0 : 3 * (P + 1) + 1 : P + 1, :])
         nc.sync.dma_start(out=tok_words[:], in_=x_words[0].rearrange("p t r -> p (t r)").bitcast(I32))
         nc.sync.dma_start(out=offs_sb[:], in_=offs)
         raw1, raw3, raw2 = {}, {}, {}
@@ -259,6 +260,11 @@ def tile_moe_shr_glu_gelu_kernel(
         raw1[0] = load_up(w1[0], True)
         for e in range(PAIRS):
             weights, raws = ((w3, raw3), (w1, raw1))[e % 2]
+            if e == LARGE_BUFS:
+                nc.sync.dma_start(
+                    out=gate_rows[GATE_ROW0 : GATE_ROW0 + 4 * GATE_STEP : GATE_STEP, :],
+                    in_=half_rows[0 : 3 * (P + 1) + 1 : P + 1, :],
+                )
             raws[e], raws[e + 1] = load_pair(weights, e)
         raw3[PAIRS] = load_up(w3[PAIRS])
         for e in range(PAIRS + 1, E - 2):
@@ -278,64 +284,61 @@ def tile_moe_shr_glu_gelu_kernel(
         nc.sync.dma_start(out=pos1_sb[:], in_=pos1)
         nc.sync.dma_start(out=pos2_sb[:], in_=pos2)
 
-        gather_slots(0)
-        up_shared_bf = [
-            keep.tile([P, PACK * H], BF16, name="up_shared_bf", tag="words" + str(s0), align_bytes=ALIGN)
-            for s0 in range(GATHER, SLOTS, GATHER)
-        ]
-        w1q = quantize(round_up(raw1[SHARED], True, up_shared_bf[0]), "w1")
-        w3q = quantize(round_up(raw3[SHARED], True, up_shared_bf[1]), "w3")
-        for s0 in range(GATHER, SLOTS, GATHER):
-            gather_slots(s0)
-
-        gates = spread_gates()
-
+        for s0 in range(0, SLOTS, GATHER):
+            gather(s0, slot_words, tok_words[:].bitcast(U32), U32, "words")
+        last_gather = SLOTS - GATHER
+        for s0 in range(0, last_gather, GATHER):
+            gather(s0, slot_scales, tok_scales[:], U8, "scales")
+        w1_bf = keep.tile([P, PACK * H], BF16, name="w1_bf", tag="scales" + str(last_gather), align_bytes=ALIGN)
+        w1q = quantize(round_up(raw1[SHARED], True, w1_bf), "w1")
+        gather(last_gather, slot_scales, tok_scales[:], U8, "scales")
+        w3q = quantize(round_up(raw3[SHARED], True), "w3")
+        w1_bf = round_up(raw1[0], False)
         acts = activations(SHARED, w1q, rooms_of(raw3[SHARED]) + rooms_of(raw1[SHARED]))
-        w1_bf = round_up(raw1[0], True)
-        h_bf = hidden(SHARED, w3q, acts)
+        h_bf = h_tile(T)
+        for place, columns in enumerate(column_groups(SHARED)):
+            multiply(w3q, columns, acts[place], h_bf, place)
         up_q = {("w1", 0): quantize(w1_bf, "w1")}
         quantize_hidden(SHARED, h_bf)
-        for e in range(PAIRS):
-            tag, raws = (("w3", raw3), ("w1", raw1))[e % 2]
-            first_bf = round_up(raws[e], e == BOTH_ON_SCALAR)
-            if e == BOTH_ON_SCALAR:
-                acts = activations(e - 1, up_q["w1", e - 1], rooms_of(raws[e]))
-            second_bf = round_up(raws[e + 1], True)
-            if e > 0 and e != BOTH_ON_SCALAR:
-                acts = activations(e - 1, up_q["w1", e - 1], rooms_of(raws[e + 1]))
-            up_q[tag, e] = quantize(first_bf, tag)
-            up_q[tag, e + 1] = quantize(second_bf, tag)
-            if e > 0:
-                quantize_hidden(e - 1, hidden(e - 1, up_q["w3", e - 1], acts))
-        acts = activations(PAIRS - 1, up_q["w1", PAIRS - 1], rooms_of(raw1[PAIRS])[1:])
-        w3_bf = round_up(raw3[PAIRS], False)
-        h_bf = hidden(PAIRS - 1, up_q["w3", PAIRS - 1], acts)
-        w1q, w3q = up_q["w1", PAIRS], quantize(w3_bf, "w3")
-        quantize_hidden(PAIRS - 1, h_bf)
+        for e in range(2):
+            up_q["w3", e] = quantize(round_up(raw3[e], True), "w3")
 
-        before = PAIRS
-        for e in range(PAIRS + 1, E - 2):
-            w1_bf = round_up(raw1[e], True)
-            acts = activations(before, w1q, rooms_of(raw1[e]))
-            w1q = quantize(w1_bf, "w1")
-            w3_bf = round_up(raw3[e], False)
-            h_bf = hidden(before, w3q, acts)
-            w3q = quantize(w3_bf, "w3")
-            quantize_hidden(before, h_bf)
-            before = e
+        def raw_of(tag, e):
+            return (raw1 if tag == "w1" else raw3)[e]
 
+        def take_in(matrices):
+            rounded = [round_up_together(raw_of(tag, e)) for tag, e in matrices]
+            for place, (tag, e) in enumerate(matrices):
+                up_q[tag, e] = quantize(rounded[place], tag)
+
+        def activation(e, room):
+            return activations(e, up_q["w1", e], [room])[0]
+
+        for e in range(1, PAIRS - 1):
+            tag = ("w3", "w1")[e % 2]
+            take_in([(tag, e), (tag, e + 1)])
+            hidden(e - 1, activation(e - 1, rooms_of(raw_of(tag, e))[0]))
+            if e == LARGE_BUFS:
+                gates = spread_gates()
+        take_in([("w1", 7), ("w1", 8)])
+        acts = [activation(e, rooms_of(raw1[7])[e - 6]) for e in (6, 7)]
+        rounded = round_up_together(raw3[8])
+        hidden(6, acts[0])
+        hidden(7, acts[1])
+        up_q["w3", 8] = quantize(rounded, "w3")
+        act = activation(8, rooms_of(raw3[8])[0])
+        rounded = round_up_together(raw1[9])
+        hidden(8, act)
+        up_q["w1", 9] = quantize(rounded, "w1")
+        take_in([("w3", 9)])
         near, final = last_two
-        w1_bf = round_up(raw1[near], True)
-        acts = activations(before, w1q, rooms_of(raw1[near]))
-        w1q = quantize(w1_bf, "w1")
-        halves = round_up_together(raw1[final])
-        h_bf = hidden(before, w3q, acts)
-        acts = activations(near, w1q, rooms_of(raw1[final]))
-        w1q = quantize_halves(halves, "w1")
-        quantize_hidden(before, h_bf)
-        halves = round_up_together(raw3[near])
-        acts = acts + activations(final, w1q, rooms_of(raw3[near]))
-        last_w3q = [quantize_halves(halves, "w3"), quantize_halves(round_up_together(raw3[final]), "w3")]
+        take_in([("w1", near)])
+        hidden(9, activation(9, rooms_of(raw1[near])[0]))
+        take_in([("w1", final)])
+        acts = [activation(near, rooms_of(raw1[final])[0])]
+        rounded = round_up_together(raw3[near])
+        acts.append(activation(final, rooms_of(raw3[near])[0]))
+        last_w3q = [quantize(rounded, "w3"), quantize_halves(round_up_together(raw3[final]), "w3")]
         h_bf = raw3[final][:, 0, :].bitcast(BF16)
         for place, e in enumerate(last_two):
             multiply(last_w3q[place], column_groups(e)[0], acts[place], h_bf, place)
@@ -369,7 +372,7 @@ def tile_moe_shr_glu_gelu_kernel(
             cols = slice(SLOTS + TURNED + c0, SLOTS + TURNED + c0 + width)
             product(ys_banks[1][:, c0 : c0 + width], w2q[SHARED], slice(0, N), h_codes[:, cols], h_scales[:, cols])
         warm_up(w2q[SHARED], 0, down_psum, "y_bank")
-        gated = keep.tile([P, 2, T], F32, name="gated", tag="hs_bf", align_bytes=ALIGN)
+        gated = keep.tile([P, 2, T], F32, name="gated", tag="h_bf", align_bytes=ALIGN)
         positions = (pos1_sb, pos2_sb)
 
         def results_of(t0, width, r):

@@ -251,11 +251,8 @@ def tile_moe_shr_glu_gelu_kernel(
         nc.sync.dma_start(out=offs_sb[:], in_=offs)
         raw1, raw3, raw2 = {}, {}, {}
         raw1[SHARED] = load_up(w1[SHARED], True)
-        for q in range(4):
-            nc.sync.dma_start(
-                out=tok_scales[32 * q : 32 * q + 4, :].bitcast(I32),
-                in_=x_scales[0, 4 * q : 4 * q + 4, :].bitcast(I32),
-            )
+        for r in range(4):
+            nc.sync.dma_start(out=tok_scales[r:P:32, :].bitcast(I32), in_=x_scales[0, r:16:4, :].bitcast(I32))
         raw3[SHARED] = load_up(w3[SHARED], True)
         raw1[0] = load_up(w1[0], True)
         for e in range(PAIRS):

@@ -30,8 +30,7 @@ SMALL_BUFS, LARGE_BUFS = 6, 4
 PAIRS = 8
 H_GROUPS = {3: (0, 4), 7: (4, 4), 9: (8, 2)}
 GATE_ROW0, GATE_STEP = 8, 4
-TURNED = 384
-CHUNKS = [(0, 256), (256, 128)]
+TURNED = 512
 
 
 def tile_moe_shr_glu_gelu_kernel(
@@ -138,8 +137,8 @@ def tile_moe_shr_glu_gelu_kernel(
                     [P, count * PACK * N], BF16, name="w2_bf", tag="w2_bf" + str(count), align_bytes=ALIGN, bufs=4
                 )
             copy(
-                out=rounded[:].rearrange("p (e c i j) -> p e c j i", e=count, i=4, j=PACK),
-                in_=raw.rearrange("p e j (c i) -> p e c j i", i=4),
+                out=rounded[:].rearrange("p (e c i j) -> p e c j i", e=count, i=2, j=PACK),
+                in_=raw.rearrange("p e j (c i) -> p e c j i", i=2),
             )
             return rounded
 
@@ -153,15 +152,20 @@ def tile_moe_shr_glu_gelu_kernel(
                 turn(bank[:, c, :], gate_rows[:, c * P : (c + 1) * P], True, True)
             columns = keep.tile([P, blocks, 4], F32, name="gate_columns")
             on_scalar(out=columns[:], in_=bank[:, :, GATE_ROW0 : GATE_ROW0 + 4 * GATE_STEP : GATE_STEP])
-            gates = [keep.tile([P, 2, T // 2], F32, name="gates", tag="gates" + str(h)) for h in range(2)]
-            for g in range(2):
-                for h in range(2):
-                    bank = down_psum.tile([P, T // 2], F32, name="spread", tag="y_bank")
-                    for c in range(blocks):
-                        column = columns[:, c, 2 * g + h : 2 * g + h + 1]
-                        turn(bank[:, c * P : (c + 1) * P], column.to_broadcast([P, P]), True, True)
-                    on_scalar(out=gates[h][:, g, :], in_=bank[:])
-            return gates
+
+            def column(g, t0):
+                row = 2 * g + t0 // (T // 2)
+                return columns[:, t0 % (T // 2) // P, row : row + 1]
+
+            first = keep.tile([P, T], F32, name="first_gate")
+            second = keep.tile([P, T - TURNED], F32, name="second_gate")
+            for g, t0, target in ((0, 0, first[:, :TURNED]), (0, TURNED, first[:, TURNED:]), (1, TURNED, second[:])):
+                width = target.shape[1]
+                bank = down_psum.tile([P, width], F32, name="spread", tag="y_bank")
+                for c0 in range(0, width, P):
+                    turn(bank[:, c0 : c0 + P], column(g, t0 + c0).to_broadcast([P, P]), True, True)
+                on_scalar(out=target, in_=bank[:])
+            return first, second, [column(1, t0) for t0 in range(0, TURNED, P)]
 
         def product(target, weights, cols, words, scales):
             codes, code_scales = weights
@@ -228,17 +232,18 @@ def tile_moe_shr_glu_gelu_kernel(
             if e == first + count - 1:
                 quantize_hidden(first, open_h[first])
 
-        def slot_outputs(e0, groups, pool, tag):
-            count = sum(codes.shape[1] // N for codes, scales in groups)
-            bank = pool.tile([P, count * C], F32, name=tag, tag=tag)
-            place = 0
-            for weights in groups:
-                for n0 in range(0, weights[0].shape[1], N):
-                    cols = slice((e0 + place) * C, (e0 + place + 1) * C)
-                    target = bank[:, place * C : (place + 1) * C]
-                    product(target, weights, slice(n0, n0 + N), h_codes[:, cols], h_scales[:, cols])
-                    place = place + 1
-            on_scalar(out=y_slots[:, e0 * C : (e0 + count) * C], in_=bank[:])
+        def slot_outputs(firsts, count, pool, tag):
+            bank = pool.tile([P, len(firsts), count * C], F32, name=tag, tag=tag)
+            for place, e0 in enumerate(firsts):
+                for e in range(e0, e0 + count):
+                    loaded = e if e in w2q else e - 1
+                    n0 = (e - loaded) * N
+                    cols = slice(e * C, (e + 1) * C)
+                    target = bank[:, place, (e - e0) * C : (e - e0 + 1) * C]
+                    product(target, w2q[loaded], slice(n0, n0 + N), h_codes[:, cols], h_scales[:, cols])
+            places = [e0 // count for e0 in firsts]
+            runs = y_slots[:].rearrange("p (g c) -> p g c", c=count * C)
+            on_scalar(out=runs[:, places[0] : places[-1] + 1 : max(places[-1] - places[0], 1), :], in_=bank[:])
 
         def gather(s0, gathered, source, dtype, tag):
             offsets = offs_sb[:, s0 // LIST : (s0 + GATHER) // LIST]
@@ -316,7 +321,7 @@ def tile_moe_shr_glu_gelu_kernel(
             take_in([(tag, e), (tag, e + 1)])
             hidden(e - 1, activation(e - 1, rooms_of(raw_of(tag, e))[0]))
             if e == LARGE_BUFS:
-                gates = spread_gates()
+                first_gate, second_gate, second_columns = spread_gates()
         take_in([("w1", 7), ("w1", 8)])
         acts = [activation(e, rooms_of(raw1[7])[e - 6]) for e in (6, 7)]
         rounded = round_up_together(raw3[8])
@@ -352,80 +357,87 @@ def tile_moe_shr_glu_gelu_kernel(
             w2q[e_scalar] = quantize(scalar_bf[e_scalar], "w2")
             w2q[e_vector] = quantize(vector_bf, "w2")
         shared_bf = round_down(raw2[SHARED], on_vector, vector_bf)
-        slot_outputs(0, [w2q[0], w2q[2]], down_psum, "y_bank")
+        slot_outputs((0,), 4, down_psum, "y_bank")
+        slot_outputs((4,), 2, down_psum, "y_bank")
         for half in range(2):
             warm_up(w2q[4], half * N, up_psum, "b_bank")
-        slot_outputs(4, [w2q[4], w2q[6], w2q[7]], down_psum, "y_bank")
-        slot_outputs(10, [w2q[10]], up_psum, "a_bank")
-        slot_outputs(8, [w2q[8]], up_psum, "a_bank")
-        slot_outputs(9, [w2q[9]], up_psum, "b_bank")
+        slot_outputs((6, 10), 2, up_psum, "a_bank")
+        slot_outputs((8,), 1, up_psum, "a_bank")
+        slot_outputs((9,), 1, up_psum, "b_bank")
 
-        w2q[SHARED] = quantize(shared_bf, "w2")
-        ys_banks = [up_psum.tile([P, T // 2], F32, name="ys_bank", tag="a_bank") for t0 in (0, TURNED)]
+        w2q[SHARED] = (
+            keep.tile([P, N], U32, name="codes", tag="picked" + str(TURNED), align_bytes=DMA_ALIGN),
+            keep.tile([P, N], U8, name="scales", tag="scaled" + str(TURNED // 2), align_bytes=DMA_ALIGN),
+        )
+        nc.vector.quantize_mx(out=w2q[SHARED][0][:].bitcast(FP8X4), scales=w2q[SHARED][1][:], in_=shared_bf[:])
+        REST = T - TURNED
+        halves = [slice(0, TURNED // 2), slice(TURNED // 2, TURNED)]
+        ys_turned = up_psum.tile([P, TURNED], F32, name="ys_turned", tag="a_bank")
         for c0 in range(0, TURNED, P):
             cols = slice(SLOTS + c0, SLOTS + c0 + P)
-            product(ys_banks[0][:, c0 : c0 + P], (h_codes, h_scales), cols, w2q[SHARED][0][:], w2q[SHARED][1][:])
-        for c0, width in CHUNKS:
-            cols = slice(SLOTS + TURNED + c0, SLOTS + TURNED + c0 + width)
-            product(ys_banks[1][:, c0 : c0 + width], w2q[SHARED], slice(0, N), h_codes[:, cols], h_scales[:, cols])
-        warm_up(w2q[SHARED], 0, down_psum, "y_bank")
-        gated = keep.tile([P, 2, T], F32, name="gated", tag="h_bf", align_bytes=ALIGN)
-        positions = (pos1_sb, pos2_sb)
+            product(ys_turned[:, c0 : c0 + P], (h_codes, h_scales), cols, w2q[SHARED][0][:], w2q[SHARED][1][:])
+        ys_rest = up_psum.tile([P, REST], F32, name="ys_rest", tag="a_bank")
+        cols = slice(SLOTS + TURNED, SLOTS + T)
+        product(ys_rest[:], w2q[SHARED], slice(0, N), h_codes[:, cols], h_scales[:, cols])
+        warm_up(w2q[9], 0, down_psum, "y_bank")
 
-        def results_of(t0, width, r):
-            return y_slots[:].indirect(positions[r][:, t0 // LIST : (t0 + width) // LIST])
+        def results_of(positions, t0, width):
+            return y_slots[:].indirect(positions[:, t0 // LIST : (t0 + width) // LIST])
 
-        def fetch_gated(t0, width, r):
-            term = gated[:, r, t0 : t0 + width]
-            g0 = t0 % TURNED
-            nc.vector.tensor_tensor(
-                out=term, in0=results_of(t0, width, r), in1=gates[t0 // TURNED][:, r, g0 : g0 + width], op=MULT
-            )
-            return term
+        def sbuf(width, name):
+            return keep.tile([P, width], F32, name=name, tag=name, align_bytes=DMA_ALIGN)
 
-        fetch_gated(0, TURNED, 0)
-        for c0 in range(0, TURNED, P):
-            fetch_gated(c0, P, 1)
+        first_terms = keep.tile([P, T], F32, name="first_terms", tag="h_bf", align_bytes=ALIGN)
+        nc.vector.tensor_tensor(out=first_terms[:], in0=results_of(pos1_sb, 0, T), in1=first_gate[:], op=MULT)
+
+        picked = {}
         ys_sb = keep.tile([P, TURNED], F32, name="ys_sb", tag="ys_sb", align_bytes=DMA_ALIGN)
-        wide, last = (slice(c0, c0 + width) for c0, width in CHUNKS)
-        wide_width, last_width = (width for c0, width in CHUNKS)
-        wide_picked = keep.tile([P, 2, wide_width], F32, name="wide_picked")
-        for r in range(2):
-            nc.scalar.activation(out=wide_picked[:, r, :], in_=results_of(TURNED, wide_width, r), func=COPY)
-        last_picked = keep.tile([P, last_width], F32, name="last_picked")
-        nc.scalar.activation(out=last_picked[:], in_=results_of(TURNED + last.start, last_width, 1), func=COPY)
-        on_scalar(out=ys_sb[:], in_=ys_banks[0][:])
 
-        sum_banks = [up_psum.tile([P, P], F32, name="sums", tag="b_bank") for c0 in range(0, TURNED, P)]
-        for sums, c0 in zip(sum_banks, range(0, TURNED, P)):
-            turn(sums[:], gated[:, 0, c0 : c0 + P], True, False)
-        turned = []
-        for sums, c0 in zip(sum_banks, range(0, TURNED, P)):
-            turn(sums[:], gated[:, 1, c0 : c0 + P], False, True)
-            block = work.tile([P, P], F32, name="turned", tag="turned")
-            on_scalar(out=block[:], in_=sums[:])
-            turned.append(block)
-        for t0, width in CHUNKS:
-            back = down_psum.tile([P, width], F32, name="back", tag="y_bank")
-            for c0 in range(0, width, P):
-                turn(back[:, c0 : c0 + P], ys_sb[:, t0 + c0 : t0 + c0 + P], True, False)
-                turn(back[:, c0 : c0 + P], turned[(t0 + c0) // P][:], False, True)
-            result = work.tile([P, width], F32, name="total", tag="total", bufs=len(CHUNKS), align_bytes=DMA_ALIGN)
-            on_scalar(out=result[:], in_=back[:])
-            nc.scalar.dma_start(out=out[:, t0 : t0 + width], in_=result[:])
+        def pick(t0, width):
+            picked[t0] = sbuf(width, "picked" + str(t0))
+            nc.scalar.activation(out=picked[t0][:], in_=results_of(pos2_sb, t0, width), func=COPY)
 
-        def combine(in0, in1, op, tag):
-            shape = [P] + list(in1.shape[1:])
-            combined = work.tile(shape, F32, name=tag, tag=tag, bufs=len(CHUNKS), align_bytes=DMA_ALIGN)
+        for half in halves:
+            pick(half.start, TURNED // 2)
+        on_scalar(out=ys_sb[:, halves[0]], in_=ys_turned[:, halves[0]])
+        pick(TURNED, REST)
+        on_scalar(out=ys_sb[:, halves[1]], in_=ys_turned[:, halves[1]])
+
+        scaled = {}
+        backs = []
+        for half, by_scalar in zip(halves, (False, True)):
+            turned = up_psum.tile([P, TURNED // 2], F32, name="turned", tag="b_bank")
+            for c0 in range(half.start, half.stop, P):
+                turn(turned[:, c0 - half.start : c0 - half.start + P], picked[half.start][:, c0 - half.start : c0 - half.start + P], True, True)
+            both = sbuf(TURNED // 2, "scaled" + str(half.start))
+            for c0 in range(half.start, half.stop, P):
+                scaled[c0] = both[:, c0 - half.start : c0 - half.start + P]
+                block, column = turned[:, c0 - half.start : c0 - half.start + P], second_columns[c0 // P]
+                if by_scalar:
+                    nc.scalar.activation(out=scaled[c0], in_=block, func=COPY, scale=column)
+                else:
+                    nc.vector.tensor_scalar(out=scaled[c0], in0=block, scalar1=column, scalar2=None, op0=MULT)
+        pieces = [(0, 2 * P, down_psum, "y_bank"), (2 * P, P, down_psum, "y_bank"), (3 * P, P, up_psum, "a_bank")]
+        for t0, width, pool, tag in pieces:
+            back = pool.tile([P, width], F32, name="back", tag=tag)
+            for c0 in range(t0, t0 + width, P):
+                target = back[:, c0 - t0 : c0 - t0 + P]
+                turn(target, ys_sb[:, c0 : c0 + P], True, False)
+                turn(target, scaled[c0], False, True)
+            backs.append(back)
+
+        def combine(in0, in1, op, name):
+            combined = sbuf(in1.shape[1], name)
             nc.vector.tensor_tensor(out=combined[:], in0=in0, in1=in1, op=op)
             return combined[:]
 
-        wide_terms = combine(wide_picked[:], gates[1][:, :, wide], MULT, "terms")
-        last_first = fetch_gated(TURNED + last.start, last_width, 0)
-        wide_partial = combine(ys_banks[1][:, wide], wide_terms[:, 0, :], ADD, "partial")
-        last_second = combine(last_picked[:], gates[1][:, 1, last], MULT, "terms")
-        last_partial = combine(ys_banks[1][:, last], last_first, ADD, "partial")
-        wide_total = combine(wide_partial, wide_terms[:, 1, :], ADD, "added")
-        nc.sync.dma_start(out=out[:, TURNED : TURNED + wide_width], in_=wide_total)
-        last_total = combine(last_partial, last_second, ADD, "added")
-        nc.sync.dma_start(out=out[:, TURNED + last.start : T], in_=last_total)
+        def finish(in0, in1, t0, name):
+            total = combine(in0, in1, ADD, name)
+            nc.sync.dma_start(out=out[:, t0 : t0 + total.shape[1]], in_=total)
+
+        partial = combine(ys_rest[:], first_terms[:, TURNED:], ADD, "picked0")
+        second_terms = combine(picked[TURNED][:], second_gate[:], MULT, "second_terms")
+        finish(backs[0][:], first_terms[:, halves[0]], 0, "total0")
+        finish(partial, second_terms, TURNED, "scaled0")
+        for back, t0 in zip(backs[1:], (2 * P, 3 * P)):
+            finish(back[:], first_terms[:, t0 : t0 + P], t0, "total" + str(t0))

@@ -232,18 +232,17 @@ def tile_moe_shr_glu_gelu_kernel(
             if e == first + count - 1:
                 quantize_hidden(first, open_h[first])
 
-        def slot_outputs(firsts, count, pool, tag):
-            bank = pool.tile([P, len(firsts), count * C], F32, name=tag, tag=tag)
-            for place, e0 in enumerate(firsts):
-                for e in range(e0, e0 + count):
-                    loaded = e if e in w2q else e - 1
-                    n0 = (e - loaded) * N
-                    cols = slice(e * C, (e + 1) * C)
-                    target = bank[:, place, (e - e0) * C : (e - e0 + 1) * C]
-                    product(target, w2q[loaded], slice(n0, n0 + N), h_codes[:, cols], h_scales[:, cols])
-            places = [e0 // count for e0 in firsts]
-            runs = y_slots[:].rearrange("p (g c) -> p g c", c=count * C)
-            on_scalar(out=runs[:, places[0] : places[-1] + 1 : max(places[-1] - places[0], 1), :], in_=bank[:])
+        def slot_outputs(e0, groups, pool, tag):
+            count = sum(codes.shape[1] // N for codes, scales in groups)
+            bank = pool.tile([P, count * C], F32, name=tag, tag=tag)
+            place = 0
+            for weights in groups:
+                for n0 in range(0, weights[0].shape[1], N):
+                    cols = slice((e0 + place) * C, (e0 + place + 1) * C)
+                    target = bank[:, place * C : (place + 1) * C]
+                    product(target, weights, slice(n0, n0 + N), h_codes[:, cols], h_scales[:, cols])
+                    place = place + 1
+            on_scalar(out=y_slots[:, e0 * C : (e0 + count) * C], in_=bank[:])
 
         def gather(s0, gathered, source, dtype, tag):
             offsets = offs_sb[:, s0 // LIST : (s0 + GATHER) // LIST]
@@ -345,8 +344,6 @@ def tile_moe_shr_glu_gelu_kernel(
         for place, e in enumerate(last_two):
             multiply(last_w3q[place], column_groups(e)[0], acts[place], h_bf, place)
 
-        warm_up(last_w3q[0], H - P, down_psum, "y_bank")
-
         raw2[6], raw2[7] = raw2[6][:, 0:1], raw2[6][:, 1:2]
         scalar_bf = {e: round_down(raw2[e], on_scalar) for e in (0, 2, 4, 6, 8)}
         w2q = {0: quantize(scalar_bf[0], "w2")}
@@ -357,13 +354,13 @@ def tile_moe_shr_glu_gelu_kernel(
             w2q[e_scalar] = quantize(scalar_bf[e_scalar], "w2")
             w2q[e_vector] = quantize(vector_bf, "w2")
         shared_bf = round_down(raw2[SHARED], on_vector, vector_bf)
-        slot_outputs((0,), 4, down_psum, "y_bank")
-        slot_outputs((4,), 2, down_psum, "y_bank")
+        slot_outputs(0, [w2q[0], w2q[2]], down_psum, "y_bank")
         for half in range(2):
             warm_up(w2q[4], half * N, up_psum, "b_bank")
-        slot_outputs((6, 10), 2, up_psum, "a_bank")
-        slot_outputs((8,), 1, up_psum, "a_bank")
-        slot_outputs((9,), 1, up_psum, "b_bank")
+        slot_outputs(4, [w2q[4], w2q[6], w2q[7]], down_psum, "y_bank")
+        slot_outputs(10, [w2q[10]], up_psum, "a_bank")
+        slot_outputs(8, [w2q[8]], up_psum, "a_bank")
+        slot_outputs(9, [w2q[9]], up_psum, "b_bank")
 
         w2q[SHARED] = (
             keep.tile([P, N], U32, name="codes", tag="picked" + str(TURNED), align_bytes=DMA_ALIGN),
@@ -379,7 +376,8 @@ def tile_moe_shr_glu_gelu_kernel(
         ys_rest = up_psum.tile([P, REST], F32, name="ys_rest", tag="a_bank")
         cols = slice(SLOTS + TURNED, SLOTS + T)
         product(ys_rest[:], w2q[SHARED], slice(0, N), h_codes[:, cols], h_scales[:, cols])
-        warm_up(w2q[9], 0, down_psum, "y_bank")
+        for place in range(2):
+            warm_up(w2q[9], 0, down_psum, "y_bank")
 
         def results_of(positions, t0, width):
             return y_slots[:].indirect(positions[:, t0 // LIST : (t0 + width) // LIST])

from contextlib import ExitStack

import concourse.mybir as mybir
from concourse.masks import make_identity

K, T, E, C, H, N = 512, 768, 12, 128, 512, 128
SLOTS = E * C
SHARED = E
FLOPS = 2 * (SLOTS + T) * (2 * K * H + H * N)

F32 = mybir.dt.float32
BF16 = mybir.dt.bfloat16
I32 = mybir.dt.int32
U32 = mybir.dt.uint32
U16 = mybir.dt.uint16
U8 = mybir.dt.uint8
FP8X4 = mybir.dt.float8_e4m3fn_x4
GELU = mybir.ActivationFunctionType.Gelu_apprx_tanh
COPY = mybir.ActivationFunctionType.Copy
MULT = mybir.AluOpType.mult
ADD = mybir.AluOpType.add

P = 128
PACK = 4
ALIGN = 64
DMA_ALIGN = 256
LIST = 16
GATHER = 512
SMALL_BUFS, LARGE_BUFS = 6, 4
PAIRS = 8
H_GROUPS = {3: (0, 4), 7: (4, 4), 9: (8, 2)}
GATE_ROW0, GATE_STEP = 8, 4
TURNED = 512


def tile_moe_shr_glu_gelu_kernel(
    tc, x_words, x_scales, w1, w3, w2, gate, offs, pos1, pos2, out
):
    nc = tc.nc
    on_vector, on_scalar = nc.vector.tensor_copy, nc.scalar.copy
    with ExitStack() as ctx:
        keep = ctx.enter_context(tc.tile_pool(name="keep", bufs=1))
        small = ctx.enter_context(tc.tile_pool(name="small", bufs=SMALL_BUFS))
        large = ctx.enter_context(tc.tile_pool(name="large", bufs=LARGE_BUFS))
        work = ctx.enter_context(tc.tile_pool(name="work", bufs=3))
        up_psum = ctx.enter_context(tc.psum_pool(name="up_psum", bufs=3))
        down_psum = ctx.enter_context(tc.psum_pool(name="down_psum", bufs=2))

        tok_words = keep.tile([P, T], I32, name="tok_words", align_bytes=DMA_ALIGN)
        tok_scales = keep.tile([P, T], U8, name="tok_scales", align_bytes=DMA_ALIGN)
        slot_words = {}
        slot_scales = {}
        offs_sb = keep.tile([P, SLOTS // LIST], U16, name="offs_sb")
        pos1_sb = keep.tile([P, T // LIST], U16, name="pos1_sb")
        pos2_sb = keep.tile([P, T // LIST], U16, name="pos2_sb")
        h_codes = keep.tile([P, SLOTS + T], U32, name="h_codes", align_bytes=ALIGN)
        h_scales = keep.tile([P, SLOTS + T], U8, name="h_scales", align_bytes=ALIGN)
        y_slots = keep.tile([P, SLOTS], F32, name="y_slots")
        nc.vector.memset(tok_scales[:].bitcast(I32), 0)
        gate_rows = keep.tile([P, T // 2], F32, name="gate_rows", tag="ys_sb", align_bytes=DMA_ALIGN)
        nc.gpsimd.memset(gate_rows[:], 0.0)
        identity = keep.tile([P, P], F32, name="identity")
        make_identity(nc, identity[:])

        late_loads = []

        def late_buffer(shape):
            pool = small if len(late_loads) % (SMALL_BUFS + LARGE_BUFS) < SMALL_BUFS else large
            late_loads.append(shape)
            return pool.tile(shape, F32, name="raw", tag="raw", align_bytes=DMA_ALIGN)

        def load_pair(weights, e):
            raw = large.tile([P, 2, PACK, H], F32, name="raw", tag="raw", align_bytes=DMA_ALIGN)
            nc.sync.dma_start(out=raw[:], in_=weights[e : e + 2].rearrange("e (p j) c -> p e j c", j=PACK))
            return raw[:, 0], raw[:, 1]

        def load_up(weight, early=False):
            if early:
                raw = small.tile([P, PACK, H], F32, name="raw", tag="raw", align_bytes=DMA_ALIGN)
            else:
                raw = late_buffer([P, PACK, H])
            nc.sync.dma_start(out=raw[:], in_=weight.rearrange("(p j) c -> p j c", j=PACK))
            return raw

        def load_down(e0, count):
            raw = late_buffer([P, count, PACK, N])
            nc.sync.dma_start(out=raw[:], in_=w2[e0 : e0 + count].rearrange("e (p j) c -> p e j c", j=PACK))
            return raw[:]

        def code_tiles(width, tag):
            bufs = 3 if width == H else 5
            tag = tag + str(width)
            codes = work.tile([P, width], U32, name=tag + "_codes", tag=tag + "_codes", align_bytes=ALIGN, bufs=bufs)
            scales = work.tile([P, width], U8, name=tag + "_scales", tag=tag + "_scales", align_bytes=ALIGN, bufs=bufs)
            return codes, scales

        def quantize(rounded, tag):
            codes, scales = code_tiles(rounded.shape[1] // PACK, tag)
            nc.vector.quantize_mx(out=codes[:].bitcast(FP8X4), scales=scales[:], in_=rounded[:])
            return codes, scales

        def round_up(raw, by_scalar, rounded=None):
            if rounded is None:
                rounded = work.tile([P, PACK * H], BF16, name="up_bf", tag="up_bf", align_bytes=ALIGN, bufs=4)
            if by_scalar:
                on_scalar(
                    out=rounded[:].rearrange("p (t m j) -> p m j t", t=PACK, j=PACK),
                    in_=raw[:].rearrange("p j (m t) -> p m j t", t=PACK),
                )
            else:
                on_vector(
                    out=rounded[:].rearrange("p (u v m j) -> p u m j v", u=2, v=2, j=PACK),
                    in_=raw[:].rearrange("p j (m u v) -> p u m j v", u=2, v=2),
                )
            return rounded

        def round_up_together(raw):
            rounded = work.tile([P, PACK * H], BF16, name="up_bf", tag="up_bf", align_bytes=ALIGN, bufs=4)
            source = raw[:].rearrange("p j (m t) -> p m j t", t=PACK)
            for u, copy in enumerate((on_vector, on_scalar)):
                half = rounded[:, u * PACK * H // 2 : (u + 1) * PACK * H // 2]
                copy(out=half.rearrange("p (t m j) -> p m j t", t=2, j=PACK), in_=source[:, :, :, 2 * u : 2 * u + 2])
            return rounded

        def quantize_halves(rounded, tag):
            codes, scales = code_tiles(H, tag)
            for u in range(2):
                cols = slice(u * H // 2, (u + 1) * H // 2)
                half = rounded[:, u * PACK * H // 2 : (u + 1) * PACK * H // 2]
                nc.vector.quantize_mx(out=codes[:, cols].bitcast(FP8X4), scales=scales[:, cols], in_=half)
            return codes, scales

        def round_down(raw, copy, rounded=None):
            count = raw.shape[1]
            if rounded is None:
                rounded = work.tile(
                    [P, count * PACK * N], BF16, name="w2_bf", tag="w2_bf" + str(count), align_bytes=ALIGN, bufs=4
                )
            copy(
                out=rounded[:].rearrange("p (e c i j) -> p e c j i", e=count, i=2, j=PACK),
                in_=raw.rearrange("p e j (c i) -> p e c j i", i=2),
            )
            return rounded

        def turn(target, term, start, stop):
            nc.tensor.matmul(target, lhsT=term, rhs=identity[:], is_transpose=True, start=start, stop=stop)

        def spread_gates():
            blocks = T // 2 // P
            bank = down_psum.tile([P, blocks, P], F32, name="columns", tag="y_bank")
            for c in range(blocks):
                turn(bank[:, c, :], gate_rows[:, c * P : (c + 1) * P], True, True)
            columns = keep.tile([P, blocks, 4], F32, name="gate_columns")
            on_scalar(out=columns[:], in_=bank[:, :, GATE_ROW0 : GATE_ROW0 + 4 * GATE_STEP : GATE_STEP])

            def column(g, t0):
                row = 2 * g + t0 // (T // 2)
                return columns[:, t0 % (T // 2) // P, row : row + 1]

            first = keep.tile([P, T], F32, name="first_gate")
            second = keep.tile([P, T - TURNED], F32, name="second_gate")
            for g, t0, target in ((0, 0, first[:, :TURNED]), (0, TURNED, first[:, TURNED:]), (1, TURNED, second[:])):
                width = target.shape[1]
                bank = down_psum.tile([P, width], F32, name="spread", tag="y_bank")
                for c0 in range(0, width, P):
                    turn(bank[:, c0 : c0 + P], column(g, t0 + c0).to_broadcast([P, P]), True, True)
                on_scalar(out=target, in_=bank[:])
            return first, second, [column(1, t0) for t0 in range(0, TURNED, P)]

        def product(target, weights, cols, words, scales):
            codes, code_scales = weights
            nc.tensor.matmul_mx(
                out=target,
                lhsT=codes[:, cols].bitcast(FP8X4),
                lhsT_scale=code_scales[:, cols],
                rhs=words.bitcast(FP8X4),
                rhs_scale=scales,
                start=True,
                stop=True,
            )

        def up_product(weights, words, scales, tag):
            bank = up_psum.tile([P, PACK, C], F32, name=tag, tag=tag)
            for t in range(PACK):
                product(bank[:, t, :], weights, slice(P * t, P * (t + 1)), words, scales)
            return bank[:].rearrange("p t n -> p n t")

        def warm_up(weights, n0, pool, tag):
            idle = pool.tile([P, 4 * C], F32, name="idle", tag=tag)
            product(idle[:], weights, slice(n0, n0 + P), h_codes[:, : 4 * C], h_scales[:, : 4 * C])

        def column_groups(e):
            if e == SHARED:
                return [(tok_words[:, t0 : t0 + C], tok_scales[:, t0 : t0 + C]) for t0 in range(0, T, C)]
            s0, c0 = e * C // GATHER * GATHER, e * C % GATHER
            return [(slot_words[s0][:, c0 : c0 + C], slot_scales[s0][:, c0 : c0 + C])]

        def rooms_of(raw):
            return [raw[:, j, :].rearrange("p (n t) -> p n t", t=PACK) for j in range(PACK)]

        def activations(e, w1q, rooms):
            groups = column_groups(e)
            for columns, room in zip(groups, rooms):
                nc.scalar.activation(out=room, in_=up_product(w1q, *columns, "a_bank"), func=GELU)
            return rooms[: len(groups)]

        def multiply(w3q, columns, act, h_bf, place):
            view = h_bf[:, place * PACK * C : (place + 1) * PACK * C].rearrange("p (n t) -> p n t", t=PACK)
            nc.vector.tensor_tensor(out=view, in0=up_product(w3q, *columns, "b_bank"), in1=act, op=MULT)

        def h_tile(columns):
            return keep.tile([P, PACK * columns], BF16, name="h_bf", tag="h_bf", align_bytes=ALIGN)

        def quantize_hidden(e, h_bf):
            count = h_bf.shape[1] // PACK
            for c0 in range(0, count, 4 * C):
                width = min(count - c0, 4 * C)
                h0 = e * C + c0
                nc.vector.quantize_mx(
                    out=h_codes[:, h0 : h0 + width].bitcast(FP8X4),
                    scales=h_scales[:, h0 : h0 + width],
                    in_=h_bf[:, c0 * PACK : (c0 + width) * PACK],
                )

        open_h = {}

        def hidden(e, act):
            first, count = H_GROUPS[min(last for last in H_GROUPS if last >= e)]
            if e == first:
                open_h[first] = h_tile(count * C)
            multiply(up_q["w3", e], column_groups(e)[0], act, open_h[first], e - first)
            if e == first + count - 1:
                quantize_hidden(first, open_h[first])

        def slot_outputs(e0, groups, pool, tag):
            count = sum(codes.shape[1] // N for codes, scales in groups)
            bank = pool.tile([P, count * C], F32, name=tag, tag=tag)
            place = 0
            for weights in groups:
                for n0 in range(0, weights[0].shape[1], N):
                    cols = slice((e0 + place) * C, (e0 + place + 1) * C)
                    target = bank[:, place * C : (place + 1) * C]
                    product(target, weights, slice(n0, n0 + N), h_codes[:, cols], h_scales[:, cols])
                    place = place + 1
            on_scalar(out=y_slots[:, e0 * C : (e0 + count) * C], in_=bank[:])

        def gather(s0, gathered, source, dtype, tag):
            offsets = offs_sb[:, s0 // LIST : (s0 + GATHER) // LIST]
            gathered[s0] = keep.tile([P, GATHER], dtype, name=tag, tag=tag + str(s0), align_bytes=ALIGN)
            on_vector(out=gathered[s0][:], in_=source.indirect(offsets))

        last_two = (E - 2, E - 1)
        half_rows = gate.rearrange("g n (h t) -> (g n h) t", h=2)
        nc.sync.dma_start(out=tok_words[:], in_=x_words[0].rearrange("p t r -> p (t r)").bitcast(I32))
        nc.sync.dma_start(out=offs_sb[:], in_=offs)
        raw1, raw3, raw2 = {}, {}, {}
        raw1[SHARED] = load_up(w1[SHARED], True)
        for r in range(4):
            nc.sync.dma_start(out=tok_scales[r:P:32, :].bitcast(I32), in_=x_scales[0, r:16:4, :].bitcast(I32))
        raw3[SHARED] = load_up(w3[SHARED], True)
        raw1[0] = load_up(w1[0], True)
        for e in range(PAIRS):
            weights, raws = ((w3, raw3), (w1, raw1))[e % 2]
            if e == LARGE_BUFS:
                nc.sync.dma_start(
                    out=gate_rows[GATE_ROW0 : GATE_ROW0 + 4 * GATE_STEP : GATE_STEP, :],
                    in_=half_rows[0 : 3 * (P + 1) + 1 : P + 1, :],
                )
            raws[e], raws[e + 1] = load_pair(weights, e)
        raw3[PAIRS] = load_up(w3[PAIRS])
        for e in range(PAIRS + 1, E - 2):
            raw1[e] = load_up(w1[e])
            raw3[e] = load_up(w3[e])
        for e in last_two:
            raw1[e] = load_up(w1[e])
        for e in last_two:
            raw3[e] = load_up(w3[e])
        for e in (0, 2, 4, 6):
            raw2[e] = load_down(e, 2)
        raw2[10] = late_buffer([P, 2, PACK, N])[:]
        for place in range(2):
            nc.sync.dma_start(out=raw2[10][:, place], in_=w2[10 + place].rearrange("(p j) c -> p j c", j=PACK))
        for e in (8, 9, SHARED):
            raw2[e] = load_down(e, 1)
        nc.sync.dma_start(out=pos1_sb[:], in_=pos1)
        nc.sync.dma_start(out=pos2_sb[:], in_=pos2)

        for s0 in range(0, SLOTS, GATHER):
            gather(s0, slot_words, tok_words[:].bitcast(U32), U32, "words")
        last_gather = SLOTS - GATHER
        for s0 in range(0, last_gather, GATHER):
            gather(s0, slot_scales, tok_scales[:], U8, "scales")
        w1_bf = keep.tile([P, PACK * H], BF16, name="w1_bf", tag="scales" + str(last_gather), align_bytes=ALIGN)
        w1q = quantize(round_up(raw1[SHARED], True, w1_bf), "w1")
        gather(last_gather, slot_scales, tok_scales[:], U8, "scales")
        w3q = quantize(round_up(raw3[SHARED], True), "w3")
        w1_bf = round_up(raw1[0], False)
        acts = activations(SHARED, w1q, rooms_of(raw3[SHARED]) + rooms_of(raw1[SHARED]))
        h_bf = h_tile(T)
        for place, columns in enumerate(column_groups(SHARED)):
            multiply(w3q, columns, acts[place], h_bf, place)
        up_q = {("w1", 0): quantize(w1_bf, "w1")}
        quantize_hidden(SHARED, h_bf)
        for e in range(2):
            up_q["w3", e] = quantize(round_up(raw3[e], True), "w3")

        def raw_of(tag, e):
            return (raw1 if tag == "w1" else raw3)[e]

        def take_in(matrices):
            rounded = [round_up_together(raw_of(tag, e)) for tag, e in matrices]
            for place, (tag, e) in enumerate(matrices):
                up_q[tag, e] = quantize(rounded[place], tag)

        def activation(e, room):
            return activations(e, up_q["w1", e], [room])[0]

        for e in range(1, PAIRS - 1):
            tag = ("w3", "w1")[e % 2]
            take_in([(tag, e), (tag, e + 1)])
            hidden(e - 1, activation(e - 1, rooms_of(raw_of(tag, e))[0]))
            if e == LARGE_BUFS:
                first_gate, second_gate, second_columns = spread_gates()
        take_in([("w1", 7), ("w1", 8)])
        acts = [activation(e, rooms_of(raw1[7])[e - 6]) for e in (6, 7)]
        rounded = round_up_together(raw3[8])
        hidden(6, acts[0])
        hidden(7, acts[1])
        up_q["w3", 8] = quantize(rounded, "w3")
        act = activation(8, rooms_of(raw3[8])[0])
        rounded = round_up_together(raw1[9])
        hidden(8, act)
        up_q["w1", 9] = quantize(rounded, "w1")
        take_in([("w3", 9)])
        near, final = last_two
        take_in([("w1", near)])
        hidden(9, activation(9, rooms_of(raw1[near])[0]))
        take_in([("w1", final)])
        acts = [activation(near, rooms_of(raw1[final])[0])]
        rounded = round_up_together(raw3[near])
        acts.append(activation(final, rooms_of(raw3[near])[0]))
        last_w3q = [quantize(rounded, "w3"), quantize_halves(round_up_together(raw3[final]), "w3")]
        h_bf = raw3[final][:, 0, :].bitcast(BF16)
        for place, e in enumerate(last_two):
            multiply(last_w3q[place], column_groups(e)[0], acts[place], h_bf, place)

        raw2[6], raw2[7] = raw2[6][:, 0:1], raw2[6][:, 1:2]
        scalar_bf = {e: round_down(raw2[e], on_scalar) for e in (0, 2, 4, 6, 8)}
        w2q = {0: quantize(scalar_bf[0], "w2")}
        quantize_hidden(near, h_bf)
        w2q[2] = quantize(scalar_bf[2], "w2")
        for e_vector, e_scalar in ((7, 4), (10, 6), (9, 8)):
            vector_bf = round_down(raw2[e_vector], on_vector)
            w2q[e_scalar] = quantize(scalar_bf[e_scalar], "w2")
            w2q[e_vector] = quantize(vector_bf, "w2")
        shared_bf = round_down(raw2[SHARED], on_vector, vector_bf)
        slot_outputs(0, [w2q[0], w2q[2]], down_psum, "y_bank")
        for half in range(2):
            warm_up(w2q[4], half * N, up_psum, "b_bank")
        slot_outputs(4, [w2q[4], w2q[6], w2q[7]], down_psum, "y_bank")
        slot_outputs(10, [w2q[10]], up_psum, "a_bank")
        slot_outputs(8, [w2q[8]], up_psum, "a_bank")
        slot_outputs(9, [w2q[9]], up_psum, "b_bank")

        w2q[SHARED] = (
            keep.tile([P, N], U32, name="codes", tag="picked" + str(TURNED), align_bytes=DMA_ALIGN),
            keep.tile([P, N], U8, name="scales", tag="scaled" + str(TURNED // 2), align_bytes=DMA_ALIGN),
        )
        nc.vector.quantize_mx(out=w2q[SHARED][0][:].bitcast(FP8X4), scales=w2q[SHARED][1][:], in_=shared_bf[:])
        REST = T - TURNED
        halves = [slice(0, TURNED // 2), slice(TURNED // 2, TURNED)]
        ys_turned = up_psum.tile([P, TURNED], F32, name="ys_turned", tag="a_bank")
        for c0 in range(0, TURNED, P):
            cols = slice(SLOTS + c0, SLOTS + c0 + P)
            product(ys_turned[:, c0 : c0 + P], (h_codes, h_scales), cols, w2q[SHARED][0][:], w2q[SHARED][1][:])
        ys_rest = up_psum.tile([P, REST], F32, name="ys_rest", tag="a_bank")
        cols = slice(SLOTS + TURNED, SLOTS + T)
        product(ys_rest[:], w2q[SHARED], slice(0, N), h_codes[:, cols], h_scales[:, cols])
        for place in range(2):
            warm_up(w2q[9], 0, down_psum, "y_bank")

        def results_of(positions, t0, width):
            return y_slots[:].indirect(positions[:, t0 // LIST : (t0 + width) // LIST])

        def sbuf(width, name):
            return keep.tile([P, width], F32, name=name, tag=name, align_bytes=DMA_ALIGN)

        first_terms = keep.tile([P, T], F32, name="first_terms", tag="h_bf", align_bytes=ALIGN)
        nc.vector.tensor_tensor(out=first_terms[:], in0=results_of(pos1_sb, 0, T), in1=first_gate[:], op=MULT)

        picked = {}
        ys_sb = keep.tile([P, TURNED], F32, name="ys_sb", tag="ys_sb", align_bytes=DMA_ALIGN)

        def pick(t0, width):
            picked[t0] = sbuf(width, "picked" + str(t0))
            nc.scalar.activation(out=picked[t0][:], in_=results_of(pos2_sb, t0, width), func=COPY)

        for half in halves:
            pick(half.start, TURNED // 2)
        on_scalar(out=ys_sb[:, halves[0]], in_=ys_turned[:, halves[0]])
        pick(TURNED, REST)
        on_scalar(out=ys_sb[:, halves[1]], in_=ys_turned[:, halves[1]])

        scaled = {}
        backs = []
        for half, by_scalar in zip(halves, (False, True)):
            turned = up_psum.tile([P, TURNED // 2], F32, name="turned", tag="b_bank")
            for c0 in range(half.start, half.stop, P):
                turn(turned[:, c0 - half.start : c0 - half.start + P], picked[half.start][:, c0 - half.start : c0 - half.start + P], True, True)
            both = sbuf(TURNED // 2, "scaled" + str(half.start))
            for c0 in range(half.start, half.stop, P):
                scaled[c0] = both[:, c0 - half.start : c0 - half.start + P]
                block, column = turned[:, c0 - half.start : c0 - half.start + P], second_columns[c0 // P]
                if by_scalar:
                    nc.scalar.activation(out=scaled[c0], in_=block, func=COPY, scale=column)
                else:
                    nc.vector.tensor_scalar(out=scaled[c0], in0=block, scalar1=column, scalar2=None, op0=MULT)
        pieces = [(0, 2 * P, down_psum, "y_bank"), (2 * P, P, down_psum, "y_bank"), (3 * P, P, up_psum, "a_bank")]
        for t0, width, pool, tag in pieces:
            back = pool.tile([P, width], F32, name="back", tag=tag)
            for c0 in range(t0, t0 + width, P):
                target = back[:, c0 - t0 : c0 - t0 + P]
                turn(target, ys_sb[:, c0 : c0 + P], True, False)
                turn(target, scaled[c0], False, True)
            backs.append(back)

        def combine(in0, in1, op, name):
            combined = sbuf(in1.shape[1], name)
            nc.vector.tensor_tensor(out=combined[:], in0=in0, in1=in1, op=op)
            return combined[:]

        def finish(in0, in1, t0, name):
            total = combine(in0, in1, ADD, name)
            nc.sync.dma_start(out=out[:, t0 : t0 + total.shape[1]], in_=total)

        partial = combine(ys_rest[:], first_terms[:, TURNED:], ADD, "picked0")
        second_terms = combine(picked[TURNED][:], second_gate[:], MULT, "second_terms")
        finish(backs[0][:], first_terms[:, halves[0]], 0, "total0")
        finish(partial, second_terms, TURNED, "scaled0")
        for back, t0 in zip(backs[1:], (2 * P, 3 * P)):
            finish(back[:], first_terms[:, t0 : t0 + P], t0, "total" + str(t0))
